import numpy as np, ml_dtypes
CORES = [48,51,52,55]
N = 4
import mx_ref
BF = ml_dtypes.bfloat16
def gcols(t, e):
    v = np.concatenate([t.reshape(8, 16, -1, 4), np.zeros((8, 16, 1, 4), BF)], axis=2)
    return np.ascontiguousarray(np.stack([v[g][:, e[g]] for g in range(8)])).reshape(128, -1)
def tile(rs):
    return np.stack(rs, axis=2).reshape(128, -1).astype(BF)
def pick(q, e):
    c = np.concatenate([q[0].reshape(128, -1, 4), np.zeros((128, 1, 4), np.uint8)], axis=1); s = np.concatenate([q[1], np.ones((16, 1), np.uint8)], axis=1)
    return (np.ascontiguousarray(c[:, e].reshape(128, -1)), np.ascontiguousarray(s[:, e]))
def join(*qs):
    return (np.concatenate([q[0] for q in qs], axis=1), np.concatenate([q[1] for q in qs], axis=1))
def put(q, e, v):
    c, s = q[0].reshape(128, -1, 4).copy(), q[1].copy(); c[:, e] = v[0].reshape(128, -1, 4); s[:, e] = v[1]
    return (c.reshape(128, -1), s)
def pk(c, s):
    return (np.ascontiguousarray(c), mx_ref.live(s))
def emit(q):
    return q[0], q[1]
def packed(v, rng):
    q = [mx_ref.quantize(np.ascontiguousarray(v[r])) for r in range(N)]
    return np.stack([a for a, b in q]), np.stack([mx_ref.plane(b, rng) for a, b in q])
def f(rng, *shape):
    return mx_ref.flush((rng.standard_normal(shape, dtype=np.float32) * np.exp2(rng.integers(-2, 3, shape[:-1] + (1,)))).astype(BF))
def wide(rng, *shape, cols=0):
    v = rng.standard_normal(shape, dtype=np.float32) * np.exp2(rng.integers(-12, 13, shape)).astype(np.float32)
    if cols: v *= np.repeat(np.exp2(rng.integers(-cols, cols + 1, shape[:-2] + (1, shape[-1] // 4))) * (rng.random(shape[:-2] + (1, shape[-1] // 4)) > 0.0625), 4, axis=-1).astype(np.float32)
    return mx_ref.flush(v.astype(BF))
C, A, R = 320, 160, 3
STEP = [1, 2, 1]
def places(p):
    return np.argsort(np.argsort(-(p[::16] + np.float32(0.0)), axis=1, kind="stable"), axis=1)
def neighbours(a, b):
    below = (a[:, None] < a[:, :, None]) & (b[:, None] < b[:, :, None])
    above = below.transpose(0, 2, 1)
    def best(m, k):
        return np.where(m.any(axis=2), np.argmax(np.where(m, k[:, None], -1), axis=2), np.arange(C))
    return best(below, a), best(below, b), best(above, C - a), best(above, C - b), np.sum(below, axis=2) % 2
def parts(m):
    return np.repeat(np.repeat(m, 16, axis=0), 4, axis=1)
def toggle(t, la, lb, ua, ub, m):
    low = np.maximum(gcols(t, la).astype(np.float32), gcols(t, lb).astype(np.float32))
    high = np.minimum(gcols(t, ua).astype(np.float32), gcols(t, ub).astype(np.float32))
    v = (low + high).astype(BF)
    h = (v.astype(np.float32) - t.astype(np.float32)).astype(BF)
    new, k = t.copy(), parts(m)
    new[k] = h[k]
    return new
def gput(t, e, h):
    a, b = t.reshape(8, 16, -1, 4).copy(), h.reshape(8, 16, -1, 4)
    for g in range(8): a[g][:, e[g]] = b[g]
    return a.reshape(128, -1)
def big(v):
    v = v.astype(np.float32)
    v[np.abs(v) < np.float32(2.0 ** -16)] = 0
    return v.astype(BF)
def numbers_of(rng):
    return {"x": big(f(rng, N, 128, 4 * C)), "u": np.array(f(rng, N, 128, 512)), "v": np.array(f(rng, N, 128, 512))}
def weights(rng, still=[]):
    w = np.array(f(rng, N, 128, 2048)).reshape(N, 8, 16, 4, 8, 16, 4)
    for i in still:
        w[:, :, i] = 0
        w[:, :, :, :, :, i] = 0
    c, p = packed(w.reshape(N, 128, 2048), rng)
    return {"wc": c, "ws": p}
def signs(rng):
    return np.stack([rng.permutation(8) % 2 * 2.0 - 1.0 for r in range(N)])
def digits(k, n):
    return ((k[..., None] >> np.arange(n)) & 1) * np.exp2(np.arange(n) * 1.0)
def setup_inputs(rng):
    return {**numbers_of(rng), **weights(rng)}
def setup_inputs_ties(rng):
    d = numbers_of(rng)
    e = rng.permutation(N)
    x = d["x"].reshape(N, 8, 16, C, 4)
    for r in range(N):
        k = np.zeros(C, int) if r == e[0] else rng.permutation(C) % 3
        a = x[r][:, :8, :3].copy()
        a[:, :, 2] = 0
        x[r][:, :8] = a[:, :, k]
    x[e[1]] = 0
    u = d["u"].reshape(N, 8, 16, 128, 4)
    u[:, :, 8:, ::16] = 0
    return {"x": x.reshape(N, 128, 4 * C), "u": u.reshape(N, 128, 512), "v": d["v"], **weights(rng, range(8))}
def setup_inputs_near(rng):
    d = numbers_of(rng)
    x = d["x"].astype(np.float32).reshape(N, 8, 16, C, 4)
    u = d["u"].reshape(N, 128, 128, 4)
    u[:, :, ::16] = 0
    o, c = rng.permutation(N) % 4, signs(rng)
    z = digits(np.argsort(rng.random((N, 8, C)), axis=2) // 2, 8)
    x[:, :, 0] = 0
    x[:, :, 8:] = 0
    for r in range(N):
        if o[r] < 2: x[r, :, 0, :, 0] = c[r][:, None]
        k = z[r] * 2.0 ** -23 if o[r] < 2 else z[r] * c[r][:, None, None] * 2.0 ** -30
        x[r, :, 8] = k[:, :, :4]
        x[r, :, 9] = k[:, :, 4:]
        size = 1.0 if o[r] == 0 else 2.0 ** -30
        for h in range(0, 128, 16):
            u[r, h, h, 0] = size
            u[r, h + 8:h + 10, h] = size
    return {"x": x.reshape(N, 128, 4 * C).astype(BF), "u": u.reshape(N, 128, 512), "v": d["v"], **weights(rng, [0, 8, 9, 10, 11, 12, 13, 14, 15])}
def setup_inputs_chains(rng):
    d = numbers_of(rng)
    x = d["x"].astype(np.float32).reshape(N, 8, 16, C, 4)
    u = d["u"].reshape(N, 128, 128, 4)
    h = C // 2
    o = np.argsort(rng.random((N, 8, C)), axis=2)
    for r in range(N):
        p = r ^ STEP[0]
        if r < p:
            k = rng.permutation(8)
            for g in range(8):
                a = o[r, g]
                if k[g] == 0: o[p, g] = a
                if k[g] == 1: o[p, g] = a[::-1]
                if k[g] == 2: o[p, g] = np.concatenate([a[:1], a[1:][::-1]])
                if k[g] == 3: o[p, g] = np.concatenate([a[:-1][::-1], a[-1:]])
                if k[g] == 4: o[p, g] = np.concatenate([a[h:], a[:h]])
                if k[g] == 5: o[p, g] = np.concatenate([a[:h][::-1], a[h:][::-1]])
                if k[g] == 6: o[p, g] = a.reshape(-1, 2)[:, ::-1].reshape(-1)
    z = digits(C - 1 - np.argsort(o, axis=2), 12)
    for i in range(3): x[:, :, 8 + i] = z[:, :, :, 4 * i:4 * i + 4]
    k = np.where(rng.permutation(N) < N // 2, 2.0 ** -30, 1.0).astype(np.float32).astype(BF)
    u[:, :, ::16] = 0
    for i in range(0, 128, 16): u[:, i + 8:i + 11, i] = k[:, None, None]
    return {"x": x.reshape(N, 128, 4 * C).astype(BF), "u": u.reshape(N, 128, 512), "v": d["v"], **weights(rng, [8, 9, 10])}
def setup_inputs_huge(rng):
    d = numbers_of(rng)
    mixed = rng.permutation(8) < 4
    side = np.array([1.0 - 2.0 * (bin(r).count("1") % 2) for r in range(N)])
    c = rng.permutation(C) % 2 * 2.0 - 1.0
    k = np.where(mixed[:, None], np.argsort(rng.random((8, C)), axis=1), rng.integers(0, 32, (N, 8, C)))
    z = digits(k, 12) * np.where(mixed, 2.0 ** 21, 2.0 ** 18)[:, None, None]
    p = np.ones(8)
    p[~mixed] = rng.permutation(4) % 2 * 2.0 - 1.0
    s = np.where(mixed, side[:, None], p)
    x = np.zeros((N, 8, 16, C, 4))
    x[:, :, :8] = (s[:, :, None] * np.where(mixed[:, None], c, 1.0))[:, :, None, :, None] * 2.0 ** 30
    for i in range(3): x[:, :, 8 + i] = z[:, :, :, 4 * i:4 * i + 4] * s[:, :, None, None]
    x[:, :, 11:] = 2.0 ** 20 * (0.5 + 0.5 * rng.random((N, 8, 5, C, 4))) * rng.choice([-1.0, 1.0], (N, 8, 5, C, 4))
    u = d["u"].reshape(N, 8, 16, 128, 4)
    u[:, :, :, ::16] = 0
    w = 2.0 ** 30 * (1 - 0.125 * rng.random((8, 8, 4))) * p[:, None, None]
    q = np.ones((N, 8))
    for r in range(N): q[r, ~mixed] = rng.permutation(4) % 2 * 2.0 - 1.0
    for g in range(8):
        for h in range(8):
            if mixed[h] == mixed[g]: u[:, h, :8, 16 * g] = (q[:, g][:, None, None] * w[h]).astype(np.float32).astype(BF)
        u[:, g, 8:11, 16 * g] = 2.0 ** 30
    return {"x": x.astype(np.float32).reshape(N, 128, 4 * C).astype(BF), "u": u.reshape(N, 128, 512), "v": d["v"], **weights(rng, range(11))}
def setup_inputs_spread(rng):
    d = setup_inputs(rng)
    d["x"] = big(wide(rng, N, 128, 4 * C, cols=6))
    return d
def check_inputs(d):
    b = []
    for k in ("x", "u", "v"):
        a = np.abs(d[k].astype(np.float32))
        if not (np.isfinite(a).all() and ((a == 0) | (a >= 2.0 ** -30) & (a <= 2.0 ** 30)).all()): b.append("a value of " + k)
    if ((d["wc"] & 0x7F) == 0x7F).any(): b.append("a code of wc that is no number")
    z = np.zeros((128, 4, 4), np.float32)
    z[:, 1] = 2.0 ** -30
    z[:, 2] = 2.0 ** 30
    c, s = emit(mx_ref.quantize(z.reshape(128, 16).astype(BF)))
    for r in range(N):
        p = mx_ref.live(d["ws"][r])
        if not ((p == s[0, 0]) | (p >= s[0, 1]) & (p <= s[0, 2])).all(): b.append("a scale of ws")
    return b
def reference(x, u, v, wc, ws):
    qu = [mx_ref.quantize(u[r]) for r in range(N)]
    lay = [pk(wc[r], ws[r]) for r in range(N)]
    now = [x[r] for r in range(N)]
    for t in range(R):
        a = [places(mx_ref.matmul(qu[r], mx_ref.quantize(now[r]))) for r in range(N)]
        e, own, sent = [], [], []
        for r in range(N):
            b = a[r ^ STEP[t]]
            la, lb, ua, ub, odd = neighbours(a[r], b)
            for k in range(2): now[r] = toggle(now[r], la, lb, ua, ub, odd == k)
            e.append(np.argsort(-(a[r] + b), axis=1, kind="stable")[:, :A])
            own.append(gcols(now[r], e[r]))
            sent.append(mx_ref.quantize(own[r]))
        for r in range(N):
            q = sent[r ^ STEP[t]]
            h = tile([mx_ref.matmul(pick(lay[r], np.arange(128 * i, 128 * i + 128)), q) * np.float32(0.015625) + own[r][:, i::4].astype(np.float32) for i in range(4)])
            now[r] = gput(now[r], e[r], h)
    y = np.zeros((N, 128, C), np.float32)
    oc, osc = np.zeros((N, 128, 4 * C), np.uint8), np.zeros((N, 16, C), np.uint8)
    for r in range(N):
        q = mx_ref.quantize(now[r])
        y[r] = mx_ref.matmul(mx_ref.quantize(v[r]), q)
        oc[r], osc[r] = emit(q)
    return {"y": y, "oc": oc, "osc": osc}

@@ -1,0 +1,547 @@
+from concourse.mybir import dt, AluOpType, ActivationFunctionType
+
+C = 320
+A = 160
+STEP = [1, 2, 1]
+NB = 20
+PW = 224
+KS = 8192.0
+OFF = 3 * 2 ** 20
+TOP = 3 * 2 ** 21 + 511
+SH = float(2 ** 23)
+HUGE = float(2 ** 26)
+F32, BF, U16, I32, F16 = "float32", "bfloat16", "uint16", "int32", "float16"
+Q4, U8 = "float8_e4m3fn_x4", "uint8"
+PAR = {"nv": 13,
+       "both": [(0, 1, 3, 1), (0, 0, 3, 1), (0, 1, 1, 1), (0, 0, 1, 1), (0, 1, 2, 0), (0, 0, 2, 0), (0, 1, 2, 1), (0, 0, 2, 1),
+                (1, 1, 3, 1), (1, 0, 3, 1), (1, 1, 1, 1), (1, 0, 1, 1), (1, 1, 2, 0), (1, 0, 2, 0), (1, 1, 1, 0), (1, 0, 3, 0)],
+       "onv": [["x_2", "x_3", "y0_2", "y0_3", "bph", "ft3"], ["x_2", "x_3", "ft3", "y0_3", "ft2", "y0_2"]],
+       "lift": {(0, "ds"): -4000, (1, "ds"): -3000, (0, "op"): -4000, (0, "oy"): -4000, (1, "oy"): -4000, (0, "bp"): 2000, (1, "bp"): 2000,
+                (0, "D1"): 2000, (1, "D1"): 2000, (1, "sw"): -2000},
+       "cyc": 1.04, "tt": 1.0, "gat": 1.56, "sca": 3.8, "sfix": 100.0, "wake": 80.0, "far": 2200.0, "issue": 400.0, "first": 1500.0,
+       "tries": 250}
+
+
+def _sb(n, d):
+    return ("sbuf", [128, n], d)
+
+
+SCRATCH = {
+    "x0": _sb(4 * C, BF), "x1": _sb(4 * C, BF), "ub": _sb(512, BF), "vb": _sb(512, BF),
+    "uq": _sb(128, Q4), "us": _sb(128, U8), "urq": _sb(128, Q4), "urs": _sb(128, U8),
+    "vq": _sb(128, Q4), "vs": _sb(128, U8), "wq": _sb(512, Q4), "wsc": _sb(512, U8),
+    "xq": _sb(C, Q4), "xs": _sb(C, U8),
+    "fq0": _sb(A, Q4), "fs0": _sb(A, U8), "fq1": _sb(A, Q4), "fs1": _sb(A, U8), "fq2": _sb(A, Q4), "fs2": _sb(A, U8),
+    "lq0": _sb(A, Q4), "ls0": _sb(A, U8), "lq1": _sb(A, Q4), "ls1": _sb(A, U8), "lq2": _sb(A, Q4), "ls2": _sb(A, U8),
+    "pa": ("psum", [128, 512], F32), "pb": ("psum", [128, 512], F32), "pw": ("psum", [128, 2048], F32),
+    "pi": _sb(16, I32), "pj": _sb(16, I32), "qc": _sb(16, F32), "q16": _sb(C, F32), "meq": _sb(C, BF), "keep": _sb(C, BF),
+    "c0a": _sb(C, F32), "c0b": _sb(C, F32), "c0": _sb(C, BF), "c0h": _sb(C, BF), "ur16": _sb(8, U16),
+    "iot": _sb(C, F32), "t512": _sb(2 * C, F32), "rho": _sb(2 * C, F32), "rhm": _sb(2 * C, F32), "phi": _sb(C, F32), "nstep": _sb(C, BF),
+    "m16": _sb(NB, F32), "c16": _sb(NB, F32), "self2": _sb(80, F32), "selfa": _sb(NB, F32), "cwin": _sb(80, F32),
+    "kwin": _sb(40, F32), "addc": _sb(80, F32), "cl16": _sb(80, U16), "cw": _sb(32 * 16, F32), "ci": _sb(16, I32),
+    "kp": _sb(PW, BF), "cpa": _sb(2 * PW, F32),
+    "dm": _sb(C, F32), "hold": _sb(C, F32), "eq": _sb(C, BF), "eqs": _sb(C, BF), "cmp": _sb(15 * C, BF), "cs": _sb(15 * C, F16),
+    "sg": _sb(9 * C, BF), "junk": _sb(19 * C, BF), "acc": _sb(32, F32), "sm1": _sb(32, F32), "aw": _sb(NB, F32),
+    "a16": _sb(72, U16), "b16": _sb(72, U16), "o16": _sb(72, U16), "ob16": _sb(72, U16), "dsn": _sb(36, F32), "dld": _sb(36, F32),
+    "n16": _sb(120, U16), "nl16": _sb(120, U16),
+    "orow": _sb(C, F32), "dg": _sb(2 * C, F32), "dh": _sb(4 * C, F16), "rrow": _sb(C, F32), "frow": _sb(C, F16), "oph": _sb(C, F16),
+    "oy16": _sb(80, U16), "krow": _sb(C, F32), "kw": _sb(80, F32), "sum16": _sb(NB, U16),
+    "brow": _sb(C, F32), "bph": _sb(C, F16), "kbw": _sb(40, F32), "bw16": _sb(NB, U16), "w8": _sb(NB, F32), "pbw": _sb(80, F32),
+    "addw": _sb(120, F32), "qv": _sb(PW, F32), "cb": _sb(PW, BF), "cab": _sb(2 * PW, F32), "pr": _sb(2 * PW, F32), "prc": _sb(PW, BF),
+    "mm": _sb(C, BF), "ma": _sb(C, F32), "rows": _sb(3 * C, F32), "gr": _sb(2 * C, F32), "gh": _sb(C, F16),
+    "gd": _sb(2 * C, F32), "seed": _sb(72, F32), "zi": _sb(96, I32), "xi": _sb(96, I32), "sml": _sb(400, F32), "ev": _sb(40, F32),
+    "l16": _sb(160, U16), "sw": _sb(140, F32), "s16": _sb(NB, U16), "erow": _sb(C, F32), "e16": _sb(10, U16), "loc16": _sb(NB, U16),
+    "y0": _sb(4 * C, BF), "y1": _sb(4 * C, BF), "y2": _sb(4 * C, BF), "gg": _sb(32 * C, BF), "lu": _sb(16 * C, BF), "vv": _sb(8 * C, BF),
+    "ft": _sb(4 * A, BF), "f64": _sb(4 * A, BF), "zz": _sb(4 * 480, BF), "yo": _sb(C, F32),
+}
+SEMAPHORES = (["sv", "ss", "st", "sp", "ldx", "ldu", "ldw", "lds", "ldv", "sto", "loc"]
+              + ["r%s%d" % (k, t) for k in "aonsf" for t in range(3)])
+
+ADD, SUB, MUL, MAX, MIN = AluOpType.add, AluOpType.subtract, AluOpType.mult, AluOpType.max, AluOpType.min
+GE, GT, LT, EQ = AluOpType.is_ge, AluOpType.is_gt, AluOpType.is_lt, AluOpType.is_equal
+AND = AluOpType.bitwise_and
+AF = ActivationFunctionType
+ORDER = {}
+
+
+def _mask(engines):
+    m = 0
+    for e in engines:
+        m |= 1 << e
+    return m
+
+
+def build(g, rank, T, topo):
+    core = T.cores[rank]
+    V, S, P, Y = g.vector, g.scalar, g.tensor, g.sync
+    NV = PAR["nv"]
+    NS = NB - NV
+    cyc, TB = PAR["cyc"], PAR["tt"] * C
+    ops, wrote, read, arrive, side = [], {}, {}, {}, [0]
+
+    def add(alts, r, w, sem=None, late=0.0, out=None):
+        r, w = r.split(), w.split()
+        q = list(alts)[0] if len(alts) == 1 else "v" if w[0] in PAR["onv"][side[0]] else "s"
+        pre = set(wrote[k] for k in r + w if k in wrote)
+        for k in w:
+            pre.update(read.get(k, []))
+        ops.append({"alts": {q: alts[q]}, "pre": sorted(pre), "far": [k for k in r if k in arrive], "sem": sem, "late": late, "out": out,
+                    "w": (side[0], w[0] if w else "")})
+        for k in r:
+            read.setdefault(k, []).append(len(ops) - 1)
+        for k in w:
+            wrote[k] = len(ops) - 1
+            read[k] = []
+
+    def vec(make, r, w, c):
+        add({"v": (make, max(64, c) * cyc)}, r, w)
+
+    def pick(n):
+        return 50 / cyc + n * PAR["gat"]
+
+    def ts(o, i, s1, s2, o0, o1, r, w, c=64):
+        if o1 is None:
+            vec(lambda: V.tensor_scalar(o, i, s1, None, o0), r, w, c)
+        else:
+            vec(lambda: V.tensor_scalar(o, i, s1, s2, o0, o1), r, w, c)
+
+    def tt(o, a, b, o0, r, w, c=64):
+        vec(lambda: V.tensor_tensor(o, a, b, o0), r, w, c)
+
+    def cp(o, i, r, w, c=64):
+        vec(lambda: V.tensor_copy(o, i), r, w, c)
+
+    def scan(o, a, b, o0, o1, r, w, c):
+        vec(lambda: V.tensor_tensor_scan(o, a, b, 0.0, o0, o1), r, w, c)
+
+    def fill(o, x, w, c=64):
+        vec(lambda: V.memset(o, x), "", w, c)
+
+    def quant(o, s, i, n, r, w):
+        add({"v": (lambda: V.quantize_mx(o, s, i), 12 + 1.1 * n)}, r, w)
+
+    def mm(o, a, sa, b, sb, n, r, w):
+        add({"t": (lambda: P.matmul_mx(o, a, sa, b, sb, True, True), (n + 16) * 0.83)}, r, w)
+
+    def act(o, i, f, r, w, n, **k):
+        add({"s": (lambda: S.activation(o, i, f, **k), PAR["sfix"] + n * cyc + (20 if "accum_out" in k else 0))}, r, w)
+
+    def gat(o, win, off, r, w, n=C, scale=None):
+        i = win.indirect(off)
+        if scale is None:
+            alts = {"s": lambda: S.activation(o, i, AF.Copy), "v": lambda: V.tensor_copy(o, i)}
+        else:
+            alts = {"s": lambda: S.activation(o, i, AF.Copy, scale=scale), "v": lambda: V.tensor_scalar(o, i, scale, None, MUL)}
+        add({"s": (alts["s"], pick(n) * cyc + 15), "v": (alts["v"], pick(n) * cyc)}, r, w)
+
+    def iota(o, pat, base, cm, w, flt=True):
+        n = 1
+        for z in pat:
+            n *= z[1]
+        if flt:
+            add({"g": (lambda: g.iota(o, pat, base, cm, allow_small_or_imprecise_dtypes=True), 130 + 2 * n * cyc)}, "", w)
+        else:
+            add({"g": (lambda: g.iota(o, pat, base, cm), 130 + 2 * n * cyc)}, "", w)
+
+    def dma(q, o, i, r, w, sem, size):
+        add({q: (lambda: {"s": S, "y": Y}[q].dma_start(o, i), 100.0)}, r, w, sem, 1800 + size / 150.0)
+
+    def diag(o, i, n, r, w):
+        scan(o, T.c0[:, 0:n], i, ADD, MIN, r + " c0", w, n)
+
+    def diag2(k, i, r, w):
+        scan(T.dh[:, C * k:C * k + C], T.c0h[:], i, ADD, MIN, r + " c0h", w, C / 2)
+        return T.dh[:, C * k + 15:C * k + C:16]
+
+    def send(dst, src, sem, peer, engines, r, w, size, before=0):
+        rid, pid, _ = topo.addr(T.cores[peer])
+        n = len(engines)
+        add({"g": (lambda: g.remote_dma(dst, src, T.sem[sem], T.sem.loc, pid, rid, _mask(engines)),
+                   PAR["issue"] + (0 if arrive else PAR["first"]))}, r, "", "far", PAR["far"] - PAR["issue"] + size / 150.0, (peer, w, n, sem))
+        arrive[w] = (sem, before + n)
+
+    QF, SHC, Q20, Q513 = [T.qc[:, k:k + 1] for k in range(4)]
+    SHH = T.qc[:, 8:9]
+    u8, u32 = dt.uint8, dt.uint32
+    sides = [0 if rank < (rank ^ s) else 1 for s in STEP]
+
+    dma("s", T.ub[:], T.u[:], "", "ub", "ldu", 131072)
+    dma("y", T.x0[:], T.x[:], "", "x0", "ldx", 458752)
+    dma("y", T.wq[:].bitcast(u8), T.wc[:], "x0", "wq", "ldw", 262144)
+    dma("y", T.wsc[:], T.ws[:], "x0", "wsc", "lds", 65536)
+    dma("y", T.vb[:], T.v[:], "x0", "vb", "ldv", 131072)
+    iota(T.pi[:, 0:1], [[0, 1]], 0, 1, "pi0", False)
+    iota(T.pi[:, 8:16], [[16, 8]], 0, 0, "pi8", False)
+    iota(T.m16[:], [[16, NB]], 0, 0, "m16")
+    iota(T.q16[:], [[0, NB], [1, 16]], 0, 0, "q16")
+    iota(T.iot[:], [[1, C]], 0, 0, "iot")
+    if 0 in sides:
+        iota(T.rho[:, 0:C], [[513, 16], [16, NB]], OFF, 0, "rho0")
+    if 1 in sides:
+        iota(T.rho[:, C:2 * C], [[-513, 16], [-16, NB]], TOP - OFF, 0, "rho1")
+    iota(T.phi[:], [[1, 16], [16, NB]], 0, 0, "phi")
+    iota(T.t512[:], [[-512, 2 * C]], 0, 0, "t512")
+    ts(T.pj[:, 0:1], T.pi[:, 0:1], 15, None, AND, None, "pi0", "pj")
+    fill(T.acc[:], 0.0, "lt gt")
+    cp(QF, T.pj[:, 0:1], "pj", "qf")
+    cp(T.ur16[:], T.pi[:, 8:16], "pi8", "ur16")
+    fill(T.kwin[:, 0:20], 1.0, "kw0")
+    fill(T.kwin[:, 20:40], 0.0, "kw1")
+    fill(T.kbw[:, 20:40], -1000.0, "kbw2")
+    fill(T.seed[:], 0.0, "seed0 seed1")
+    fill(T.nstep[:], -KS, "nstep", C / 2)
+    ts(SHC, QF, 15.0, SH, LT, MUL, "qf", "shc")
+    ts(SHH, QF, 15.0, 1024.0, LT, MUL, "qf", "shh")
+    ts(Q20, QF, 20.0, None, MUL, None, "qf", "q20")
+    ts(Q513, QF, 513.0, float(OFF), MUL, ADD, "qf", "q513")
+    ts(T.self2[:, 0:20], T.m16[:], QF, None, ADD, None, "m16 qf", "selfx")
+    ts(T.self2[:, 20:40], T.m16[:], QF, None, ADD, None, "m16 qf", "selfz")
+    cp(T.self2[:, 40:80], T.self2[:, 0:40], "selfx selfz", "selfy")
+    ts(T.c16[:], T.m16[:], 16.0, None, ADD, None, "m16", "c16")
+    ts(T.meq[:], T.q16[:], QF, None, EQ, None, "q16 qf", "meq", C)
+    ts(T.keep[:], T.q16[:], QF, None, AluOpType.not_equal, None, "q16 qf", "keep", C)
+    quant(T.uq[:], T.us[:], T.ub[:], 128, "ub", "uq")
+    quant(T.vq[:], T.vs[:], T.vb[:], 128, "vb", "vq")
+    ts(T.cl16[:, 60:80], T.m16[:], 0.0625, Q20, MUL, ADD, "m16 q20", "clf")
+    cp(T.urq[:].bitcast(u32), T.uq[:].bitcast(u32).indirect(T.ur16[:]), "uq ur16", "urq", pick(128))
+    cp(T.urs[:], T.us[:].indirect(T.ur16[:]), "uq ur16", "urs", pick(128))
+    ts(T.c0a[:], T.q16[:], QF, HUGE, EQ, MUL, "q16 qf", "c0a", C)
+    ts(T.c0b[:], T.q16[:], -1.0, QF, ADD, EQ, "q16 qf", "c0b", C)
+    ts(T.c0b[:], T.c0b[:], -SH, None, MUL, None, "c0b", "c0b", C)
+    tt(T.c0[:], T.c0a[:], T.c0b[:], ADD, "c0a c0b", "c0", 2 * C)
+    ts(T.c0h[:], T.c0[:], 1024.0 / SH, None, MUL, None, "c0", "c0h", C / 2)
+    W = [T.cw[:, 16 * k:16 * k + 14] for k in range(32)]
+    E = [T.cw[:, 16 * k + 14:16 * k + 16] for k in range(32)]
+    ts(W[0], T.self2[:, 0:14], -10.0, 1.0 / 21.0, ADD, MUL, "selfx", "W0")
+    ts(T.selfa[:], T.self2[:, 0:20], -1.0, 511.0, MUL, ADD, "selfx", "selfa")
+    cp(T.ci[:, 0:14], W[0], "W0", "ci")
+    ts(T.cwin[:, 0:20], T.m16[:], Q513, None, ADD, None, "m16 q513", "cw0")
+    ts(W[1], T.ci[:, 0:14], -21.0, None, MUL, None, "ci", "W1")
+    ts(W[2], T.ci[:, 0:14], -2.0, 19.0, MUL, ADD, "ci", "W2")
+    ts(W[3], T.ci[:, 0:14], 1.0, None, ADD, None, "ci", "W3")
+    tt(W[4], W[1], T.self2[:, 0:14], ADD, "W1 selfx", "W4")
+    ts(T.cwin[:, 20:40], T.self2[:, 0:20], float(OFF - 512), None, ADD, None, "selfx", "cw1")
+    tt(W[5], W[4], W[3], GE, "W4 W3", "W5")
+    ts(T.cwin[:, 60:80], T.selfa[:], 51200.0, None, ADD, None, "selfa", "cw3")
+    tt(W[6], W[5], W[2], MUL, "W5 W2", "W6")
+    tt(W[7], W[5], W[3], MUL, "W5 W3", "W7")
+    ts(T.cwin[:, 40:60], T.cwin[:, 0:20], -1.0, float(TOP), MUL, ADD, "cw0", "cw2")
+    tt(W[8], W[6], T.ci[:, 0:14], ADD, "W6 ci", "W8")
+    tt(W[9], W[4], W[7], SUB, "W4 W7", "W9")
+    ts(W[10], W[9], 0.5, None, LT, None, "W9", "W10")
+    ts(T.addc[:, 0:20], T.m16[:], 0.0, SHC, MUL, ADD, "m16 shc", "ac0")
+    for d in sorted(set(sides)):
+        c, b = 30 * d, 11 + 8 * d
+        sg, z = (1.0, 0.0) if d == 0 else (-1.0, 19.0)
+        n = ["V%d" % (b + k) for k in range(8)]
+        e = ["E%d" % (b + k) for k in range(8)]
+        rho, tau = T.rho[:, C * d:C * d + C], T.qc[:, 4 + d:5 + d]
+        cp(T.pbw[:, 40 * d + 20:40 * d + 40], T.cwin[:, 40 * d + 20:40 * d + 40], "cw1 cw3", "pbw2%d" % d)
+        ts(T.addw[:, 60 * d:60 * d + 20], T.m16[:], 0.0, SHC, MUL, ADD, "m16 shc", "adw0%d" % d)
+        if d == 0:
+            ts(T.addw[:, 40:60], T.m16[:], 0.0, SHH, MUL, ADD, "m16 shh", "adw20")
+        else:
+            ts(T.addc[:, 60:80], T.m16[:], 0.0625, SHH, MUL, ADD, "m16 shh", "acm")
+        ts(tau, QF, 512.0 * sg, float(OFF if d == 0 else TOP - OFF - 511), MUL, ADD, "qf", "tau%d" % d)
+        ts(T.c0a[:], rho, tau, None, LT, None, "rho%d tau%d" % (d, d), "c0a", C)
+        tt(T.rhm[:, C * d:C * d + C], rho, T.c0a[:], MUL, "rho%d c0a" % d, "rhm%d" % d, 2 * C)
+        ts(W[b], W[8], sg, z, MUL, ADD, "W8", n[0])
+        ts(W[b + 1], W[9], sg, z - sg, MUL, ADD, "W9", n[1])
+        cp(T.cl16[:, c + 14:c + 28], W[b], n[0], "clq%d" % d)
+        tt(W[b + 2], W[b], W[b + 1], SUB, n[0] + " " + n[1], n[2])
+        ts(W[b + 3], W[b + 2], 20.0, None, ADD, None, n[2], n[3])
+        tt(W[b + 4], W[b + 3], W[10], MUL, n[3] + " W10", n[4])
+        tt(W[b + 5], W[b + 4], W[b + 1], ADD, n[4] + " " + n[1], n[5])
+        cp(T.cl16[:, c:c + 14], W[b + 5], n[5], "clp%d" % d)
+        ts(E[b], T.self2[:, 0:2], 19.0, sg, MIN, MUL, "selfx", e[0])
+        ts(E[b + 1], E[b], z, None, ADD, None, e[0], e[1])
+        ts(E[b + 2], E[b + 1], 9.5, None, GT, None, e[1], e[2])
+        ts(E[b + 3], E[b + 1], -43.0, 419.0, MUL, ADD, e[1], e[3])
+        ts(E[b + 4], E[b + 1], 22.0, None, MUL, None, e[1], e[4])
+        tt(E[b + 5], E[b + 2], E[b + 3], MUL, e[2] + " " + e[3], e[5])
+        tt(E[b + 6], E[b + 5], E[b + 4], ADD, e[5] + " " + e[4], e[6])
+        cp(T.cl16[:, c + 28:c + 30], E[b + 6], e[6], "cle%d" % d)
+        gat(T.cpa[:, PW * d:PW * d + PW], T.cwin[:, 40 * d:40 * d + 40], T.cl16[:, c:c + 14], "cw0 cw1 cw2 cw3 clp%d" % d, "cpa%d" % d, PW)
+    c = 30 * sides[0]
+    gat(T.kp[:], T.kwin[:], T.cl16[:, c:c + 14], "kw0 kw1 clp%d" % sides[0], "kp", PW)
+
+    xall = "x_0 x_1 x_2 x_3"
+    for t in range(3):
+        peer = rank ^ STEP[t]
+        d = side[0] = sides[t]
+        eng = topo.engines(core, T.cores[peer])
+        half = len(eng) // 2
+        X = T.x0 if t == 0 else T.x1
+        xk = "x0" if t == 0 else xall
+        a16, b16 = T.a16[:, 24 * t:24 * t + NB], T.b16[:, 24 * t:24 * t + NB]
+        o16, ob16 = T.o16[:, 24 * t:24 * t + NB], T.ob16[:, 24 * t:24 * t + NB]
+        n16, nl16 = T.n16[:, 40 * t:40 * t + 40], T.nl16[:, 40 * t:40 * t + 40]
+        ka, kb, ko, kob, kd, kdl, kn, knl = ["%s%d" % (k, t) for k in ("a", "b", "o", "ob", "ds", "dl", "n", "nl")]
+        fq, fs, lq, ls = T["fq%d" % t], T["fs%d" % t], T["lq%d" % t], T["ls%d" % t]
+        quant(T.xq[:], T.xs[:], X[:], C, xk, "xq")
+        mm(T.pa[:, 0:C], T.urq[:], T.urs[:], T.xq[:], T.xs[:], C, "urq urs xq", "pa")
+        mm(T.pb[:, 0:C], T.urq[:], T.urs[:], T.xq[:], T.xs[:], C, "urq urs xq pa", "pb")
+        tt(T.dm[:], T.pa[:, 0:C], T.meq[:], MUL, "pa meq", "dm", C)
+        scan(T.hold[:], T.keep[:], T.dm[:], MUL, ADD, "keep dm", "hold", C)
+        for k in range(NS):
+            n = 16 * (NV + k) + 16
+            act(T.sg[:, C * k:C * k + C], T.pb[:, 0:C], AF.Sign, "pb hold", "sg%d" % k, C, bias=T.hold[:, n - 1:n], scale=-1.0)
+            act(T.junk[:, C * k:C * k + n], T.sg[:, C * k:C * k + n], AF.Relu, "sg%d lt" % k, "lt%d jk%d" % (k, k), n, accum_out=T.acc[:, k:k + 1])
+            if n < C:
+                act(T.junk[:, C * k + n:C * k + C], T.sg[:, C * k + n:C * k + C], AF.Relu, "sg%d gt" % k, "gt%d jr%d" % (k, k), C - n,
+                    scale=-1.0, accum_out=T.acc[:, 16 + k:17 + k])
+        tt(T.eq[:], T.pa[:, 0:C], T.hold[:], EQ, "pa hold", "eq", C)
+        scan(T.eqs[:], T.keep[:], T.eq[:], MUL, ADD, "keep eq", "eqs", C / 2)
+        for m in range(NV):
+            n = 16 * m + 16
+            sc, z = T.hold[:, n - 1:n], T.cmp[:, C * m:C * m + C]
+            ts(T.cmp[:, C * m:C * m + n], T.pa[:, 0:n], sc, None, GE, None, "pa hold", "cl%d_" % m, n)
+            ts(T.cmp[:, C * m + n:C * m + C], T.pa[:, n:C], sc, None, GT, None, "pa hold", "cr%d_" % m, C - n)
+            scan(T.cs[:, C * m:C * m + C], z, z, ADD, MAX, "cl%d_ cr%d_" % (m, m), "cs%d" % m, C / 2)
+        tt(T.sm1[:, 0:NS], T.c16[:, NV:NB], T.eqs[:, 16 * NV + 15:C:16], SUB, "c16 eqs", "sm1a")
+        tt(T.sm1[:, 16:16 + NS], T.acc[:, 16:16 + NS], T.acc[:, 0:NS], SUB, " ".join("lt%d gt%d" % (k, k) for k in range(NS)), "sm1b")
+        tt(T.aw[:, NV:NB], T.sm1[:, 0:NS], T.sm1[:, 16:16 + NS], ADD, "sm1a sm1b", "aw1")
+        tt(T.aw[:, 0:NV], T.cs[:, C - 1:NV * C:C], T.eqs[:, 15:16 * NV:16], SUB, "eqs " + " ".join("cs%d" % m for m in range(NV)), "aw0")
+        cp(a16, T.aw[:], "aw0 aw1", ka)
+        send(b16, a16, "ra%d" % t, peer, eng[:half] if t == 0 else eng, ka, kb, 5120)
+
+        al, kal, be, kbe = (a16, ka, b16, kb) if d == 0 else (b16, kb, a16, ka)
+        osl, kosl, opl, kopl = (o16, ko, ob16, kob) if d == 0 else (ob16, kob, o16, ko)
+        pl, ql, el = T.cl16[:, 30 * d:30 * d + 14], T.cl16[:, 30 * d + 14:30 * d + 28], T.cl16[:, 30 * d + 28:30 * d + 30]
+        kbw = "kbw0 kbw2"
+        cp(T.orow[:].indirect(a16), T.iot[:], ka + " iot", "orow", 50 + C * PAR["sca"])
+        if d == 0:
+            gat(T.oph[:], T.orow[:], T.cl16[:, 60:80], "orow clf", "oph")
+            ts(o16, diag2(0, T.oph[:], "oph", "dg0"), SHH, None, ADD, None, "dg0 shh", ko)
+        else:
+            diag(T.dg[:, 0:C], T.orow[:], C, "orow", "dh0")
+            ts(o16, T.dg[:, 15:C:16], SHC, None, ADD, None, "dh0 shc", ko)
+        send(ob16, o16, "ro%d" % t, peer, eng[half:] if t == 0 else eng, ko, kob, 5120)
+        gat(T.rrow[:], T.rhm[:, C * d:C * d + C], al, kal + " rhm%d" % d, "rrow")
+        gat(T.frow[:], T.phi[:], al, kal + " phi", "frow")
+        gat(T.brow[:], T.iot[:], be, kbe + " iot", "brow")
+        gat(T.bph[:], T.brow[:], osl, "brow " + kosl, "bph")
+        gat(T.ma[:], T.rrow[:], opl, "rrow " + kopl, "ma")
+        for k in range(4):
+            ts(T.oy16[:, NB * k:NB * k + NB], osl, 4.0, float(k), MUL, ADD, kosl, "oy%d" % k)
+            gat(T.y0[:, C * k:C * k + C], X[:], T.oy16[:, NB * k:NB * k + NB], xk + " oy%d" % k, "y0_%d" % k)
+        ts(T.kw[:, 0:20], b16, 0.0, None, ADD, None, kb, "kwa")
+        tt(T.kw[:, 20:40], T.kw[:, 0:20], T.aw[:], ADD, "kwa aw0 aw1", "kwb")
+        cp(T.sum16[:], T.kw[:, 20:40], "kwb", "sum16")
+        ts(T.kw[:, 40:60], T.kw[:, 20:40], -512.0, None, MUL, None, "kwb", "kwc")
+        tt(T.krow[:], T.t512[:].indirect(T.sum16[:]), T.iot[:], ADD, "sum16 t512 iot", "krow", 50 + 2 * C)
+        tt(T.kw[:, 60:80], T.kw[:, 40:60], T.self2[:, 0:20], ADD, "kwc selfx", "kwd")
+        dsn, dld = T.dsn[:, 12 * t:12 * t + 10], T.dld[:, 12 * t:12 * t + 10]
+        dk = " ".join("%s_%d" % (kd, k) for k in range(10))
+        for k in range(10):
+            m = 10 * d + k
+            act(T.junk[:, C * (9 + k):C * (10 + k)], T.krow[:], AF.Sign, "krow kwd", "%s_%d js%d" % (kd, k, k), C,
+                bias=T.kw[:, 60 + m:61 + m], scale=-1.0, accum_out=T.dsn[:, 12 * t + k:12 * t + k + 1])
+        send(dld, dsn, "rs%d" % t, peer, eng, dk, kdl, 5120)
+        ts(T.sw[:, 10 * d:10 * d + 10], dsn, 319.0, 0.5, ADD, MUL, dk, "sw0")
+        ts(T.sw[:, 10 - 10 * d:20 - 10 * d], dld, 319.0, 0.5, ADD, MUL, kdl, "sw1")
+        cp(T.s16[:], T.sw[:, 0:20], "sw0 sw1", "s16")
+        cp(T.erow[:].indirect(T.s16[:]), T.frow[:], "s16 frow", "erow", 50 + C * PAR["sca"])
+        diag(T.dg[:, C:C + A], T.erow[:, 0:A], A, "erow", "dg3")
+        ts(T.e16[:], T.dg[:, C + 15:C + A:16], SHC, None, ADD, None, "dg3 shc", "e16")
+        ends = diag2(1, T.bph[:], "bph", "dg1")
+        ts(T.kbw[:, 0:20], ends, SHH, 1.0 - 2 * d, ADD, MUL, "dg1 shh", "kbw0")
+        ts(T.bw16[:], ends, SHH, None, ADD, None, "dg1 shh", "bw16")
+        gat(T.qv[:], T.kbw[:], ql, kbw + " clq%d" % d, "qv", PW)
+        ts(T.w8[:], T.kbw[:, 0:20], KS, None, MUL, None, kbw, "w8")
+        if d == 1:
+            tt(T.addw[:, 100:120], T.addc[:, 60:80], T.kbw[:, 0:20], SUB, "acm kbw0", "adw21")
+        tt(T.pbw[:, 40 * d:40 * d + 20], T.w8[:], T.cwin[:, 40 * d:40 * d + 20], ADD, "w8 cw0 cw2", "pbw0")
+        tt(T.addw[:, 60 * d + 20:60 * d + 40], T.w8[:], T.addc[:, 0:20], ADD, "w8 ac0", "adw1")
+        tt(T.cb[:], T.kbw[:].indirect(pl), T.qv[:], LT, kbw + " qv clp%d" % d, "cb", 50 + 2 * PW)
+        tt(T.cab[:, 0:PW], T.cb[:], T.cpa[:, PW * d:PW * d + PW], MUL, "cb cpa%d" % d, "ca", 2 * PW)
+        tt(T.cab[:, PW:2 * PW], T.pbw[:, 40 * d:40 * d + 40].indirect(pl), T.cb[:], MUL, "cb pbw0 pbw2%d" % d, "cbb", 50 + 2 * PW)
+        scan(T.prc[:], T.kp[:], T.cb[:], MUL, ADD, "kp cb", "pr2", PW / 2)
+        scan(T.pr[:, 0:PW], T.kp[:], T.cab[:, 0:PW], MUL, MAX, "kp ca", "pr0", PW)
+        scan(T.pr[:, PW:2 * PW], T.kp[:], T.cab[:, PW:2 * PW], MUL, MAX, "kp cbb", "pr1", PW)
+
+        def along(b, k=0):
+            if d == 0:
+                return b[:, C * k:C * k + C]
+            return b[:, C * k + C - 1:C * k - 1:-1] if k else b[:, C - 1::-1]
+        ts(T.mm[:], T.ma[:], 0.5, None, GT, None, "ma", "mm", C)
+        scan(along(T.rows, 2), along(T.mm), along(T.mm), ADD, MAX, "mm", "row2", C)
+        scan(along(T.rows, 0), along(T.ma), along(T.ma), MAX, MAX, "ma", "row0", C)
+        scan(along(T.rows, 1), T.nstep[:], along(T.ma), ADD, MAX, "ma nstep", "row1", C)
+        gat(T.gh[:], T.rows[:, 2 * C:3 * C], T.bw16[:], "row2 bw16", "gr2")
+        for k in range(2):
+            gat(T.gr[:, C * k:C * k + C], T.rows[:, C * k:C * k + C], T.bw16[:], "row%d bw16" % k, "gr%d" % k)
+            diag(T.gd[:, C * k:C * k + C], T.gr[:, C * k:C * k + C], C, "gr%d" % k, "gd%d" % k)
+        ad = 60 * d
+        tt(T.seed[:, 40:60], diag2(3, T.gh[:], "gr2", "gd2"), T.addw[:, ad + 40:ad + 60], ADD, "gd2 adw2%d" % d, "seed1")
+        tt(T.zi[:, 64:96], T.prc[:].indirect(el), T.seed[:, 40:72], ADD, "pr2 cle%d seed1" % d, "zi2", 112)
+        tt(T.seed[:, 0:40], T.gd[:, 15:2 * C:16], T.addw[:, ad:ad + 40], ADD, "gd0 gd1 adw1 adw0%d" % d, "seed0", 80)
+        ts(T.xi[:, 64:84], T.zi[:, 64:84], 1, None, AND, None, "zi2", "xi2")
+        for k in range(2):
+            tt(T.zi[:, 32 * k:32 * k + 32], T.pr[:, PW * k:PW * k + PW].indirect(el), T.seed[:, 20 * k:20 * k + 32], MAX,
+               "pr%d cle%d seed0 seed1" % (k, d), "zi%d" % k, 112)
+            ts(T.ev[:, 20 * k:20 * k + 20], T.xi[:, 64:84], 1.0 - 2 * d, float(d), MUL, ADD, "xi2", "ev%d" % k)
+        ts(T.xi[:, 0:64], T.zi[:, 0:64], 511, None, AND, None, "zi0 zi1", "xi0")
+        for k in range(2):
+            o, x = T.sml[:, 20 * k:20 * k + 20], T.xi[:, 32 * k:32 * k + 20]
+            if d == 0:
+                tt(o, x, T.self2[:, 0:20], SUB, "xi0 selfx", "D0_%d" % k)
+            else:
+                tt(o, T.selfa[:], x, SUB, "xi0 selfa", "D0_%d" % k)
+        ts(n16, T.sml[:, 0:40], 512.0, None, ADD, None, "D0_0 D0_1", kn)
+        send(nl16, n16, "rn%d" % t, peer, eng, kn, knl, 10240)
+        ts(T.sml[:, 200:240], nl16, -512.0, None, ADD, None, knl, "D1_0 D1_1")
+        for j in range(2):
+            b, r = 200 * j, "D%d_0 D%d_1" % (j, j)
+            tt(T.sml[:, b + 40:b + 80], T.sml[:, b:b + 40], T.ev[:], MUL, "ev0 ev1 " + r, "ED%d" % j, 80)
+            tt(T.sml[:, b + 80:b + 120], T.sml[:, b:b + 40], T.sml[:, b + 40:b + 80], SUB, "ED%d " % j + r, "OD%d" % j, 80)
+            tt(T.sml[:, b + 120:b + 200], T.sml[:, b + 40:b + 120], T.self2[:], ADD, "ED%d OD%d selfx selfy" % (j, j), "L1%d" % j, 160)
+            cp(T.l16[:, 80 * j:80 * j + 80], T.sml[:, b + 120:b + 200], "L1%d" % j, "l16_%d" % j, 80)
+
+        for w in range(2):
+            src, dst = (T.y0, T.y1) if w == 0 else (T.y1, T.y2)
+            for k in range(4):
+                win, s = src[:, C * k:C * k + C], 4 * w + k
+                for j in range(2):
+                    c, b = 80 * j + 40 * w, C * (4 * s + 2 * j)
+                    r = "y%d_%d l16_%d" % (w, k, j)
+                    o, fold = T.lu[:, C * (2 * s + j):C * (2 * s + j + 1)], MAX if j == d else MIN
+                    gat(T.gg[:, b:b + C], win, T.l16[:, c:c + NB], r, "ga%d%d" % (s, j))
+                    if (d, w, k, j) in PAR["both"]:
+                        gat(T.gg[:, b + C:b + 2 * C], win, T.l16[:, c + NB:c + 2 * NB], r, "gb%d%d" % (s, j))
+                        tt(o, T.gg[:, b + C:b + 2 * C], T.gg[:, b:b + C], fold, "ga%d%d gb%d%d" % (s, j, s, j), "lu%d%d" % (s, j), TB)
+                    else:
+                        tt(o, win.indirect(T.l16[:, c + NB:c + 2 * NB]), T.gg[:, b:b + C], fold, r + " ga%d%d" % (s, j), "lu%d%d" % (s, j),
+                           max(pick(C), 50 + TB))
+                tt(T.vv[:, C * s:C * s + C], T.lu[:, 2 * C * s:2 * C * s + C], T.lu[:, 2 * C * s + C:2 * C * s + 2 * C], ADD,
+                   "lu%d0 lu%d1" % (s, s), "vv%d" % s, TB)
+                tt(dst[:, C * k:C * k + C], T.vv[:, C * s:C * s + C], win, SUB, "vv%d y%d_%d" % (s, w, k), "y%d_%d" % (w + 1, k), TB)
+        for k in range(4):
+            gat(T.ft[:, k:4 * A:4], T.y2[:, C * k:C * k + C], T.e16[:], "y2_%d e16" % k, "ft%d" % k, A)
+        fts = "ft0 ft1 ft2 ft3"
+        quant(fq[:], fs[:], T.ft[:], A, fts, "fq%d" % t)
+        send(lq[:].bitcast(u8), fq[:].bitcast(u8), "rf%d" % t, peer, eng, "fq%d" % t, "lc%d" % t, 81920, len(eng))
+        send(ls[:], fs[:], "rf%d" % t, peer, eng, "fq%d" % t, "lq%d" % t, 20480, len(eng))
+
+        ts(T.f64[:], T.ft[:], 64.0, None, MUL, None, fts, "f64", 2 * A)
+        for k in range(4):
+            act(T.zz[:, 480 * k:480 * k + C], T.y2[:, C * k:C * k + C], AF.Copy, "y2_%d fq%d" % (k, t), "zy%d" % k, C, scale=64.0)
+        late = " fq%d" % t
+        ts(T.sw[:, 20:40], diag2(2, T.frow[:], "frow" + late, "dg2"), SHH, None, ADD, None, "dg2 shh", "swf")
+        ts(T.sw[:, 40:60], T.sw[:, 0:20], float(C), None, ADD, None, "sw0 sw1" + late, "swp")
+        ts(T.sw[:, 60:80], T.sw[:, 0:20], float(A), None, LT, None, "sw0 sw1" + late, "swl")
+        tt(T.sw[:, 80:100], T.sw[:, 40:60], T.sw[:, 20:40], SUB, "swp swf", "swd")
+        tt(T.sw[:, 100:120], T.sw[:, 80:100], T.sw[:, 60:80], MUL, "swd swl", "swe")
+        tt(T.sw[:, 120:140], T.sw[:, 100:120], T.sw[:, 20:40], ADD, "swe swf", "swg")
+        cp(T.loc16[:], T.sw[:, 120:140], "swg", "loc16")
+        for k in range(4):
+            mm(T.pw[:, 512 * k:512 * k + A], T.wq[:, 128 * k:128 * k + 128], T.wsc[:, 128 * k:128 * k + 128], lq[:], ls[:], A,
+               "wq wsc lc%d lq%d" % (t, t), "pw%d" % k)
+            tt(T.zz[:, 480 * k + C:480 * k + 480], T.pw[:, 512 * k:512 * k + A], T.f64[:, k:4 * A:4], ADD, "pw%d f64" % k, "zh%d" % k, A)
+            gat(T.x1[:, k:4 * C:4], T.zz[:, 480 * k:480 * k + 480], T.loc16[:], "zy%d zh%d loc16" % (k, k), "x_%d" % k, C, 0.015625)
+
+    quant(T.xq[:], T.xs[:], T.x1[:], C, xall, "xq")
+    mm(T.pa[:, 0:A], T.vq[:], T.vs[:], T.xq[:, 0:A], T.xs[:, 0:A], A, "vq xq", "pa")
+    mm(T.pb[:, 0:A], T.vq[:], T.vs[:], T.xq[:, A:C], T.xs[:, A:C], A, "vq xq", "pb")
+    dma("y", T.oc[:], T.xq[:].bitcast(u8), "xq", "", "sto", 163840)
+    for k in range(4):
+        dma("ys"[k % 2], T.osc[4 * k:4 * k + 4, :], T.xs[32 * k:32 * k + 4, :], "xq", "", "sto", 1280)
+    cp(T.yo[:, 0:A], T.pa[:, 0:A], "pa", "yo0", A)
+    act(T.yo[:, A:C], T.pb[:, 0:A], AF.Copy, "pb", "yo1", A)
+    dma("y", T.y[:, 0:A], T.yo[:, 0:A], "yo0", "", "sto", 81920)
+    dma("s", T.y[:, A:C], T.yo[:, A:C], "yo1", "", "sto", 81920)
+    return ops, arrive
+
+
+def arrange(progs):
+    wake = PAR["wake"]
+    node, at = [], {}
+    for r, (ops, _) in enumerate(progs):
+        for i, o in enumerate(ops):
+            at[(r, i)] = len(node)
+            q = list(o["alts"])[0]
+            node.append((r, i, q, o["alts"][q][1], o["late"] + wake, (o["w"][0], o["w"][1][:2])))
+    pre = [[at[(z[0], p)] for p in progs[z[0]][0][z[1]]["pre"]] for z in node]
+    for n, z in enumerate(node):
+        out = progs[z[0]][0][z[1]]["out"]
+        if out:
+            for j, o in enumerate(progs[out[0]][0]):
+                if out[1] in o["far"]:
+                    pre[at[(out[0], j)]].append(n)
+    suc = [[] for _ in node]
+    for n in range(len(node)):
+        for p in pre[n]:
+            suc[p].append(n)
+
+    def run(before, after, weight, back):
+        left = [len(b) for b in before]
+        ready = {}
+        for n in range(len(node)):
+            if not left[n]:
+                ready.setdefault((node[n][0], node[n][2]), {})[n] = node[n][4] if back else 0.0
+        done, free, order = [0.0] * len(node), {}, []
+        while len(order) < len(node):
+            t0, q = min((max(min(w.values()), free.get(k, 0.0)), k) for k, w in ready.items() if w)
+            n = max((z for z, x in ready[q].items() if x <= t0), key=lambda z: (weight[z], -z))
+            del ready[q][n]
+            done[n] = free[q] = t0 + node[n][3]
+            order.append(n)
+            for s in after[n]:
+                left[s] -= 1
+                if not left[s]:
+                    ready.setdefault((node[s][0], node[s][2]), {})[s] = max(done[p] + (node[s][4] if back else node[p][4]) for p in before[s])
+        return done, order, max(done[n] + (0.0 if back else node[n][4]) for n in range(len(node)))
+
+    rest = run(suc, pre, run(pre, suc, [-n for n in range(len(node))], False)[0], True)[0]
+    kinds = sorted(set(z[5] for z in node if z[2] in "vs" and z[1] > 110))
+    lift, best, seed = dict(PAR["lift"]), None, 12345
+    for k in range(PAR["tries"] + 1):
+        trial = dict(lift)
+        if k:
+            seed = (seed * 1103515245 + 12345) % 2 ** 31
+            kind = kinds[(seed >> 8) % len(kinds)]
+            step = (-4000, -2000, -1000, -400, 400, 1000, 2000, 4000)[(seed >> 20) % 8]
+            for z in ([kind] if (seed >> 24) % 2 else [(0, kind[1]), (1, kind[1])]):
+                trial[z] = trial.get(z, 0) + step
+        done, order, end = run(pre, suc, [x + trial.get(z[5], 0) for x, z in zip(rest, node)], False)
+        if best is None or end < best[1]:
+            lift, best = trial, (order, end)
+    return [[(node[n][1], node[n][2]) for n in best[0] if node[n][0] == r] for r in range(len(progs))], best[1]
+
+
+def rank_program(g, core, T, topo):
+    rank = T.rank_of(core)
+    if rank is None:
+        return
+    if "order" not in ORDER:
+        ORDER["order"] = arrange([build(g, r, T, topo) for r in range(len(T.cores))])[0]
+    ops, arrive = build(g, rank, T, topo)
+    queue = {"v": g.vector, "s": g.scalar, "t": g.tensor, "g": g, "y": g.sync}
+    own = {"v": "sv", "s": "ss", "t": "st", "g": "sp"}
+    count = {}
+    known = {q: {} for q in queue}
+    clocks, token = {}, {}
+    for i, q in ORDER["order"][rank]:
+        o = ops[i]
+        need = {}
+        for s, n in [token[p] for p in o["pre"]] + [arrive[k] for k in o["far"]]:
+            need[s] = max(need.get(s, 0), n)
+        for s, n in sorted(need.items(), key=lambda z: -len(clocks.get(z, {}))):
+            if known[q].get(s, 0) < n:
+                queue[q].wait_ge(T.sem[s], n)
+                known[q][s] = n
+                for s2, n2 in clocks.get((s, n), {}).items():
+                    known[q][s2] = max(known[q].get(s2, 0), n2)
+        ins = o["alts"][q][0]()
+        if o["out"]:
+            count["loc"] = count.get("loc", 0) + o["out"][2]
+            continue
+        s, n = (o["sem"], 16) if o["sem"] else (own[q], 1)
+        ins.then_inc(T.sem[s], n)
+        count[s] = count.get(s, 0) + n
+        token[i] = (s, count[s])
+        clocks[token[i]] = dict(known[q])
+    for s, n in arrive.values():
+        count[s] = max(count.get(s, 0), n)
+    for s in sorted(count):
+        g.wait_ge(T.sem[s], count[s])

@@ -12,14 +12,17 @@ SH = float(2 ** 23)
 HUGE = float(2 ** 26)
 F32, BF, U16, I32, F16 = "float32", "bfloat16", "uint16", "int32", "float16"
 Q4, U8 = "float8_e4m3fn_x4", "uint8"
-PAR = {"nv": 13,
-       "both": [(0, 1, 3, 1), (0, 0, 3, 1), (0, 1, 1, 1), (0, 0, 1, 1), (0, 1, 2, 0), (0, 0, 2, 0), (0, 1, 2, 1), (0, 0, 2, 1),
-                (1, 1, 3, 1), (1, 0, 3, 1), (1, 1, 1, 1), (1, 0, 1, 1), (1, 1, 2, 0), (1, 0, 2, 0), (1, 1, 1, 0), (1, 0, 3, 0)],
-       "onv": [["x_2", "x_3", "y0_2", "y0_3", "bph", "ft3"], ["x_2", "x_3", "ft3", "y0_3", "ft2", "y0_2"]],
-       "lift": {(0, "ds"): -4000, (1, "ds"): -3000, (0, "op"): -4000, (0, "oy"): -4000, (1, "oy"): -4000, (0, "bp"): 2000, (1, "bp"): 2000,
-                (0, "D1"): 2000, (1, "D1"): 2000, (1, "sw"): -2000},
-       "cyc": 1.04, "tt": 1.0, "gat": 1.56, "sca": 3.8, "sfix": 100.0, "wake": 80.0, "far": 2200.0, "issue": 400.0, "first": 1500.0,
-       "tries": 250}
+PAR = {"nv": 14,
+       "both": [(1, "a1")], "run": [1, 1],
+       "plain": [(d, z) for d in range(2) for z in ("a0", "a2", "b0", "c2")] + [(0, "b1"), (1, "b2")],
+       "onv": [["x_21", "x_31", "x_30", "gr1", "gr2", "y0_1", "y0_2", "yeb3"], ["x_21", "x_31", "x_30", "gr0", "gr1", "gr2", "y0_0"]],
+       "lift": {(0, "ds"): -3000, (1, "ds"): -3000, (0, "dg"): -300, (1, "dg"): -300, (1, "cl"): -700, (0, "fr"): -700, (1, "fr"): -700,
+                (0, "y0"): -700, (1, "y0"): -700, (1, "pr"): 700, (1, "se"): 1500, (1, "cr0_"): 1500, (0, "cl9"): -700, (0, "cr1"): -4500,
+                (0, "kw"): 1500, (1, "kw"): 1500, (1, "cr1"): -1500, (0, "cr2_"): 700, (0, "x_30"): 1500, (1, "x_30"): 1500, (0, "gac11"): 1500},
+       "also": [{"cyc": 0.83, "wake": 150.0, "gat": 1.3, "sca": 3.0}, {"cyc": 1.15, "wake": 80.0, "gat": 1.9, "sca": 5.0}],
+       "weigh": [1.0, 0.96, 1.3],
+       "scn": 1.0, "cyc": 0.9, "tt": 1.0, "gat": 1.56, "sca": 3.8, "sfix": 100.0, "wake": 110.0, "far": 2200.0, "issue": 400.0, "first": 1500.0,
+       "tries": 1000}
 
 
 def _sb(n, d):
@@ -34,28 +37,29 @@ SCRATCH = {
     "fq0": _sb(A, Q4), "fs0": _sb(A, U8), "fq1": _sb(A, Q4), "fs1": _sb(A, U8), "fq2": _sb(A, Q4), "fs2": _sb(A, U8),
     "lq0": _sb(A, Q4), "ls0": _sb(A, U8), "lq1": _sb(A, Q4), "ls1": _sb(A, U8), "lq2": _sb(A, Q4), "ls2": _sb(A, U8),
     "pa": ("psum", [128, 512], F32), "pb": ("psum", [128, 512], F32), "pw": ("psum", [128, 2048], F32),
-    "pi": _sb(16, I32), "pj": _sb(16, I32), "qc": _sb(16, F32), "q16": _sb(C, F32), "meq": _sb(C, BF), "keep": _sb(C, BF),
-    "c0a": _sb(C, F32), "c0b": _sb(C, F32), "c0": _sb(C, BF), "c0h": _sb(C, BF), "ur16": _sb(8, U16),
+    "pi": _sb(32, I32), "qc": _sb(16, F32), "q16": _sb(C, F32), "meq": _sb(C, BF), "keep": _sb(C, BF),
+    "c0a": _sb(C, F32), "c0b": _sb(C + 16, BF), "c0": _sb(C, BF), "c0h": _sb(C, BF), "ur16": _sb(8, U16),
     "iot": _sb(C, F32), "t512": _sb(2 * C, F32), "rho": _sb(2 * C, F32), "rhm": _sb(2 * C, F32), "phi": _sb(C, F32), "nstep": _sb(C, BF),
     "m16": _sb(NB, F32), "c16": _sb(NB, F32), "self2": _sb(80, F32), "selfa": _sb(NB, F32), "cwin": _sb(80, F32),
     "kwin": _sb(40, F32), "addc": _sb(80, F32), "cl16": _sb(80, U16), "cw": _sb(32 * 16, F32), "ci": _sb(16, I32),
     "kp": _sb(PW, BF), "cpa": _sb(2 * PW, F32),
     "dm": _sb(C, F32), "hold": _sb(C, F32), "eq": _sb(C, BF), "eqs": _sb(C, BF), "cmp": _sb(15 * C, BF), "cs": _sb(15 * C, F16),
     "sg": _sb(9 * C, BF), "junk": _sb(19 * C, BF), "acc": _sb(32, F32), "sm1": _sb(32, F32), "aw": _sb(NB, F32),
-    "a16": _sb(72, U16), "b16": _sb(72, U16), "o16": _sb(72, U16), "ob16": _sb(72, U16), "dsn": _sb(36, F32), "dld": _sb(36, F32),
-    "n16": _sb(120, U16), "nl16": _sb(120, U16),
-    "orow": _sb(C, F32), "dg": _sb(2 * C, F32), "dh": _sb(4 * C, F16), "rrow": _sb(C, F32), "frow": _sb(C, F16), "oph": _sb(C, F16),
+    "a16": _sb(72, U16), "b16": _sb(72, U16), "o16": _sb(72, U16), "ob16": _sb(72, U16), "dsn": _sb(36, F32), "s16": _sb(72, U16), "sl16": _sb(48, U16),
+    "n16": _sb(240, U16), "nl16": _sb(120, U16), "p16": _sb(120, U16), "pl16": _sb(120, U16),
+    "orow": _sb(C, BF), "dg": _sb(4 * C, F32), "dh": _sb(4 * C, F16), "rrow": _sb(C, F32), "hf": _sb(4 * C, F16),
     "oy16": _sb(80, U16), "krow": _sb(C, F32), "kw": _sb(80, F32), "sum16": _sb(NB, U16),
-    "brow": _sb(C, F32), "bph": _sb(C, F16), "kbw": _sb(40, F32), "bw16": _sb(NB, U16), "w8": _sb(NB, F32), "pbw": _sb(80, F32),
+    "brow": _sb(C, F32), "kbw": _sb(40, F32), "bw16": _sb(NB, U16), "w8": _sb(NB, F32), "pbw": _sb(80, F32),
     "addw": _sb(120, F32), "qv": _sb(PW, F32), "cb": _sb(PW, BF), "cab": _sb(2 * PW, F32), "pr": _sb(2 * PW, F32), "prc": _sb(PW, BF),
-    "mm": _sb(C, BF), "ma": _sb(C, F32), "rows": _sb(3 * C, F32), "gr": _sb(2 * C, F32), "gh": _sb(C, F16),
-    "gd": _sb(2 * C, F32), "seed": _sb(72, F32), "zi": _sb(96, I32), "xi": _sb(96, I32), "sml": _sb(400, F32), "ev": _sb(40, F32),
-    "l16": _sb(160, U16), "sw": _sb(140, F32), "s16": _sb(NB, U16), "erow": _sb(C, F32), "e16": _sb(10, U16), "loc16": _sb(NB, U16),
-    "y0": _sb(4 * C, BF), "y1": _sb(4 * C, BF), "y2": _sb(4 * C, BF), "gg": _sb(32 * C, BF), "lu": _sb(16 * C, BF), "vv": _sb(8 * C, BF),
-    "ft": _sb(4 * A, BF), "f64": _sb(4 * A, BF), "zz": _sb(4 * 480, BF), "yo": _sb(C, F32),
+    "mm": _sb(2 * C, BF), "ma": _sb(C, F32), "rows": _sb(2 * C, F32), "gr": _sb(2 * C, F32),
+    "gd": _sb(2 * C, F32), "seed": _sb(72, F32), "zi": _sb(120, I32), "zf": _sb(52, F32), "ev": _sb(80, F32),
+    "own": _sb(80, F32), "li": _sb(80, I32), "lj": _sb(120, I32), "pk": _sb(3 * C, F32),
+    "iotc": _sb(C, BF), "erow": _sb(C, BF), "e16": _sb(NB, U16),
+    "y0": _sb(4 * C, BF), "y1": _sb(4 * C, BF), "ye": _sb(4 * C, BF), "ga": _sb(16 * C, BF), "gb": _sb(16 * C, BF), "vw": _sb(8 * C, BF),
+    "d0": _sb(24 * C, BF), "d1": _sb(24 * C, BF), "vv": _sb(12 * C, BF), "ft": _sb(4 * A, BF), "f64": _sb(4 * A, BF), "zz": _sb(4 * C, BF), "yo": _sb(C, F32),
 }
-SEMAPHORES = (["sv", "ss", "st", "sp", "ldx", "ldu", "ldw", "lds", "ldv", "sto", "loc"]
-              + ["r%s%d" % (k, t) for k in "aonsf" for t in range(3)])
+SEMAPHORES = (["sv", "ss", "st", "sp", "ldx", "ldz", "ldu", "ldw", "lds", "ldv", "sto", "loc"]
+              + ["r%s%d" % (k, t) for k in "aopnsf" for t in range(3)])
 
 ADD, SUB, MUL, MAX, MIN = AluOpType.add, AluOpType.subtract, AluOpType.mult, AluOpType.max, AluOpType.min
 GE, GT, LT, EQ = AluOpType.is_ge, AluOpType.is_gt, AluOpType.is_lt, AluOpType.is_equal
@@ -111,8 +115,8 @@ def build(g, rank, T, topo):
     def cp(o, i, r, w, c=64):
         vec(lambda: V.tensor_copy(o, i), r, w, c)
 
-    def scan(o, a, b, o0, o1, r, w, c):
-        vec(lambda: V.tensor_tensor_scan(o, a, b, 0.0, o0, o1), r, w, c)
+    def scan(o, a, b, o0, o1, r, w, c, first=0.0):
+        vec(lambda: V.tensor_tensor_scan(o, a, b, first, o0, o1), r, w, c * PAR["scn"])
 
     def fill(o, x, w, c=64):
         vec(lambda: V.memset(o, x), "", w, c)
@@ -126,10 +130,16 @@ def build(g, rank, T, topo):
     def act(o, i, f, r, w, n, **k):
         add({"s": (lambda: S.activation(o, i, f, **k), PAR["sfix"] + n * cyc + (20 if "accum_out" in k else 0))}, r, w)
 
-    def gat(o, win, off, r, w, n=C, scale=None):
+    def lin(o, i, scale, bias, r, w, n=NB):
+        add({"s": (lambda: S.activation(o, i, AF.Identity, bias=bias, scale=scale), PAR["sfix"] + n * cyc),
+             "v": (lambda: V.tensor_scalar(o, i, scale, bias, MUL, ADD), max(64, n) * cyc)}, r, w)
+
+    def gat(o, win, off, r, w, n=C, scale=None, bias=None):
         i = win.indirect(off)
         if scale is None:
             alts = {"s": lambda: S.activation(o, i, AF.Copy), "v": lambda: V.tensor_copy(o, i)}
+        elif bias is not None:
+            alts = {"s": lambda: S.activation(o, i, AF.Identity, bias=bias, scale=scale), "v": lambda: V.tensor_scalar(o, i, scale, bias, MUL, ADD)}
         else:
             alts = {"s": lambda: S.activation(o, i, AF.Copy, scale=scale), "v": lambda: V.tensor_scalar(o, i, scale, None, MUL)}
         add({"s": (alts["s"], pick(n) * cyc + 15), "v": (alts["v"], pick(n) * cyc)}, r, w)
@@ -158,7 +168,11 @@ def build(g, rank, T, topo):
         n = len(engines)
         add({"g": (lambda: g.remote_dma(dst, src, T.sem[sem], T.sem.loc, pid, rid, _mask(engines)),
                    PAR["issue"] + (0 if arrive else PAR["first"]))}, r, "", "far", PAR["far"] - PAR["issue"] + size / 150.0, (peer, w, n, sem))
-        arrive[w] = (sem, before + n)
+        if before is not None:
+            expect(sem, w, before + n)
+
+    def expect(sem, w, n):
+        arrive[w] = (sem, n)
 
     QF, SHC, Q20, Q513 = [T.qc[:, k:k + 1] for k in range(4)]
     SHH = T.qc[:, 8:9]
@@ -166,10 +180,11 @@ def build(g, rank, T, topo):
     sides = [0 if rank < (rank ^ s) else 1 for s in STEP]
 
     dma("s", T.ub[:], T.u[:], "", "ub", "ldu", 131072)
-    dma("y", T.x0[:], T.x[:], "", "x0", "ldx", 458752)
-    dma("y", T.wq[:].bitcast(u8), T.wc[:], "x0", "wq", "ldw", 262144)
-    dma("y", T.wsc[:], T.ws[:], "x0", "wsc", "lds", 65536)
-    dma("y", T.vb[:], T.v[:], "x0", "vb", "ldv", 131072)
+    dma("y", T.x0[:, 4 * A:4 * C], T.x[:, 4 * A:4 * C], "", "xl1", "ldx", 294912)
+    dma("y", T.x0[:, 0:4 * A], T.x[:, 0:4 * A], "", "xl0", "ldz", 458752)
+    dma("y", T.wq[:].bitcast(u8), T.wc[:], "xl0", "wq", "ldw", 262144)
+    dma("y", T.wsc[:], T.ws[:], "xl0", "wsc", "lds", 65536)
+    dma("y", T.vb[:], T.v[:], "xl0", "vb", "ldv", 131072)
     iota(T.pi[:, 0:1], [[0, 1]], 0, 1, "pi0", False)
     iota(T.pi[:, 8:16], [[16, 8]], 0, 0, "pi8", False)
     iota(T.m16[:], [[16, NB]], 0, 0, "m16")
@@ -179,11 +194,12 @@ def build(g, rank, T, topo):
         iota(T.rho[:, 0:C], [[513, 16], [16, NB]], OFF, 0, "rho0")
     if 1 in sides:
         iota(T.rho[:, C:2 * C], [[-513, 16], [-16, NB]], TOP - OFF, 0, "rho1")
-    iota(T.phi[:], [[1, 16], [16, NB]], 0, 0, "phi")
+    iota(T.phi[:], [[1, 16], [16, NB]], -A, 0, "phi")
+    iota(T.iotc[:], [[1, C]], -A, 0, "iotc")
     iota(T.t512[:], [[-512, 2 * C]], 0, 0, "t512")
-    ts(T.pj[:, 0:1], T.pi[:, 0:1], 15, None, AND, None, "pi0", "pj")
+    ts(T.pi[:, 16:17], T.pi[:, 0:1], 15, None, AND, None, "pi0", "pj")
     fill(T.acc[:], 0.0, "lt gt")
-    cp(QF, T.pj[:, 0:1], "pj", "qf")
+    cp(QF, T.pi[:, 16:17], "pj", "qf")
     cp(T.ur16[:], T.pi[:, 8:16], "pi8", "ur16")
     fill(T.kwin[:, 0:20], 1.0, "kw0")
     fill(T.kwin[:, 20:40], 0.0, "kw1")
@@ -192,72 +208,74 @@ def build(g, rank, T, topo):
     fill(T.nstep[:], -KS, "nstep", C / 2)
     ts(SHC, QF, 15.0, SH, LT, MUL, "qf", "shc")
     ts(SHH, QF, 15.0, 1024.0, LT, MUL, "qf", "shh")
-    ts(Q20, QF, 20.0, None, MUL, None, "qf", "q20")
-    ts(Q513, QF, 513.0, float(OFF), MUL, ADD, "qf", "q513")
-    ts(T.self2[:, 0:20], T.m16[:], QF, None, ADD, None, "m16 qf", "selfx")
-    ts(T.self2[:, 20:40], T.m16[:], QF, None, ADD, None, "m16 qf", "selfz")
-    cp(T.self2[:, 40:80], T.self2[:, 0:40], "selfx selfz", "selfy")
-    ts(T.c16[:], T.m16[:], 16.0, None, ADD, None, "m16", "c16")
-    ts(T.meq[:], T.q16[:], QF, None, EQ, None, "q16 qf", "meq", C)
-    ts(T.keep[:], T.q16[:], QF, None, AluOpType.not_equal, None, "q16 qf", "keep", C)
+    lin(Q20, QF, 20.0, 0.0, "qf", "q20")
+    lin(Q513, QF, 513.0, float(OFF), "qf", "q513")
+    lin(T.self2[:, 0:20], T.m16[:], 1.0, QF, "m16 qf", "selfx")
+    lin(T.self2[:, 20:40], T.m16[:], 1.0, QF, "m16 qf", "selfz")
+    lin(T.c16[:], T.m16[:], 1.0, 16.0, "m16", "c16")
+    act(T.dm[:], T.q16[:], AF.Abs, "q16 qf", "dm", C, bias=QF, scale=-1.0)
+    act(T.meq[:], T.dm[:], AF.Relu, "dm", "meq", C, bias=1.0, scale=-1.0)
+    act(T.keep[:], T.dm[:], AF.Sign, "dm", "keep", C)
     quant(T.uq[:], T.us[:], T.ub[:], 128, "ub", "uq")
     quant(T.vq[:], T.vs[:], T.vb[:], 128, "vb", "vq")
     ts(T.cl16[:, 60:80], T.m16[:], 0.0625, Q20, MUL, ADD, "m16 q20", "clf")
     cp(T.urq[:].bitcast(u32), T.uq[:].bitcast(u32).indirect(T.ur16[:]), "uq ur16", "urq", pick(128))
     cp(T.urs[:], T.us[:].indirect(T.ur16[:]), "uq ur16", "urs", pick(128))
-    ts(T.c0a[:], T.q16[:], QF, HUGE, EQ, MUL, "q16 qf", "c0a", C)
-    ts(T.c0b[:], T.q16[:], -1.0, QF, ADD, EQ, "q16 qf", "c0b", C)
-    ts(T.c0b[:], T.c0b[:], -SH, None, MUL, None, "c0b", "c0b", C)
-    tt(T.c0[:], T.c0a[:], T.c0b[:], ADD, "c0a c0b", "c0", 2 * C)
-    ts(T.c0h[:], T.c0[:], 1024.0 / SH, None, MUL, None, "c0", "c0h", C / 2)
+    fill(T.c0b[:, 0:1], 0.0, "c0z")
+    lin(T.c0b[:, 1:C + 1], T.meq[:], SH, 0.0, "meq", "c0b", C)
+    lin(T.eq[:], T.meq[:], HUGE, 0.0, "meq", "eq", C)
+    tt(T.c0[:], T.eq[:], T.c0b[:, 0:C], SUB, "eq c0b c0z", "c0", TB)
+    lin(T.c0h[:], T.c0[:], 1024.0 / SH, 0.0, "c0", "c0h", C)
     W = [T.cw[:, 16 * k:16 * k + 14] for k in range(32)]
     E = [T.cw[:, 16 * k + 14:16 * k + 16] for k in range(32)]
-    ts(W[0], T.self2[:, 0:14], -10.0, 1.0 / 21.0, ADD, MUL, "selfx", "W0")
-    ts(T.selfa[:], T.self2[:, 0:20], -1.0, 511.0, MUL, ADD, "selfx", "selfa")
-    cp(T.ci[:, 0:14], W[0], "W0", "ci")
-    ts(T.cwin[:, 0:20], T.m16[:], Q513, None, ADD, None, "m16 q513", "cw0")
-    ts(W[1], T.ci[:, 0:14], -21.0, None, MUL, None, "ci", "W1")
-    ts(W[2], T.ci[:, 0:14], -2.0, 19.0, MUL, ADD, "ci", "W2")
-    ts(W[3], T.ci[:, 0:14], 1.0, None, ADD, None, "ci", "W3")
+    ts(T.ci[:, 0:14], T.self2[:, 0:14], -10.0, 1.0 / 21.0, ADD, MUL, "selfx", "ci")
+    lin(T.selfa[:], T.self2[:, 0:20], -1.0, 511.0, "selfx", "selfa")
+    cp(W[0], T.ci[:, 0:14], "ci", "W0")
+    lin(T.cwin[:, 0:20], T.m16[:], 1.0, Q513, "m16 q513", "cw0")
+    lin(W[1], W[0], -21.0, 0.0, "W0", "W1")
+    lin(W[2], W[0], -2.0, 19.0, "W0", "W2")
+    lin(W[3], W[0], 1.0, 1.0, "W0", "W3")
     tt(W[4], W[1], T.self2[:, 0:14], ADD, "W1 selfx", "W4")
-    ts(T.cwin[:, 20:40], T.self2[:, 0:20], float(OFF - 512), None, ADD, None, "selfx", "cw1")
+    lin(T.cwin[:, 20:40], T.self2[:, 0:20], 1.0, float(OFF - 512), "selfx", "cw1")
     tt(W[5], W[4], W[3], GE, "W4 W3", "W5")
-    ts(T.cwin[:, 60:80], T.selfa[:], 51200.0, None, ADD, None, "selfa", "cw3")
+    lin(T.cwin[:, 60:80], T.selfa[:], 1.0, 51200.0, "selfa", "cw3")
     tt(W[6], W[5], W[2], MUL, "W5 W2", "W6")
     tt(W[7], W[5], W[3], MUL, "W5 W3", "W7")
-    ts(T.cwin[:, 40:60], T.cwin[:, 0:20], -1.0, float(TOP), MUL, ADD, "cw0", "cw2")
-    tt(W[8], W[6], T.ci[:, 0:14], ADD, "W6 ci", "W8")
+    lin(T.cwin[:, 40:60], T.cwin[:, 0:20], -1.0, float(TOP), "cw0", "cw2")
+    tt(W[8], W[6], W[0], ADD, "W6 W0", "W8")
     tt(W[9], W[4], W[7], SUB, "W4 W7", "W9")
-    ts(W[10], W[9], 0.5, None, LT, None, "W9", "W10")
-    ts(T.addc[:, 0:20], T.m16[:], 0.0, SHC, MUL, ADD, "m16 shc", "ac0")
+    act(W[10], W[9], AF.Relu, "W9", "W10", 14, bias=1.0, scale=-1.0)
+    lin(T.addc[:, 0:20], T.m16[:], 0.0, SHC, "m16 shc", "ac0")
     for d in sorted(set(sides)):
         c, b = 30 * d, 11 + 8 * d
         sg, z = (1.0, 0.0) if d == 0 else (-1.0, 19.0)
         n = ["V%d" % (b + k) for k in range(8)]
         e = ["E%d" % (b + k) for k in range(8)]
-        rho, tau = T.rho[:, C * d:C * d + C], T.qc[:, 4 + d:5 + d]
-        cp(T.pbw[:, 40 * d + 20:40 * d + 40], T.cwin[:, 40 * d + 20:40 * d + 40], "cw1 cw3", "pbw2%d" % d)
-        ts(T.addw[:, 60 * d:60 * d + 20], T.m16[:], 0.0, SHC, MUL, ADD, "m16 shc", "adw0%d" % d)
+        rho, tau, far = T.rho[:, C * d:C * d + C], T.qc[:, 4 + d:5 + d], 2.0 ** 22
+        lin(T.pbw[:, 40 * d + 20:40 * d + 40], T.cwin[:, 40 * d + 20:40 * d + 40], 1.0, 0.0, "cw1 cw3", "pbw2%d" % d)
+        lin(T.addw[:, 60 * d:60 * d + 20], T.m16[:], 0.0, SHC, "m16 shc", "adw0%d" % d)
         if d == 0:
-            ts(T.addw[:, 40:60], T.m16[:], 0.0, SHH, MUL, ADD, "m16 shh", "adw20")
+            lin(T.addw[:, 40:60], T.m16[:], 0.0, SHH, "m16 shh", "adw20")
+            lin(T.own[:, 0:40], T.self2[:, 0:40], 1.0, SH, "selfx selfz", "own0")
         else:
-            ts(T.addc[:, 60:80], T.m16[:], 0.0625, SHH, MUL, ADD, "m16 shh", "acm")
-        ts(tau, QF, 512.0 * sg, float(OFF if d == 0 else TOP - OFF - 511), MUL, ADD, "qf", "tau%d" % d)
-        ts(T.c0a[:], rho, tau, None, LT, None, "rho%d tau%d" % (d, d), "c0a", C)
-        tt(T.rhm[:, C * d:C * d + C], rho, T.c0a[:], MUL, "rho%d c0a" % d, "rhm%d" % d, 2 * C)
-        ts(W[b], W[8], sg, z, MUL, ADD, "W8", n[0])
-        ts(W[b + 1], W[9], sg, z - sg, MUL, ADD, "W9", n[1])
+            lin(T.addc[:, 60:80], T.m16[:], 0.0625, SHH, "m16 shh", "acm")
+            lin(T.own[:, 40:80], T.self2[:, 0:40], -1.0, SH + 511.0, "selfx selfz", "own1")
+        lin(tau, QF, 512.0 * sg * far, far * (OFF if d == 0 else TOP - OFF - 511), "qf", "tau%d" % d)
+        lin(T.c0a[:], rho, -far, tau, "rho%d tau%d" % (d, d), "c0a", C)
+        tt(T.rhm[:, C * d:C * d + C], rho, T.c0a[:], MIN, "rho%d c0a" % d, "rhm%d" % d, 2 * C)
+        lin(W[b], W[8], sg, z, "W8", n[0])
+        lin(W[b + 1], W[9], sg, z - sg, "W9", n[1])
         cp(T.cl16[:, c + 14:c + 28], W[b], n[0], "clq%d" % d)
         tt(W[b + 2], W[b], W[b + 1], SUB, n[0] + " " + n[1], n[2])
-        ts(W[b + 3], W[b + 2], 20.0, None, ADD, None, n[2], n[3])
+        lin(W[b + 3], W[b + 2], 1.0, 20.0, n[2], n[3])
         tt(W[b + 4], W[b + 3], W[10], MUL, n[3] + " W10", n[4])
         tt(W[b + 5], W[b + 4], W[b + 1], ADD, n[4] + " " + n[1], n[5])
         cp(T.cl16[:, c:c + 14], W[b + 5], n[5], "clp%d" % d)
         ts(E[b], T.self2[:, 0:2], 19.0, sg, MIN, MUL, "selfx", e[0])
-        ts(E[b + 1], E[b], z, None, ADD, None, e[0], e[1])
+        lin(E[b + 1], E[b], 1.0, z, e[0], e[1])
         ts(E[b + 2], E[b + 1], 9.5, None, GT, None, e[1], e[2])
-        ts(E[b + 3], E[b + 1], -43.0, 419.0, MUL, ADD, e[1], e[3])
-        ts(E[b + 4], E[b + 1], 22.0, None, MUL, None, e[1], e[4])
+        lin(E[b + 3], E[b + 1], -43.0, 419.0, e[1], e[3])
+        lin(E[b + 4], E[b + 1], 22.0, 0.0, e[1], e[4])
         tt(E[b + 5], E[b + 2], E[b + 3], MUL, e[2] + " " + e[3], e[5])
         tt(E[b + 6], E[b + 5], E[b + 4], ADD, e[5] + " " + e[4], e[6])
         cp(T.cl16[:, c + 28:c + 30], E[b + 6], e[6], "cle%d" % d)
@@ -265,88 +283,108 @@ def build(g, rank, T, topo):
     c = 30 * sides[0]
     gat(T.kp[:], T.kwin[:], T.cl16[:, c:c + 14], "kw0 kw1 clp%d" % sides[0], "kp", PW)
 
-    xall = "x_0 x_1 x_2 x_3"
+    for low in sorted(set(int(PAR["run"][d] == d) for d in sides)):
+        for k in range(4):
+            at, big = 3 * C * (4 * low + k), 1e29 if low else -1e29
+            zero = T.d0[:, at + 1:at + 3 * C:3]
+            iota(zero, [[0, C]], 0, 0, "cz%d%d" % (low, k))
+            for o, w in ((T.d0[:, at:at + 3 * C:3], "ct%d%d"), (T.d1[:, at + 2:at + 3 * C:3], "cs%d%d")):
+                add({"g": (lambda o=o, zero=zero, big=big: g.affine_select(o, zero, [[0, C]], GT, big, 0, 0), 170 + 2 * C * cyc)},
+                    "cz%d%d ct%d%d" % (low, k, low, k), w % (low, k))
+    frow, oph, bph, gh = [T.hf[:, C * k:C * k + C] for k in range(4)]
+    xi = T.zi[:, 64:84]
+    xall = [" ".join("x_%d%d" % (k, h) for k in range(4)) for h in range(2)]
     for t in range(3):
         peer = rank ^ STEP[t]
         d = side[0] = sides[t]
         eng = topo.engines(core, T.cores[peer])
         half = len(eng) // 2
         X = T.x0 if t == 0 else T.x1
-        xk = "x0" if t == 0 else xall
+        xh = ["xl0", "xl1"] if t == 0 else xall
+        xk = " ".join(xh)
         a16, b16 = T.a16[:, 24 * t:24 * t + NB], T.b16[:, 24 * t:24 * t + NB]
-        o16, ob16 = T.o16[:, 24 * t:24 * t + NB], T.ob16[:, 24 * t:24 * t + NB]
-        n16, nl16 = T.n16[:, 40 * t:40 * t + 40], T.nl16[:, 40 * t:40 * t + 40]
-        ka, kb, ko, kob, kd, kdl, kn, knl = ["%s%d" % (k, t) for k in ("a", "b", "o", "ob", "ds", "dl", "n", "nl")]
+        o16, ob16, ko = T.o16[:, 24 * t:24 * t + NB], T.ob16[:, 24 * t:24 * t + NB], "o%d" % t
+        nl16 = T.nl16[:, 40 * t:40 * t + 40]
+        ka, kb, kd, kdl, kn, knl = ["%s%d" % (k, t) for k in ("a", "b", "ds", "dl", "n", "nl")]
         fq, fs, lq, ls = T["fq%d" % t], T["fs%d" % t], T["lq%d" % t], T["ls%d" % t]
-        quant(T.xq[:], T.xs[:], X[:], C, xk, "xq")
-        mm(T.pa[:, 0:C], T.urq[:], T.urs[:], T.xq[:], T.xs[:], C, "urq urs xq", "pa")
-        mm(T.pb[:, 0:C], T.urq[:], T.urs[:], T.xq[:], T.xs[:], C, "urq urs xq pa", "pb")
-        tt(T.dm[:], T.pa[:, 0:C], T.meq[:], MUL, "pa meq", "dm", C)
-        scan(T.hold[:], T.keep[:], T.dm[:], MUL, ADD, "keep dm", "hold", C)
+        for h in (1, 0):
+            quant(T.xq[:, A * h:A * h + A], T.xs[:, A * h:A * h + A], X[:, 4 * A * h:4 * A * h + 4 * A], A, xh[h], "xq%d" % h)
+        mm(T.pw[:, 0:A], T.urq[:], T.urs[:], T.xq[:, A:C], T.xs[:, A:C], A, "urq urs xq1", "pw0")
+        mm(T.pb[:, 0:C], T.urq[:], T.urs[:], T.xq[:], T.xs[:], C, "urq urs xq0 xq1", "pb")
+        mm(T.pa[:, 0:C], T.urq[:], T.urs[:], T.xq[:], T.xs[:], C, "urq urs xq0 xq1", "pa")
+        for h, s, ks in ((1, T.pw[:, 0:A], "pw0"), (0, T.pa[:, 0:A], "pa")):
+            a, b = A * h, A * h + A
+            tt(T.dm[:, a:b], s, T.meq[:, a:b], MUL, ks + " meq keep", "dm%d" % h, A)
+            scan(T.hold[:, a:b], T.keep[:, a:b], T.dm[:, a:b], MUL, ADD, "keep dm%d" % h, "hold%d" % h, A)
+            tt(T.eq[:, a:b], s, T.hold[:, a:b], EQ, ks + " hold%d c0" % h, "eq%d" % h, A)
+            scan(T.eqs[:, a:b], T.keep[:, a:b], T.eq[:, a:b], MUL, ADD, "keep eq%d" % h, "eqs%d" % h, A / 2)
         for k in range(NS):
             n = 16 * (NV + k) + 16
-            act(T.sg[:, C * k:C * k + C], T.pb[:, 0:C], AF.Sign, "pb hold", "sg%d" % k, C, bias=T.hold[:, n - 1:n], scale=-1.0)
+            act(T.sg[:, C * k:C * k + C], T.pb[:, 0:C], AF.Sign, "pb hold1", "sg%d" % k, C, bias=T.hold[:, n - 1:n], scale=-1.0)
             act(T.junk[:, C * k:C * k + n], T.sg[:, C * k:C * k + n], AF.Relu, "sg%d lt" % k, "lt%d jk%d" % (k, k), n, accum_out=T.acc[:, k:k + 1])
             if n < C:
                 act(T.junk[:, C * k + n:C * k + C], T.sg[:, C * k + n:C * k + C], AF.Relu, "sg%d gt" % k, "gt%d jr%d" % (k, k), C - n,
                     scale=-1.0, accum_out=T.acc[:, 16 + k:17 + k])
-        tt(T.eq[:], T.pa[:, 0:C], T.hold[:], EQ, "pa hold", "eq", C)
-        scan(T.eqs[:], T.keep[:], T.eq[:], MUL, ADD, "keep eq", "eqs", C / 2)
-        for m in range(NV):
+        for m in range(NV - 1, -1, -1):
             n = 16 * m + 16
-            sc, z = T.hold[:, n - 1:n], T.cmp[:, C * m:C * m + C]
-            ts(T.cmp[:, C * m:C * m + n], T.pa[:, 0:n], sc, None, GE, None, "pa hold", "cl%d_" % m, n)
-            ts(T.cmp[:, C * m + n:C * m + C], T.pa[:, n:C], sc, None, GT, None, "pa hold", "cr%d_" % m, C - n)
-            scan(T.cs[:, C * m:C * m + C], z, z, ADD, MAX, "cl%d_ cr%d_" % (m, m), "cs%d" % m, C / 2)
-        tt(T.sm1[:, 0:NS], T.c16[:, NV:NB], T.eqs[:, 16 * NV + 15:C:16], SUB, "c16 eqs", "sm1a")
+            sc, r = T.hold[:, n - 1:n], "pa hold%d" % (m // 10)
+            ts(T.cmp[:, C * m:C * m + n], T.pa[:, 0:n], sc, None, GE, None, r, "cl%d_" % m, n)
+            ts(T.cmp[:, C * m + n:C * m + C], T.pa[:, n:C], sc, None, GT, None, r, "cr%d_" % m, C - n)
+            scan(T.cs[:, C * m + A:C * m + C], T.cmp[:, C * m:C * m + A], T.cmp[:, C * m + A:C * m + C], ADD, ADD,
+                 "cl%d_ cr%d_" % (m, m), "cs%d" % m, C / 4)
+        tt(T.sm1[:, 0:NS], T.c16[:, NV:NB], T.eqs[:, 16 * NV + 15:C:16], SUB, "c16 eqs1", "sm1a")
         tt(T.sm1[:, 16:16 + NS], T.acc[:, 16:16 + NS], T.acc[:, 0:NS], SUB, " ".join("lt%d gt%d" % (k, k) for k in range(NS)), "sm1b")
         tt(T.aw[:, NV:NB], T.sm1[:, 0:NS], T.sm1[:, 16:16 + NS], ADD, "sm1a sm1b", "aw1")
-        tt(T.aw[:, 0:NV], T.cs[:, C - 1:NV * C:C], T.eqs[:, 15:16 * NV:16], SUB, "eqs " + " ".join("cs%d" % m for m in range(NV)), "aw0")
+        tt(T.aw[:, 0:NV], T.cs[:, C - 1:NV * C:C], T.eqs[:, 15:16 * NV:16], SUB, "eqs0 eqs1 " + " ".join("cs%d" % m for m in range(NV)), "aw0")
         cp(a16, T.aw[:], "aw0 aw1", ka)
         send(b16, a16, "ra%d" % t, peer, eng[:half] if t == 0 else eng, ka, kb, 5120)
 
-        al, kal, be, kbe = (a16, ka, b16, kb) if d == 0 else (b16, kb, a16, ka)
-        osl, kosl, opl, kopl = (o16, ko, ob16, kob) if d == 0 else (ob16, kob, o16, ko)
+        al, kal = (a16, ka) if d == 0 else (b16, kb)
         pl, ql, el = T.cl16[:, 30 * d:30 * d + 14], T.cl16[:, 30 * d + 14:30 * d + 28], T.cl16[:, 30 * d + 28:30 * d + 30]
         kbw = "kbw0 kbw2"
-        cp(T.orow[:].indirect(a16), T.iot[:], ka + " iot", "orow", 50 + C * PAR["sca"])
-        if d == 0:
-            gat(T.oph[:], T.orow[:], T.cl16[:, 60:80], "orow clf", "oph")
-            ts(o16, diag2(0, T.oph[:], "oph", "dg0"), SHH, None, ADD, None, "dg0 shh", ko)
-        else:
-            diag(T.dg[:, 0:C], T.orow[:], C, "orow", "dh0")
-            ts(o16, T.dg[:, 15:C:16], SHC, None, ADD, None, "dh0 shc", ko)
-        send(ob16, o16, "ro%d" % t, peer, eng[half:] if t == 0 else eng, ko, kob, 5120)
+        scatter = 50 + C * PAR["sca"]
+        cp(T.orow[:].indirect(a16), T.iotc[:], ka + " iotc", "orow", scatter)
         gat(T.rrow[:], T.rhm[:, C * d:C * d + C], al, kal + " rhm%d" % d, "rrow")
-        gat(T.frow[:], T.phi[:], al, kal + " phi", "frow")
-        gat(T.brow[:], T.iot[:], be, kbe + " iot", "brow")
-        gat(T.bph[:], T.brow[:], osl, "brow " + kosl, "bph")
-        gat(T.ma[:], T.rrow[:], opl, "rrow " + kopl, "ma")
+        gat(frow, T.phi[:], al, kal + " phi", "frow")
+        if d == 0:
+            gat(oph, T.orow[:], T.cl16[:, 60:80], "orow clf", "oph")
+            ts(o16, diag2(0, oph, "oph", "dg0"), SHH, float(A), ADD, ADD, "dg0 shh", ko)
+            send(ob16, o16, "ro%d" % t, peer, eng, ko, "ob%d" % t, 5120, None)
+            cp(T.ma[:].indirect(b16), T.rrow[:], kb + " rrow", "ma", scatter)
+            gat(T.brow[:], T.iot[:], b16, kb + " iot", "brow")
+            osl, kosl = o16, ko
+        else:
+            ts(o16, diag2(0, T.orow[:], "orow", "dg0"), SHH, float(A), ADD, ADD, "dg0 shh", ko)
+            gat(T.ma[:], T.rrow[:], o16, "rrow " + ko, "ma")
+            osl, kosl = ob16, "ob%d" % t
+            expect("ro%d" % t, kosl, len(eng))
+            gat(T.brow[:], T.iot[:], a16, ka + " iot", "brow")
+        gat(bph, T.brow[:], osl, "brow " + kosl, "bph")
+        ends = diag2(1, bph, "bph", "dg1")
+        ts(T.bw16[:], ends, SHH, None, ADD, None, "dg1 shh", "bw16")
+        ts(T.kbw[:, 0:20], ends, SHH, 1.0 - 2 * d, ADD, MUL, "dg1 shh", "kbw0")
         for k in range(4):
             ts(T.oy16[:, NB * k:NB * k + NB], osl, 4.0, float(k), MUL, ADD, kosl, "oy%d" % k)
-            gat(T.y0[:, C * k:C * k + C], X[:], T.oy16[:, NB * k:NB * k + NB], xk + " oy%d" % k, "y0_%d" % k)
+            gat(T.y0[:, C * k:C * k + C], X[:], T.oy16[:, NB * k:NB * k + NB], xk + " oy%d" % k, "y0_%d" % k, C, 64.0)
         ts(T.kw[:, 0:20], b16, 0.0, None, ADD, None, kb, "kwa")
         tt(T.kw[:, 20:40], T.kw[:, 0:20], T.aw[:], ADD, "kwa aw0 aw1", "kwb")
         cp(T.sum16[:], T.kw[:, 20:40], "kwb", "sum16")
         ts(T.kw[:, 40:60], T.kw[:, 20:40], -512.0, None, MUL, None, "kwb", "kwc")
         tt(T.krow[:], T.t512[:].indirect(T.sum16[:]), T.iot[:], ADD, "sum16 t512 iot", "krow", 50 + 2 * C)
         tt(T.kw[:, 60:80], T.kw[:, 40:60], T.self2[:, 0:20], ADD, "kwc selfx", "kwd")
-        dsn, dld = T.dsn[:, 12 * t:12 * t + 10], T.dld[:, 12 * t:12 * t + 10]
+        dsn = T.dsn[:, 12 * t:12 * t + 10]
         dk = " ".join("%s_%d" % (kd, k) for k in range(10))
         for k in range(10):
             m = 10 * d + k
             act(T.junk[:, C * (9 + k):C * (10 + k)], T.krow[:], AF.Sign, "krow kwd", "%s_%d js%d" % (kd, k, k), C,
                 bias=T.kw[:, 60 + m:61 + m], scale=-1.0, accum_out=T.dsn[:, 12 * t + k:12 * t + k + 1])
-        send(dld, dsn, "rs%d" % t, peer, eng, dk, kdl, 5120)
-        ts(T.sw[:, 10 * d:10 * d + 10], dsn, 319.0, 0.5, ADD, MUL, dk, "sw0")
-        ts(T.sw[:, 10 - 10 * d:20 - 10 * d], dld, 319.0, 0.5, ADD, MUL, kdl, "sw1")
-        cp(T.s16[:], T.sw[:, 0:20], "sw0 sw1", "s16")
-        cp(T.erow[:].indirect(T.s16[:]), T.frow[:], "s16 frow", "erow", 50 + C * PAR["sca"])
-        diag(T.dg[:, C:C + A], T.erow[:, 0:A], A, "erow", "dg3")
-        ts(T.e16[:], T.dg[:, C + 15:C + A:16], SHC, None, ADD, None, "dg3 shc", "e16")
-        ends = diag2(1, T.bph[:], "bph", "dg1")
-        ts(T.kbw[:, 0:20], ends, SHH, 1.0 - 2 * d, ADD, MUL, "dg1 shh", "kbw0")
-        ts(T.bw16[:], ends, SHH, None, ADD, None, "dg1 shh", "bw16")
+        s16, sl16, ks = T.s16[:, 24 * t:24 * t + NB], T.sl16[:, 16 * t:16 * t + 10], "sa%d sb%d" % (t, t)
+        mine, other = [T.s16[:, 24 * t + 10 * k:24 * t + 10 * k + 10] for k in (d, 1 - d)]
+        ts(mine, dsn, 319.0, 0.5, ADD, MUL, dk, "sa%d" % t)
+        send(sl16, mine, "rs%d" % t, peer, eng[half:] if t == 0 else eng, "sa%d" % t, kdl, 2560)
+        cp(other, sl16, kdl, "sb%d" % t)
+        cp(T.erow[:].indirect(s16), frow, ks + " frow", "erow", scatter)
+        ts(T.e16[:], diag2(2, T.erow[:], "erow", "dg3"), SHH, float(A), ADD, ADD, "dg3 shh", "e16")
         gat(T.qv[:], T.kbw[:], ql, kbw + " clq%d" % d, "qv", PW)
         ts(T.w8[:], T.kbw[:, 0:20], KS, None, MUL, None, kbw, "w8")
         if d == 1:
@@ -364,103 +402,132 @@ def build(g, rank, T, topo):
             if d == 0:
                 return b[:, C * k:C * k + C]
             return b[:, C * k + C - 1:C * k - 1:-1] if k else b[:, C - 1::-1]
-        ts(T.mm[:], T.ma[:], 0.5, None, GT, None, "ma", "mm", C)
-        scan(along(T.rows, 2), along(T.mm), along(T.mm), ADD, MAX, "mm", "row2", C)
+        act(T.mm[:, 0:C], T.ma[:], AF.Sign, "ma", "mm", C, bias=0.5, scale=-1.0)
+        scan(along(T.mm, 1), along(T.mm), T.nstep[:], MUL, MAX, "mm nstep", "row2", C / 2, 1.0)
         scan(along(T.rows, 0), along(T.ma), along(T.ma), MAX, MAX, "ma", "row0", C)
         scan(along(T.rows, 1), T.nstep[:], along(T.ma), ADD, MAX, "ma nstep", "row1", C)
-        gat(T.gh[:], T.rows[:, 2 * C:3 * C], T.bw16[:], "row2 bw16", "gr2")
+        gat(gh, T.mm[:, C:2 * C], T.bw16[:], "row2 bw16", "gr2", C, -0.5, 0.5)
         for k in range(2):
             gat(T.gr[:, C * k:C * k + C], T.rows[:, C * k:C * k + C], T.bw16[:], "row%d bw16" % k, "gr%d" % k)
             diag(T.gd[:, C * k:C * k + C], T.gr[:, C * k:C * k + C], C, "gr%d" % k, "gd%d" % k)
         ad = 60 * d
-        tt(T.seed[:, 40:60], diag2(3, T.gh[:], "gr2", "gd2"), T.addw[:, ad + 40:ad + 60], ADD, "gd2 adw2%d" % d, "seed1")
-        tt(T.zi[:, 64:96], T.prc[:].indirect(el), T.seed[:, 40:72], ADD, "pr2 cle%d seed1" % d, "zi2", 112)
+        tt(T.seed[:, 40:60], diag2(3, gh, "gr2", "gd2"), T.addw[:, ad + 40:ad + 60], ADD, "gd2 adw2%d" % d, "seed1")
+        tt(T.zi[:, 0:32], T.prc[:].indirect(el), T.seed[:, 40:72], ADD, "pr2 cle%d seed1" % d, "zi2", 112)
         tt(T.seed[:, 0:40], T.gd[:, 15:2 * C:16], T.addw[:, ad:ad + 40], ADD, "gd0 gd1 adw1 adw0%d" % d, "seed0", 80)
-        ts(T.xi[:, 64:84], T.zi[:, 64:84], 1, None, AND, None, "zi2", "xi2")
+        ts(xi, T.zi[:, 0:20], 1, None, AND, None, "zi2", "xi2")
         for k in range(2):
-            tt(T.zi[:, 32 * k:32 * k + 32], T.pr[:, PW * k:PW * k + PW].indirect(el), T.seed[:, 20 * k:20 * k + 32], MAX,
-               "pr%d cle%d seed0 seed1" % (k, d), "zi%d" % k, 112)
-            ts(T.ev[:, 20 * k:20 * k + 20], T.xi[:, 64:84], 1.0 - 2 * d, float(d), MUL, ADD, "xi2", "ev%d" % k)
-        ts(T.xi[:, 0:64], T.zi[:, 0:64], 511, None, AND, None, "zi0 zi1", "xi0")
-        for k in range(2):
-            o, x = T.sml[:, 20 * k:20 * k + 20], T.xi[:, 32 * k:32 * k + 20]
-            if d == 0:
-                tt(o, x, T.self2[:, 0:20], SUB, "xi0 selfx", "D0_%d" % k)
-            else:
-                tt(o, T.selfa[:], x, SUB, "xi0 selfa", "D0_%d" % k)
-        ts(n16, T.sml[:, 0:40], 512.0, None, ADD, None, "D0_0 D0_1", kn)
-        send(nl16, n16, "rn%d" % t, peer, eng, kn, knl, 10240)
-        ts(T.sml[:, 200:240], nl16, -512.0, None, ADD, None, knl, "D1_0 D1_1")
-        for j in range(2):
-            b, r = 200 * j, "D%d_0 D%d_1" % (j, j)
-            tt(T.sml[:, b + 40:b + 80], T.sml[:, b:b + 40], T.ev[:], MUL, "ev0 ev1 " + r, "ED%d" % j, 80)
-            tt(T.sml[:, b + 80:b + 120], T.sml[:, b:b + 40], T.sml[:, b + 40:b + 80], SUB, "ED%d " % j + r, "OD%d" % j, 80)
-            tt(T.sml[:, b + 120:b + 200], T.sml[:, b + 40:b + 120], T.self2[:], ADD, "ED%d OD%d selfx selfy" % (j, j), "L1%d" % j, 160)
-            cp(T.l16[:, 80 * j:80 * j + 80], T.sml[:, b + 120:b + 200], "L1%d" % j, "l16_%d" % j, 80)
-
+            tt(T.zf[:, 20 * k:20 * k + 32], T.pr[:, PW * k:PW * k + PW].indirect(el), T.seed[:, 20 * k:20 * k + 32], MAX,
+               "pr%d cle%d seed0 seed1" % (k, d), "zf", 112)
+            tt(T.ev[:, 20 * k:20 * k + 20], xi, T.own[:, 40 * d:40 * d + 20], MUL, "xi2 own%d" % d, "ev%d" % k)
+        tt(T.ev[:, 40:80], T.own[:, 40 * d:40 * d + 40], T.ev[:, 0:40], SUB, "ev0 ev1 own%d" % d, "ev2", 80)
         for w in range(2):
-            src, dst = (T.y0, T.y1) if w == 0 else (T.y1, T.y2)
-            for k in range(4):
-                win, s = src[:, C * k:C * k + C], 4 * w + k
-                for j in range(2):
-                    c, b = 80 * j + 40 * w, C * (4 * s + 2 * j)
-                    r = "y%d_%d l16_%d" % (w, k, j)
-                    o, fold = T.lu[:, C * (2 * s + j):C * (2 * s + j + 1)], MAX if j == d else MIN
-                    gat(T.gg[:, b:b + C], win, T.l16[:, c:c + NB], r, "ga%d%d" % (s, j))
-                    if (d, w, k, j) in PAR["both"]:
-                        gat(T.gg[:, b + C:b + 2 * C], win, T.l16[:, c + NB:c + 2 * NB], r, "gb%d%d" % (s, j))
-                        tt(o, T.gg[:, b + C:b + 2 * C], T.gg[:, b:b + C], fold, "ga%d%d gb%d%d" % (s, j, s, j), "lu%d%d" % (s, j), TB)
-                    else:
-                        tt(o, win.indirect(T.l16[:, c + NB:c + 2 * NB]), T.gg[:, b:b + C], fold, r + " ga%d%d" % (s, j), "lu%d%d" % (s, j),
-                           max(pick(C), 50 + TB))
-                tt(T.vv[:, C * s:C * s + C], T.lu[:, 2 * C * s:2 * C * s + C], T.lu[:, 2 * C * s + C:2 * C * s + 2 * C], ADD,
-                   "lu%d0 lu%d1" % (s, s), "vv%d" % s, TB)
-                tt(dst[:, C * k:C * k + C], T.vv[:, C * s:C * s + C], win, SUB, "vv%d y%d_%d" % (s, w, k), "y%d_%d" % (w + 1, k), TB)
-        for k in range(4):
-            gat(T.ft[:, k:4 * A:4], T.y2[:, C * k:C * k + C], T.e16[:], "y2_%d e16" % k, "ft%d" % k, A)
-        fts = "ft0 ft1 ft2 ft3"
-        quant(fq[:], fs[:], T.ft[:], A, fts, "fq%d" % t)
-        send(lq[:].bitcast(u8), fq[:].bitcast(u8), "rf%d" % t, peer, eng, "fq%d" % t, "lc%d" % t, 81920, len(eng))
-        send(ls[:], fs[:], "rf%d" % t, peer, eng, "fq%d" % t, "lq%d" % t, 20480, len(eng))
+            c = 40 * ((w + d + 1) % 2)
+            tt(T.li[:, 40 * w:40 * w + 40], T.zf[:, 0:40], T.ev[:, c:c + 40], MAX, "zf ev0 ev1 ev2" if c else "zf ev0 ev1", "li%d" % w, 80)
+        ts(T.lj[:, 0:80], T.li[:], 511, None, AND, None, "li0 li1", "lj", 80)
+        ts(T.n16[:, 80 * t:80 * t + 80], T.lj[:, 0:80], 1.0 - 2 * d, 511.0 * d, MUL, ADD, "lj", kn, 80)
+        send(nl16, T.n16[:, 80 * t:80 * t + 40], "rn%d" % t, peer, eng, kn, knl, 10240)
+        p16, pl16, kp, kpl = T.p16[:, 40 * t:40 * t + 40], T.pl16[:, 40 * t:40 * t + 40], "p%d" % t, "pl%d" % t
+        gat(T.pk[:, 0:C], T.iot[:], T.n16[:, 80 * t + 40:80 * t + 60], "iot " + kn, "pk0", C, 512.0)
+        tt(T.pk[:, C:2 * C], T.iot[:].indirect(T.n16[:, 80 * t + 60:80 * t + 80]), T.pk[:, 0:C], ADD, "iot pk0 " + kn, "pk1",
+           max(pick(C), 50 + 2 * TB))
+        gat(T.pk[:, 2 * C:3 * C], T.pk[:, C:2 * C], T.e16[:], "pk1 e16", "pk2")
+        diag(T.dg[:, 3 * C:4 * C], T.pk[:, 2 * C:3 * C], C, "pk2", "dg4")
+        ts(T.zi[:, 32:52], T.dg[:, 3 * C + 15:4 * C:16], SHC, None, ADD, None, "dg4 shc", "zi3")
+        ts(T.lj[:, 80:100], T.zi[:, 32:52], 9, None, AluOpType.arith_shift_right, None, "zi3", "lk0")
+        ts(T.lj[:, 100:120], T.zi[:, 32:52], 511, None, AND, None, "zi3", "lk1")
+        cp(p16, T.lj[:, 80:120], "lk0 lk1", kp)
+        send(pl16, p16, "rp%d" % t, peer, eng, kp, kpl, 10240)
 
-        ts(T.f64[:], T.ft[:], 64.0, None, MUL, None, fts, "f64", 2 * A)
+        def toggle(win, kw, lists, c, n, s, own, kown, dst, kd):
+            k, z, m = s[0] % 4, s[1], n // 16
+            js = PAR["run"][d]
+            low = js == d
+            at = 3 * (C * (4 * low + k) + 16 * c)
+            d0, d1, v = T.d0[:, at:at + 3 * n], T.d1[:, at:at + 3 * n], T.vv[:, at % (12 * C):at % (12 * C) + 3 * n]
+            kc, old = " cs%d%d" % (low, k), ["a%d" % k] if z[0] != "a" else ["b%d" % k, "c%d" % k]
+            war = "".join(" vv" + o for o in old)
+            if (d, z) in PAR["plain"]:
+                for j, (l, kl, a) in enumerate(lists):
+                    la, lb = [l[:, a + c + i:a + c + i + m] for i in (0, NB)]
+                    ga, o = [u[:, C * (8 * j + s[0]) + 16 * c:C * (8 * j + s[0]) + 16 * c + n] for u in (T.ga, T.gb)]
+                    gat(ga, win, la, kw + " " + kl, "ga%s%d" % (z, j), n)
+                    tt(o, win.indirect(lb), ga, MAX if j == d else MIN, "%s %s ga%s%d" % (kw, kl, z, j), "gb%s%d" % (z, j),
+                       max(pick(n), 50 + TB * n / C))
+                lo, hi, v = [u[:, C * i + 16 * c:C * i + 16 * c + n] for u, i in ((T.gb, s[0]), (T.gb, 8 + s[0]), (T.vw, s[0]))]
+                tt(v, lo, hi, ADD, "gb%s0 gb%s1" % (z, z), "vw" + z, TB * n / C)
+                tt(dst, v, own, SUB, "vw%s %s" % (z, kown), kd, TB * n / C)
+                return
+            l, kl, a = lists[js]
+            la, lb = [l[:, a + c + i:a + c + i + m] for i in (0, NB)]
+            gat(T.d1[:, at:at + 3 * n:3], win, la, kw + " " + kl + war, "ga%s%d" % (z, js), n)
+            gat(T.d1[:, at + 1:at + 3 * n:3], win, lb, kw + " " + kl + war, "gb%s%d" % (z, js), n, -1.0)
+            l, kl, a = lists[1 - js]
+            la, lb = [l[:, a + c + i:a + c + i + m] for i in (0, NB)]
+            r, y = kw + " " + kl, "%s%d" % (z, 1 - js)
+            ga, gb = [u[:, C * (8 * (1 - js) + s[0]) + 16 * c:C * (8 * (1 - js) + s[0]) + 16 * c + n] for u in (T.ga, T.gb)]
+            o, fold = T.d0[:, at + 2:at + 3 * n:3], MIN if low else MAX
+            gat(ga, win, la, r, "ga" + y, n)
+            if (d, z) in PAR["both"]:
+                gat(gb, win, lb, r, "gb" + y, n)
+                tt(o, gb, ga, fold, "ga%s gb%s" % (y, y) + war, "lu" + z, TB * n / C)
+            else:
+                tt(o, win.indirect(lb), ga, fold, r + " ga" + y + war, "lu" + z, max(pick(n), 50 + TB * n / C))
+            scan(v, d0, d1, SUB, MIN if low else MAX, "ga%s%d gb%s%d lu%s" % (z, js, z, js, z) + kc + "".join(" yy" + o for o in old),
+                 "vv" + z, 1.5 * n)
+            tt(dst, T.vv[:, at % (12 * C) + 2:at % (12 * C) + 3 * n:3], own, SUB, "vv%s %s" % (z, kown), kd + " yy" + z, TB * n / C)
+
         for k in range(4):
-            act(T.zz[:, 480 * k:480 * k + C], T.y2[:, C * k:C * k + C], AF.Copy, "y2_%d fq%d" % (k, t), "zy%d" % k, C, scale=64.0)
-        late = " fq%d" % t
-        ts(T.sw[:, 20:40], diag2(2, T.frow[:], "frow" + late, "dg2"), SHH, None, ADD, None, "dg2 shh", "swf")
-        ts(T.sw[:, 40:60], T.sw[:, 0:20], float(C), None, ADD, None, "sw0 sw1" + late, "swp")
-        ts(T.sw[:, 60:80], T.sw[:, 0:20], float(A), None, LT, None, "sw0 sw1" + late, "swl")
-        tt(T.sw[:, 80:100], T.sw[:, 40:60], T.sw[:, 20:40], SUB, "swp swf", "swd")
-        tt(T.sw[:, 100:120], T.sw[:, 80:100], T.sw[:, 60:80], MUL, "swd swl", "swe")
-        tt(T.sw[:, 120:140], T.sw[:, 100:120], T.sw[:, 20:40], ADD, "swe swf", "swg")
-        cp(T.loc16[:], T.sw[:, 120:140], "swg", "loc16")
+            win = T.y0[:, C * k:C * k + C]
+            toggle(win, "y0_%d" % k, [(T.n16, kn, 80 * t), (T.nl16, knl, 40 * t)], 0, C, (k, "a%d" % k), win, "y0_%d" % k, T.y1[:, C * k:C * k + C], "y1_%d" % k)
+        for h in range(2):
+            for k in range(4):
+                win, own, z = T.y1[:, C * k:C * k + C], T.ye[:, C * k + A * h:C * k + A * h + A], "bc"[h] + str(k)
+                gat(own, win, T.e16[:, 10 * h:10 * h + 10], "y1_%d e16" % k, "ye" + z, A)
+                dst = T.f64[:, A * k:A * k + A] if h == 0 else T.zz[:, C * k + A:C * k + C]
+                toggle(win, "y1_%d" % k, [(T.p16, kp, 40 * t), (T.pl16, kpl, 40 * t)], 10 * h, A, (4 + k, z), own, "ye" + z, dst, ("f64_%d", "zy%d")[h] % k)
+                if h == 0:
+                    ts(T.ft[:, k:4 * A:4], dst, 0.015625, None, MUL, None, "f64_%d" % k, "ft%d" % k, A / 2)
+            if h == 0:
+                quant(fq[:], fs[:], T.ft[:], A, "ft0 ft1 ft2 ft3", "fq%d" % t)
+                send(lq[:].bitcast(u8), fq[:].bitcast(u8), "rf%d" % t, peer, eng, "fq%d" % t, "lc%d" % t, 81920, len(eng))
+                send(ls[:], fs[:], "rf%d" % t, peer, eng, "fq%d" % t, "lq%d" % t, 20480, len(eng))
         for k in range(4):
             mm(T.pw[:, 512 * k:512 * k + A], T.wq[:, 128 * k:128 * k + 128], T.wsc[:, 128 * k:128 * k + 128], lq[:], ls[:], A,
                "wq wsc lc%d lq%d" % (t, t), "pw%d" % k)
-            tt(T.zz[:, 480 * k + C:480 * k + 480], T.pw[:, 512 * k:512 * k + A], T.f64[:, k:4 * A:4], ADD, "pw%d f64" % k, "zh%d" % k, A)
-            gat(T.x1[:, k:4 * C:4], T.zz[:, 480 * k:480 * k + 480], T.loc16[:], "zy%d zh%d loc16" % (k, k), "x_%d" % k, C, 0.015625)
+            tt(T.zz[:, C * k:C * k + A], T.pw[:, 512 * k:512 * k + A], T.f64[:, A * k:A * k + A], ADD, "pw%d f64_%d" % (k, k), "zh%d" % k, A)
+        for h in (1, 0):
+            for k in range(4):
+                gat(T.x1[:, 4 * A * h + k:4 * A * h + 4 * A:4], T.zz[:, C * k:C * k + C], T.s16[:, 24 * t + 10 * h:24 * t + 10 * h + 10],
+                    "zy%d zh%d %s" % (k, k, ks), "x_%d%d" % (k, h), A, 0.015625)
 
-    quant(T.xq[:], T.xs[:], T.x1[:], C, xall, "xq")
-    mm(T.pa[:, 0:A], T.vq[:], T.vs[:], T.xq[:, 0:A], T.xs[:, 0:A], A, "vq xq", "pa")
-    mm(T.pb[:, 0:A], T.vq[:], T.vs[:], T.xq[:, A:C], T.xs[:, A:C], A, "vq xq", "pb")
-    dma("y", T.oc[:], T.xq[:].bitcast(u8), "xq", "", "sto", 163840)
+    for h in (1, 0):
+        quant(T.xq[:, A * h:A * h + A], T.xs[:, A * h:A * h + A], T.x1[:, 4 * A * h:4 * A * h + 4 * A], A, xall[h], "xq%d" % h)
+    mm(T.pb[:, 0:A], T.vq[:], T.vs[:], T.xq[:, A:C], T.xs[:, A:C], A, "vq xq1", "pb")
+    mm(T.pa[:, 0:A], T.vq[:], T.vs[:], T.xq[:, 0:A], T.xs[:, 0:A], A, "vq xq0", "pa")
+    dma("y", T.oc[:], T.xq[:].bitcast(u8), "xq0 xq1", "", "sto", 163840)
     for k in range(4):
-        dma("ys"[k % 2], T.osc[4 * k:4 * k + 4, :], T.xs[32 * k:32 * k + 4, :], "xq", "", "sto", 1280)
-    cp(T.yo[:, 0:A], T.pa[:, 0:A], "pa", "yo0", A)
+        dma("ys"[k % 2], T.osc[4 * k:4 * k + 4, :], T.xs[32 * k:32 * k + 4, :], "xq0 xq1", "", "sto", 1280)
     act(T.yo[:, A:C], T.pb[:, 0:A], AF.Copy, "pb", "yo1", A)
-    dma("y", T.y[:, 0:A], T.yo[:, 0:A], "yo0", "", "sto", 81920)
+    cp(T.yo[:, 0:A], T.pa[:, 0:A], "pa", "yo0", A)
     dma("s", T.y[:, A:C], T.yo[:, A:C], "yo1", "", "sto", 81920)
+    dma("y", T.y[:, 0:A], T.yo[:, 0:A], "yo0", "", "sto", 81920)
     return ops, arrive
 
 
-def arrange(progs):
-    wake = PAR["wake"]
+def arrange(make):
+    others, held = [], dict(PAR)
+    for change in PAR["also"]:
+        PAR.update(change)
+        ops = [o for p, _ in make() for o in p]
+        others.append(([list(o["alts"].values())[0][1] for o in ops], [o["late"] + PAR["wake"] for o in ops]))
+        PAR.update(held)
+    progs, wake = make(), PAR["wake"]
     node, at = [], {}
     for r, (ops, _) in enumerate(progs):
         for i, o in enumerate(ops):
             at[(r, i)] = len(node)
             q = list(o["alts"])[0]
-            node.append((r, i, q, o["alts"][q][1], o["late"] + wake, (o["w"][0], o["w"][1][:2])))
+            node.append((r, i, q, o["alts"][q][1], o["late"] + wake, o["w"]))
     pre = [[at[(z[0], p)] for p in progs[z[0]][0][z[1]]["pre"]] for z in node]
     for n, z in enumerate(node):
         out = progs[z[0]][0][z[1]]["out"]
@@ -473,40 +540,67 @@ def arrange(progs):
         for p in pre[n]:
             suc[p].append(n)
 
+    lane = [5 * z[0] + "vstgy".index(z[2]) for z in node]
+    took, lag, never = [z[3] for z in node], [z[4] for z in node], 1e18
+
     def run(before, after, weight, back):
-        left = [len(b) for b in before]
-        ready = {}
+        left, since = [len(b) for b in before], [x if back else 0.0 for x in lag]
+        ready, free = [[] for _ in range(5 * len(progs))], [0.0] * (5 * len(progs))
+        start = [never] * len(ready)
         for n in range(len(node)):
             if not left[n]:
-                ready.setdefault((node[n][0], node[n][2]), {})[n] = node[n][4] if back else 0.0
-        done, free, order = [0.0] * len(node), {}, []
-        while len(order) < len(node):
-            t0, q = min((max(min(w.values()), free.get(k, 0.0)), k) for k, w in ready.items() if w)
-            n = max((z for z, x in ready[q].items() if x <= t0), key=lambda z: (weight[z], -z))
-            del ready[q][n]
-            done[n] = free[q] = t0 + node[n][3]
+                ready[lane[n]].append(n)
+                start[lane[n]] = min(start[lane[n]], since[n])
+        done, order = [0.0] * len(node), []
+        for _ in node:
+            t0 = min(start)
+            q = start.index(t0)
+            n = max((z for z in ready[q] if since[z] <= t0), key=lambda z: weight[z])
+            ready[q].remove(n)
+            done[n] = free[q] = t = t0 + took[n]
             order.append(n)
+            start[q] = max(t, min(since[z] for z in ready[q])) if ready[q] else never
             for s in after[n]:
+                since[s] = max(since[s], t + (lag[s] if back else lag[n]))
                 left[s] -= 1
                 if not left[s]:
-                    ready.setdefault((node[s][0], node[s][2]), {})[s] = max(done[p] + (node[s][4] if back else node[p][4]) for p in before[s])
-        return done, order, max(done[n] + (0.0 if back else node[n][4]) for n in range(len(node)))
+                    ready[lane[s]].append(s)
+                    start[lane[s]] = min(start[lane[s]], max(free[lane[s]], since[s]))
+        return done, order
+
+    def span(order, times):
+        done, free, (took, lag) = [0.0] * len(node), [0.0] * (5 * len(progs)), times
+        for n in order:
+            t = free[lane[n]]
+            for p in pre[n]:
+                if done[p] > t:
+                    t = done[p]
+            free[lane[n]] = t = t + took[n]
+            done[n] = t + lag[n]
+        return max(done)
 
     rest = run(suc, pre, run(pre, suc, [-n for n in range(len(node))], False)[0], True)[0]
-    kinds = sorted(set(z[5] for z in node if z[2] in "vs" and z[1] > 110))
+    rest = [x - 1e-3 * n for n, x in enumerate(rest)]
+    kinds = sorted(set((z[5][0], z[5][1][:k]) for z in node if z[2] in "vs" and z[1] > 110 for k in (2, 3, 5)))
     lift, best, seed = dict(PAR["lift"]), None, 12345
     for k in range(PAR["tries"] + 1):
         trial = dict(lift)
         if k:
             seed = (seed * 1103515245 + 12345) % 2 ** 31
             kind = kinds[(seed >> 8) % len(kinds)]
-            step = (-4000, -2000, -1000, -400, 400, 1000, 2000, 4000)[(seed >> 20) % 8]
+            step = (-3000, -1500, -700, -300, 300, 700, 1500, 3000)[(seed >> 20) % 8]
             for z in ([kind] if (seed >> 24) % 2 else [(0, kind[1]), (1, kind[1])]):
                 trial[z] = trial.get(z, 0) + step
-        done, order, end = run(pre, suc, [x + trial.get(z[5], 0) for x, z in zip(rest, node)], False)
+        by = {}
+        for z in set(z[5] for z in node):
+            by[z] = sum(trial.get(y, 0) for y in set((z[0], z[1][:j]) for j in (2, 3, 5)))
+        order = run(pre, suc, [x + by[z[5]] for x, z in zip(rest, node)], False)[1]
+        ends = [span(order, times) for times in [(took, lag)] + others]
+        end = sum(x / w for x, w in zip(ends, PAR["weigh"]))
         if best is None or end < best[1]:
-            lift, best = trial, (order, end)
-    return [[(node[n][1], node[n][2]) for n in best[0] if node[n][0] == r] for r in range(len(progs))], best[1]
+            lift, best = trial, (order, end, ends)
+    ORDER["lift"] = lift
+    return [[(node[n][1], node[n][2]) for n in best[0] if node[n][0] == r] for r in range(len(progs))], best[2]
 
 
 def rank_program(g, core, T, topo):
@@ -514,7 +608,7 @@ def rank_program(g, core, T, topo):
     if rank is None:
         return
     if "order" not in ORDER:
-        ORDER["order"] = arrange([build(g, r, T, topo) for r in range(len(T.cores))])[0]
+        ORDER["order"] = arrange(lambda: [build(g, r, T, topo) for r in range(len(T.cores))])[0]
     ops, arrive = build(g, rank, T, topo)
     queue = {"v": g.vector, "s": g.scalar, "t": g.tensor, "g": g, "y": g.sync}
     own = {"v": "sv", "s": "ss", "t": "st", "g": "sp"}

@@ -12,17 +12,23 @@ SH = float(2 ** 23)
 HUGE = float(2 ** 26)
 F32, BF, U16, I32, F16 = "float32", "bfloat16", "uint16", "int32", "float16"
 Q4, U8 = "float8_e4m3fn_x4", "uint8"
-PAR = {"nv": 14,
-       "both": [(1, "a1")], "run": [1, 1],
-       "plain": [(d, z) for d in range(2) for z in ("a0", "a2", "b0", "c2")] + [(0, "b1"), (1, "b2")],
-       "onv": [["x_21", "x_31", "x_30", "gr1", "gr2", "y0_1", "y0_2", "yeb3"], ["x_21", "x_31", "x_30", "gr0", "gr1", "gr2", "y0_0"]],
-       "lift": {(0, "ds"): -3000, (1, "ds"): -3000, (0, "dg"): -300, (1, "dg"): -300, (1, "cl"): -700, (0, "fr"): -700, (1, "fr"): -700,
-                (0, "y0"): -700, (1, "y0"): -700, (1, "pr"): 700, (1, "se"): 1500, (1, "cr0_"): 1500, (0, "cl9"): -700, (0, "cr1"): -4500,
-                (0, "kw"): 1500, (1, "kw"): 1500, (1, "cr1"): -1500, (0, "cr2_"): 700, (0, "x_30"): 1500, (1, "x_30"): 1500, (0, "gac11"): 1500},
-       "also": [{"cyc": 0.83, "wake": 150.0, "gat": 1.3, "sca": 3.0}, {"cyc": 1.15, "wake": 80.0, "gat": 1.9, "sca": 5.0}],
-       "weigh": [1.0, 0.96, 1.3],
-       "scn": 1.0, "cyc": 0.9, "tt": 1.0, "gat": 1.56, "sca": 3.8, "sfix": 100.0, "wake": 110.0, "far": 2200.0, "issue": 400.0, "first": 1500.0,
-       "tries": 1000}
+PAR = {"nv": 12,
+       "both": [(1, "a1")], "run": [1, 1], "pack": [0, 1], "low": 12, "big": False, "steps": True, "ahead": [1], "slot": True,
+       "self": [(0, z) for z in ("b0", "b1", "b3", "c1", "c2", "c3")] + [(1, z) for z in ("b0", "b1", "b2", "b3", "c0", "c1", "c2")],
+       "plain": [(0, z) for z in ("a0", "a1", "a3", "b0", "b1", "c2")] + [(1, z) for z in ("a0", "a3", "b0", "b3", "c0", "c3")],
+       "onv": [z + ["x_21", "x_31", "x_30", "kwc", "gr1"] + ["f64_%d" % k for k in range(4)]
+               for z in (["gr2", "adw1", "yec2", "x_00"], ["yec0", "frow"])],
+       "lift": {(0, "ds"): -3000, (1, "ds"): -3000, (0, "dg"): -300, (1, "dg"): -300, (1, "cl"): -700, (0, "fr"): -700, (1, "fr"): -3000,
+                (0, "y0"): -700, (1, "y0"): -700, (1, "pr"): 700, (1, "se"): -1500, (1, "cr0_"): 1500, (0, "cl9"): -700, (0, "cr1"): -4500,
+                (0, "kw"): 1500, (1, "kw"): 1500, (1, "cr1"): -1500, (0, "cr2_"): 700, (0, "x_30"): 1500, (1, "x_30"): 1500, (0, "gac11"): 1500,
+                (1, "gba01"): -1400, (0, "pbw"): -100, (0, "row"): 700, (0, "ev"): 1500, (1, "ev"): 1500, (0, "ad"): -9000,
+                (0, "seed0"): 1500, (1, "seed0"): 1500, (0, "lua"): 700, (1, "lua"): 700, (1, "cr9_"): -1400, (1, "cr4"): -1500,
+                (0, "gd"): 1500, (1, "gd"): 1500, (0, "gd2"): -1500, (1, "gd2"): -1500, (0, "or"): -700, (1, "or"): -700, (0, "fa"): -1500,
+                (0, "cl4"): -700, (0, "cb"): 1500, (1, "cb"): 1500, (0, "kro"): 700, (1, "kro"): 700},
+       "also": [{"cyc": 0.83, "wake": 130.0, "gat": 1.2, "sca": 2.5}, {"cyc": 1.2, "wake": 100.0, "gat": 2.0, "sca": 5.5}],
+       "weigh": [1.0, 0.92, 1.42],
+       "scn": 1.0, "cyc": 0.9, "tt": 1.0, "gat": 1.56, "sca": 3.8, "sfix": 0.0, "wake": 110.0, "far": 2200.0, "issue": 400.0, "first": 1500.0,
+       "tries": 300, "polish": 7000, "slack": 100.0}
 
 
 def _sb(n, d):
@@ -38,27 +44,27 @@ SCRATCH = {
     "lq0": _sb(A, Q4), "ls0": _sb(A, U8), "lq1": _sb(A, Q4), "ls1": _sb(A, U8), "lq2": _sb(A, Q4), "ls2": _sb(A, U8),
     "pa": ("psum", [128, 512], F32), "pb": ("psum", [128, 512], F32), "pw": ("psum", [128, 2048], F32),
     "pi": _sb(32, I32), "qc": _sb(16, F32), "q16": _sb(C, F32), "meq": _sb(C, BF), "keep": _sb(C, BF),
-    "c0a": _sb(C, F32), "c0b": _sb(C + 16, BF), "c0": _sb(C, BF), "c0h": _sb(C, BF), "ur16": _sb(8, U16),
+    "c0a": _sb(C, F32), "c0b": _sb(C + 16, BF), "c0": _sb(C, BF), "c0h": _sb(2 * C, BF), "ur16": _sb(8, U16),
     "iot": _sb(C, F32), "t512": _sb(2 * C, F32), "rho": _sb(2 * C, F32), "rhm": _sb(2 * C, F32), "phi": _sb(C, F32), "nstep": _sb(C, BF),
     "m16": _sb(NB, F32), "c16": _sb(NB, F32), "self2": _sb(80, F32), "selfa": _sb(NB, F32), "cwin": _sb(80, F32),
     "kwin": _sb(40, F32), "addc": _sb(80, F32), "cl16": _sb(80, U16), "cw": _sb(32 * 16, F32), "ci": _sb(16, I32),
     "kp": _sb(PW, BF), "cpa": _sb(2 * PW, F32),
-    "dm": _sb(C, F32), "hold": _sb(C, F32), "eq": _sb(C, BF), "eqs": _sb(C, BF), "cmp": _sb(15 * C, BF), "cs": _sb(15 * C, F16),
-    "sg": _sb(9 * C, BF), "junk": _sb(19 * C, BF), "acc": _sb(32, F32), "sm1": _sb(32, F32), "aw": _sb(NB, F32),
+    "dm": _sb(C, F32), "hold": _sb(C, F32), "eq": _sb(C, BF), "eqs": _sb(C, BF), "cmp": _sb(15 * C, BF), "cs": _sb(NB * C, F16),
+    "sg": _sb(9 * C, BF), "junk": _sb(21 * C, BF), "acc": _sb(32, F32), "sm1": _sb(32, F32),
     "a16": _sb(72, U16), "b16": _sb(72, U16), "o16": _sb(72, U16), "ob16": _sb(72, U16), "dsn": _sb(36, F32), "s16": _sb(72, U16), "sl16": _sb(48, U16),
     "n16": _sb(240, U16), "nl16": _sb(120, U16), "p16": _sb(120, U16), "pl16": _sb(120, U16),
-    "orow": _sb(C, BF), "dg": _sb(4 * C, F32), "dh": _sb(4 * C, F16), "rrow": _sb(C, F32), "hf": _sb(4 * C, F16),
-    "oy16": _sb(80, U16), "krow": _sb(C, F32), "kw": _sb(80, F32), "sum16": _sb(NB, U16),
-    "brow": _sb(C, F32), "kbw": _sb(40, F32), "bw16": _sb(NB, U16), "w8": _sb(NB, F32), "pbw": _sb(80, F32),
+    "orow": _sb(C, BF), "dg": _sb(C, F32), "dh": _sb(6 * C, F16), "pb2": _sb(4 * C, BF), "rrow": _sb(C, F32), "hf": _sb(4 * C, F16),
+    "oy16": _sb(80, U16), "krow": _sb(C, F32), "kw": _sb(120, F32), "sum16": _sb(44, U16),
+    "brow": _sb(C, F32), "kbw": _sb(40, F32), "bw16": _sb(NB, U16), "pbw": _sb(80, F32),
     "addw": _sb(120, F32), "qv": _sb(PW, F32), "cb": _sb(PW, BF), "cab": _sb(2 * PW, F32), "pr": _sb(2 * PW, F32), "prc": _sb(PW, BF),
     "mm": _sb(2 * C, BF), "ma": _sb(C, F32), "rows": _sb(2 * C, F32), "gr": _sb(2 * C, F32),
     "gd": _sb(2 * C, F32), "seed": _sb(72, F32), "zi": _sb(120, I32), "zf": _sb(52, F32), "ev": _sb(80, F32),
     "own": _sb(80, F32), "li": _sb(80, I32), "lj": _sb(120, I32), "pk": _sb(3 * C, F32),
     "iotc": _sb(C, BF), "erow": _sb(C, BF), "e16": _sb(NB, U16),
     "y0": _sb(4 * C, BF), "y1": _sb(4 * C, BF), "ye": _sb(4 * C, BF), "ga": _sb(16 * C, BF), "gb": _sb(16 * C, BF), "vw": _sb(8 * C, BF),
-    "d0": _sb(24 * C, BF), "d1": _sb(24 * C, BF), "vv": _sb(12 * C, BF), "ft": _sb(4 * A, BF), "f64": _sb(4 * A, BF), "zz": _sb(4 * C, BF), "yo": _sb(C, F32),
+    "d0": _sb(24 * C, BF), "d1": _sb(24 * C, BF), "vv": _sb(12 * C, BF), "ft": _sb(8 * A, BF), "f64": _sb(4 * A, BF), "zz": _sb(4 * C, BF), "yo": _sb(C, F32),
 }
-SEMAPHORES = (["sv", "ss", "st", "sp", "ldx", "ldz", "ldu", "ldw", "lds", "ldv", "sto", "loc"]
+SEMAPHORES = (["sv", "ss", "st", "sp", "ldx", "ldz", "ldu", "ldw", "lds", "ldv", "sto", "loc", "lc00", "lc01", "lc10", "lc11"]
               + ["r%s%d" % (k, t) for k in "aopnsf" for t in range(3)])
 
 ADD, SUB, MUL, MAX, MIN = AluOpType.add, AluOpType.subtract, AluOpType.mult, AluOpType.max, AluOpType.min
@@ -128,11 +134,11 @@ def build(g, rank, T, topo):
         add({"t": (lambda: P.matmul_mx(o, a, sa, b, sb, True, True), (n + 16) * 0.83)}, r, w)
 
     def act(o, i, f, r, w, n, **k):
-        add({"s": (lambda: S.activation(o, i, f, **k), PAR["sfix"] + n * cyc + (20 if "accum_out" in k else 0))}, r, w)
+        add({"s": (lambda: S.activation(o, i, f, **k), PAR["sfix"] + max(64, n) * cyc + (20 if "accum_out" in k else 0))}, r, w)
 
-    def lin(o, i, scale, bias, r, w, n=NB):
-        add({"s": (lambda: S.activation(o, i, AF.Identity, bias=bias, scale=scale), PAR["sfix"] + n * cyc),
-             "v": (lambda: V.tensor_scalar(o, i, scale, bias, MUL, ADD), max(64, n) * cyc)}, r, w)
+    def lin(o, i, scale, bias, r, w, n=NB, fast=1.0):
+        add({"s": (lambda: S.activation(o, i, AF.Identity, bias=bias, scale=scale), PAR["sfix"] + max(64, n) * cyc),
+             "v": (lambda: V.tensor_scalar(o, i, scale, bias, MUL, ADD), max(64, n * fast) * cyc)}, r, w)
 
     def gat(o, win, off, r, w, n=C, scale=None, bias=None):
         i = win.indirect(off)
@@ -160,7 +166,7 @@ def build(g, rank, T, topo):
         scan(o, T.c0[:, 0:n], i, ADD, MIN, r + " c0", w, n)
 
     def diag2(k, i, r, w):
-        scan(T.dh[:, C * k:C * k + C], T.c0h[:], i, ADD, MIN, r + " c0h", w, C / 2)
+        scan(T.dh[:, C * k:C * k + C], T.c0h[:, 0:C], i, ADD, MIN, r + " c0h", w, C / 2)
         return T.dh[:, C * k + 15:C * k + C:16]
 
     def send(dst, src, sem, peer, engines, r, w, size, before=0):
@@ -225,7 +231,8 @@ def build(g, rank, T, topo):
     lin(T.c0b[:, 1:C + 1], T.meq[:], SH, 0.0, "meq", "c0b", C)
     lin(T.eq[:], T.meq[:], HUGE, 0.0, "meq", "eq", C)
     tt(T.c0[:], T.eq[:], T.c0b[:, 0:C], SUB, "eq c0b c0z", "c0", TB)
-    lin(T.c0h[:], T.c0[:], 1024.0 / SH, 0.0, "c0", "c0h", C)
+    lin(T.c0h[:, 0:C], T.c0[:], 1024.0 / SH, 0.0, "c0", "c0h", C)
+    lin(T.c0h[:, C:2 * C], T.c0[:], 1024.0 / SH, 0.0, "c0", "c0i", C)
     W = [T.cw[:, 16 * k:16 * k + 14] for k in range(32)]
     E = [T.cw[:, 16 * k + 14:16 * k + 16] for k in range(32)]
     ts(T.ci[:, 0:14], T.self2[:, 0:14], -10.0, 1.0 / 21.0, ADD, MUL, "selfx", "ci")
@@ -245,8 +252,8 @@ def build(g, rank, T, topo):
     tt(W[8], W[6], W[0], ADD, "W6 W0", "W8")
     tt(W[9], W[4], W[7], SUB, "W4 W7", "W9")
     act(W[10], W[9], AF.Relu, "W9", "W10", 14, bias=1.0, scale=-1.0)
-    lin(T.addc[:, 0:20], T.m16[:], 0.0, SHC, "m16 shc", "ac0")
     for d in sorted(set(sides)):
+        ts(T.addc[:, 20 * d:20 * d + 20], T.cwin[:, 40 * d:40 * d + 20], SHC, None, SUB, None, "cw0 cw2 shc", "ac%d" % d)
         c, b = 30 * d, 11 + 8 * d
         sg, z = (1.0, 0.0) if d == 0 else (-1.0, 19.0)
         n = ["V%d" % (b + k) for k in range(8)]
@@ -283,14 +290,15 @@ def build(g, rank, T, topo):
     c = 30 * sides[0]
     gat(T.kp[:], T.kwin[:], T.cl16[:, c:c + 14], "kw0 kw1 clp%d" % sides[0], "kp", PW)
 
-    for low in sorted(set(int(PAR["run"][d] == d) for d in sides)):
-        for k in range(4):
-            at, big = 3 * C * (4 * low + k), 1e29 if low else -1e29
-            zero = T.d0[:, at + 1:at + 3 * C:3]
-            iota(zero, [[0, C]], 0, 0, "cz%d%d" % (low, k))
-            for o, w in ((T.d0[:, at:at + 3 * C:3], "ct%d%d"), (T.d1[:, at + 2:at + 3 * C:3], "cs%d%d")):
-                add({"g": (lambda o=o, zero=zero, big=big: g.affine_select(o, zero, [[0, C]], GT, big, 0, 0), 170 + 2 * C * cyc)},
-                    "cz%d%d ct%d%d" % (low, k, low, k), w % (low, k))
+    for low in range(2 if PAR["steps"] else 0):
+        at, big, n = 12 * C * low, 1e29 if low else -1e29, 3 * A
+        iota(T.d0[:, at:at + n], [[0, n]], 0, 0, "c0%d" % low)
+        for o, i, m, w in ((T.d1[:, at:at + n], T.d0[:, at:at + n], n, "c1%d"), (T.d0[:, at:at + n:3], T.d0[:, at + 1:at + n:3], A, "c0%d")):
+            add({"g": (lambda o=o, i=i, m=m, big=big: g.affine_select(o, i, [[0, m]], GT, big, 0, 0), 170 + 2 * m * cyc)}, "c0%d" % low, w % low)
+        for k in range(3):
+            for j, u in enumerate((T.d0, T.d1)):
+                w = "c%d%d" % (j, low)
+                dma("y", u[:, at + (n << k):at + (n << k + 1)], u[:, at:at + (n << k)], w, w, "l" + w, 256 * n << k)
     frow, oph, bph, gh = [T.hf[:, C * k:C * k + C] for k in range(4)]
     xi = T.zi[:, 64:84]
     xall = [" ".join("x_%d%d" % (k, h) for k in range(4)) for h in range(2)]
@@ -317,7 +325,7 @@ def build(g, rank, T, topo):
             tt(T.dm[:, a:b], s, T.meq[:, a:b], MUL, ks + " meq keep", "dm%d" % h, A)
             scan(T.hold[:, a:b], T.keep[:, a:b], T.dm[:, a:b], MUL, ADD, "keep dm%d" % h, "hold%d" % h, A)
             tt(T.eq[:, a:b], s, T.hold[:, a:b], EQ, ks + " hold%d c0" % h, "eq%d" % h, A)
-            scan(T.eqs[:, a:b], T.keep[:, a:b], T.eq[:, a:b], MUL, ADD, "keep eq%d" % h, "eqs%d" % h, A / 2)
+            scan(T.eqs[:, a:b], T.keep[:, a:b], T.eq[:, a:b], MUL, SUB, "keep eq%d" % h, "eqs%d" % h, A / 2)
         for k in range(NS):
             n = 16 * (NV + k) + 16
             act(T.sg[:, C * k:C * k + C], T.pb[:, 0:C], AF.Sign, "pb hold1", "sg%d" % k, C, bias=T.hold[:, n - 1:n], scale=-1.0)
@@ -331,25 +339,36 @@ def build(g, rank, T, topo):
             ts(T.cmp[:, C * m:C * m + n], T.pa[:, 0:n], sc, None, GE, None, r, "cl%d_" % m, n)
             ts(T.cmp[:, C * m + n:C * m + C], T.pa[:, n:C], sc, None, GT, None, r, "cr%d_" % m, C - n)
             scan(T.cs[:, C * m + A:C * m + C], T.cmp[:, C * m:C * m + A], T.cmp[:, C * m + A:C * m + C], ADD, ADD,
-                 "cl%d_ cr%d_" % (m, m), "cs%d" % m, C / 4)
-        tt(T.sm1[:, 0:NS], T.c16[:, NV:NB], T.eqs[:, 16 * NV + 15:C:16], SUB, "c16 eqs1", "sm1a")
-        tt(T.sm1[:, 16:16 + NS], T.acc[:, 16:16 + NS], T.acc[:, 0:NS], SUB, " ".join("lt%d gt%d" % (k, k) for k in range(NS)), "sm1b")
-        tt(T.aw[:, NV:NB], T.sm1[:, 0:NS], T.sm1[:, 16:16 + NS], ADD, "sm1a sm1b", "aw1")
-        tt(T.aw[:, 0:NV], T.cs[:, C - 1:NV * C:C], T.eqs[:, 15:16 * NV:16], SUB, "eqs0 eqs1 " + " ".join("cs%d" % m for m in range(NV)), "aw0")
-        cp(a16, T.aw[:], "aw0 aw1", ka)
-        send(b16, a16, "ra%d" % t, peer, eng[:half] if t == 0 else eng, ka, kb, 5120)
+                 "cl%d_ cr%d_ eqs%d" % (m, m, m // 10), "cs%d" % m, C / 4, T.eqs[:, n - 1:n])
+        tt(T.sm1[:, 0:NS], T.c16[:, NV:NB], T.eqs[:, 16 * NV + 15:C:16], ADD, "c16 eqs1", "sm1a")
+        tt(T.sm1[:, 16:16 + NS], T.acc[:, 16:16 + NS], T.sm1[:, 0:NS], ADD, "sm1a gt " + " ".join("gt%d" % k for k in range(NS - 1)), "sm1b")
+        tt(T.cs[:, C * NV + C - 1:NB * C:C], T.sm1[:, 16:16 + NS], T.acc[:, 0:NS], SUB, "sm1b " + " ".join("lt%d" % k for k in range(NS)), "aw1")
+        aw, kaw = T.cs[:, C - 1:NB * C:C], "aw1 " + " ".join("cs%d" % m for m in range(NV))
+        cp(a16, aw, kaw, ka)
+        few = eng[:half] if t == 0 else eng
+        send(b16, a16, "ra%d" % t, peer, few, ka, kb, 5120)
 
         al, kal = (a16, ka) if d == 0 else (b16, kb)
         pl, ql, el = T.cl16[:, 30 * d:30 * d + 14], T.cl16[:, 30 * d + 14:30 * d + 28], T.cl16[:, 30 * d + 28:30 * d + 30]
         kbw = "kbw0 kbw2"
         scatter = 50 + C * PAR["sca"]
-        cp(T.orow[:].indirect(a16), T.iotc[:], ka + " iotc", "orow", scatter)
+        if d == 0 and PAR["slot"]:
+            ts(T.zi[:, 96:116], aw, -9.5, 0.05, ADD, MUL, kaw, "fa")
+            ts(T.kw[:, 80:100], T.zi[:, 96:116], -319.0 / 16, None, MUL, None, "fa", "fb")
+            tt(T.kw[:, 100:120], T.kw[:, 80:100], aw, ADD, "fb " + kaw, "fc")
+            ts(T.sum16[:, 24:44], T.kw[:, 100:120], 16.0, None, MUL, None, "fc", "fd")
+            cp(T.orow[:].indirect(T.sum16[:, 24:44]), T.iotc[:], "fd iotc", "orow", scatter)
+        else:
+            cp(T.orow[:].indirect(a16), T.iotc[:], ka + " iotc", "orow", scatter)
         gat(T.rrow[:], T.rhm[:, C * d:C * d + C], al, kal + " rhm%d" % d, "rrow")
         gat(frow, T.phi[:], al, kal + " phi", "frow")
         if d == 0:
-            gat(oph, T.orow[:], T.cl16[:, 60:80], "orow clf", "oph")
-            ts(o16, diag2(0, oph, "oph", "dg0"), SHH, float(A), ADD, ADD, "dg0 shh", ko)
-            send(ob16, o16, "ro%d" % t, peer, eng, ko, "ob%d" % t, 5120, None)
+            if PAR["slot"]:
+                ts(o16, diag2(0, T.orow[:], "orow", "dg0"), SHH, float(A), ADD, ADD, "dg0 shh", ko)
+            else:
+                gat(oph, T.orow[:], T.cl16[:, 60:80], "orow clf", "oph")
+                ts(o16, diag2(0, oph, "oph", "dg0"), SHH, float(A), ADD, ADD, "dg0 shh", ko)
+            send(ob16, o16, "ro%d" % t, peer, few, ko, "ob%d" % t, 5120, None)
             cp(T.ma[:].indirect(b16), T.rrow[:], kb + " rrow", "ma", scatter)
             gat(T.brow[:], T.iot[:], b16, kb + " iot", "brow")
             osl, kosl = o16, ko
@@ -357,7 +376,7 @@ def build(g, rank, T, topo):
             ts(o16, diag2(0, T.orow[:], "orow", "dg0"), SHH, float(A), ADD, ADD, "dg0 shh", ko)
             gat(T.ma[:], T.rrow[:], o16, "rrow " + ko, "ma")
             osl, kosl = ob16, "ob%d" % t
-            expect("ro%d" % t, kosl, len(eng))
+            expect("ro%d" % t, kosl, len(few))
             gat(T.brow[:], T.iot[:], a16, ka + " iot", "brow")
         gat(bph, T.brow[:], osl, "brow " + kosl, "bph")
         ends = diag2(1, bph, "bph", "dg1")
@@ -365,32 +384,39 @@ def build(g, rank, T, topo):
         ts(T.kbw[:, 0:20], ends, SHH, 1.0 - 2 * d, ADD, MUL, "dg1 shh", "kbw0")
         for k in range(4):
             ts(T.oy16[:, NB * k:NB * k + NB], osl, 4.0, float(k), MUL, ADD, kosl, "oy%d" % k)
-            gat(T.y0[:, C * k:C * k + C], X[:], T.oy16[:, NB * k:NB * k + NB], xk + " oy%d" % k, "y0_%d" % k, C, 64.0)
-        ts(T.kw[:, 0:20], b16, 0.0, None, ADD, None, kb, "kwa")
-        tt(T.kw[:, 20:40], T.kw[:, 0:20], T.aw[:], ADD, "kwa aw0 aw1", "kwb")
-        cp(T.sum16[:], T.kw[:, 20:40], "kwb", "sum16")
-        ts(T.kw[:, 40:60], T.kw[:, 20:40], -512.0, None, MUL, None, "kwb", "kwc")
-        tt(T.krow[:], T.t512[:].indirect(T.sum16[:]), T.iot[:], ADD, "sum16 t512 iot", "krow", 50 + 2 * C)
-        tt(T.kw[:, 60:80], T.kw[:, 40:60], T.self2[:, 0:20], ADD, "kwc selfx", "kwd")
-        dsn = T.dsn[:, 12 * t:12 * t + 10]
-        dk = " ".join("%s_%d" % (kd, k) for k in range(10))
-        for k in range(10):
-            m = 10 * d + k
-            act(T.junk[:, C * (9 + k):C * (10 + k)], T.krow[:], AF.Sign, "krow kwd", "%s_%d js%d" % (kd, k, k), C,
-                bias=T.kw[:, 60 + m:61 + m], scale=-1.0, accum_out=T.dsn[:, 12 * t + k:12 * t + k + 1])
-        s16, sl16, ks = T.s16[:, 24 * t:24 * t + NB], T.sl16[:, 16 * t:16 * t + 10], "sa%d sb%d" % (t, t)
-        mine, other = [T.s16[:, 24 * t + 10 * k:24 * t + 10 * k + 10] for k in (d, 1 - d)]
-        ts(mine, dsn, 319.0, 0.5, ADD, MUL, dk, "sa%d" % t)
-        send(sl16, mine, "rs%d" % t, peer, eng[half:] if t == 0 else eng, "sa%d" % t, kdl, 2560)
-        cp(other, sl16, kdl, "sb%d" % t)
+            gat(T.y0[:, C * k:C * k + C], X[:], T.oy16[:, NB * k:NB * k + NB], xk + " oy%d" % k, "y0_%d" % k, C, 64.0 if PAR["big"] else None)
+        if d in PAR["ahead"]:
+            tt(T.c0a[:], T.t512[:].indirect(a16), T.iot[:], ADD, ka + " t512 iot", "c0a", 50 + 2 * C)
+            ts(T.kw[:, 0:20], aw, -512.0, None, MUL, None, kaw, "kwa")
+            tt(T.kw[:, 20:40], T.kw[:, 0:20], T.self2[:, 0:20], ADD, "kwa selfx", "kwb")
+            tt(T.krow[:], T.t512[:].indirect(b16), T.c0a[:], ADD, kb + " t512 c0a", "krow", 50 + 2 * C)
+            ts(T.kw[:, 40:60], b16, -512.0, None, MUL, None, kb, "kwc")
+            tt(T.kw[:, 60:80], T.kw[:, 40:60], T.kw[:, 20:40], ADD, "kwc kwb", "kwd")
+        else:
+            ts(T.kw[:, 0:20], b16, 0.0, None, ADD, None, kb, "kwa")
+            tt(T.kw[:, 20:40], T.kw[:, 0:20], aw, ADD, "kwa " + kaw, "kwb")
+            cp(T.sum16[:, 0:NB], T.kw[:, 20:40], "kwb", "sum16")
+            lin(T.kw[:, 40:60], T.kw[:, 20:40], -512.0, 0.0, "kwb", "kwc")
+            tt(T.krow[:], T.t512[:].indirect(T.sum16[:, 0:NB]), T.iot[:], ADD, "sum16 t512 iot", "krow", 50 + 2 * C)
+            tt(T.kw[:, 60:80], T.kw[:, 40:60], T.self2[:, 0:20], ADD, "kwc selfx", "kwd")
+        cut = [(0, PAR["low"]), (PAR["low"], NB)]
+        (m0, m1), (k0, k1) = cut[d], cut[1 - d]
+        dk = " ".join("ds_%d" % k for k in range(m1 - m0))
+        for k in range(m1 - m0):
+            act(T.junk[:, C * (9 + k):C * (10 + k)], T.krow[:], AF.Sign, "krow kwd", "ds_%d js%d" % (k, k), C,
+                bias=T.kw[:, 60 + m0 + k:61 + m0 + k], scale=-1.0, accum_out=T.dsn[:, k:k + 1])
+        s16, ks = T.s16[:, 24 * t:24 * t + NB], "sa%d sb%d" % (t, t)
+        mine = T.s16[:, 24 * t + m0:24 * t + m1]
+        ts(mine, T.dsn[:, 0:m1 - m0], 319.0, 0.5, ADD, MUL, dk, "sa%d" % t)
+        send(T.sl16[:, 16 * t:16 * t + m1 - m0], mine, "rs%d" % t, peer, eng[half:] if t == 0 else eng, "sa%d" % t, kdl, 2560)
+        cp(T.s16[:, 24 * t + k0:24 * t + k1], T.sl16[:, 16 * t:16 * t + k1 - k0], kdl, "sb%d" % t)
         cp(T.erow[:].indirect(s16), frow, ks + " frow", "erow", scatter)
         ts(T.e16[:], diag2(2, T.erow[:], "erow", "dg3"), SHH, float(A), ADD, ADD, "dg3 shh", "e16")
         gat(T.qv[:], T.kbw[:], ql, kbw + " clq%d" % d, "qv", PW)
-        ts(T.w8[:], T.kbw[:, 0:20], KS, None, MUL, None, kbw, "w8")
+        lin(T.addw[:, 60 * d + 20:60 * d + 40], T.kbw[:, 0:20], KS, SHC, "kbw0 shc", "adw1")
         if d == 1:
             tt(T.addw[:, 100:120], T.addc[:, 60:80], T.kbw[:, 0:20], SUB, "acm kbw0", "adw21")
-        tt(T.pbw[:, 40 * d:40 * d + 20], T.w8[:], T.cwin[:, 40 * d:40 * d + 20], ADD, "w8 cw0 cw2", "pbw0")
-        tt(T.addw[:, 60 * d + 20:60 * d + 40], T.w8[:], T.addc[:, 0:20], ADD, "w8 ac0", "adw1")
+        tt(T.pbw[:, 40 * d:40 * d + 20], T.addw[:, 60 * d + 20:60 * d + 40], T.addc[:, 20 * d:20 * d + 20], ADD, "adw1 ac%d" % d, "pbw0")
         tt(T.cb[:], T.kbw[:].indirect(pl), T.qv[:], LT, kbw + " qv clp%d" % d, "cb", 50 + 2 * PW)
         tt(T.cab[:, 0:PW], T.cb[:], T.cpa[:, PW * d:PW * d + PW], MUL, "cb cpa%d" % d, "ca", 2 * PW)
         tt(T.cab[:, PW:2 * PW], T.pbw[:, 40 * d:40 * d + 40].indirect(pl), T.cb[:], MUL, "cb pbw0 pbw2%d" % d, "cbb", 50 + 2 * PW)
@@ -425,37 +451,49 @@ def build(g, rank, T, topo):
             tt(T.li[:, 40 * w:40 * w + 40], T.zf[:, 0:40], T.ev[:, c:c + 40], MAX, "zf ev0 ev1 ev2" if c else "zf ev0 ev1", "li%d" % w, 80)
         ts(T.lj[:, 0:80], T.li[:], 511, None, AND, None, "li0 li1", "lj", 80)
         ts(T.n16[:, 80 * t:80 * t + 80], T.lj[:, 0:80], 1.0 - 2 * d, 511.0 * d, MUL, ADD, "lj", kn, 80)
-        send(nl16, T.n16[:, 80 * t:80 * t + 40], "rn%d" % t, peer, eng, kn, knl, 10240)
+        send(nl16, T.n16[:, 80 * t:80 * t + 40], "rn%d" % t, peer, few, kn, knl, 10240)
         p16, pl16, kp, kpl = T.p16[:, 40 * t:40 * t + 40], T.pl16[:, 40 * t:40 * t + 40], "p%d" % t, "pl%d" % t
-        gat(T.pk[:, 0:C], T.iot[:], T.n16[:, 80 * t + 40:80 * t + 60], "iot " + kn, "pk0", C, 512.0)
-        tt(T.pk[:, C:2 * C], T.iot[:].indirect(T.n16[:, 80 * t + 60:80 * t + 80]), T.pk[:, 0:C], ADD, "iot pk0 " + kn, "pk1",
-           max(pick(C), 50 + 2 * TB))
-        gat(T.pk[:, 2 * C:3 * C], T.pk[:, C:2 * C], T.e16[:], "pk1 e16", "pk2")
-        diag(T.dg[:, 3 * C:4 * C], T.pk[:, 2 * C:3 * C], C, "pk2", "dg4")
-        ts(T.zi[:, 32:52], T.dg[:, 3 * C + 15:4 * C:16], SHC, None, ADD, None, "dg4 shc", "zi3")
-        ts(T.lj[:, 80:100], T.zi[:, 32:52], 9, None, AluOpType.arith_shift_right, None, "zi3", "lk0")
-        ts(T.lj[:, 100:120], T.zi[:, 32:52], 511, None, AND, None, "zi3", "lk1")
-        cp(p16, T.lj[:, 80:120], "lk0 lk1", kp)
+        if d in PAR["pack"]:
+            gat(T.pk[:, 0:C], T.iot[:], T.n16[:, 80 * t + 40:80 * t + 60], "iot " + kn, "pk0", C, 512.0)
+            tt(T.pk[:, C:2 * C], T.iot[:].indirect(T.n16[:, 80 * t + 60:80 * t + 80]), T.pk[:, 0:C], ADD, "iot pk0 " + kn, "pk1",
+               max(pick(C), 50 + 2 * TB))
+            gat(T.pk[:, 2 * C:3 * C], T.pk[:, C:2 * C], T.e16[:], "pk1 e16", "pk2")
+            diag(T.dg[:], T.pk[:, 2 * C:3 * C], C, "pk2", "dg4")
+            ts(T.zi[:, 32:52], T.dg[:, 15:C:16], SHC, None, ADD, None, "dg4 shc", "zi3")
+            ts(T.lj[:, 80:100], T.zi[:, 32:52], 9, None, AluOpType.arith_shift_right, None, "zi3", "lk0")
+            ts(T.lj[:, 100:120], T.zi[:, 32:52], 511, None, AND, None, "zi3", "lk1")
+            cp(p16, T.lj[:, 80:120], "lk0 lk1", kp)
+        else:
+            gat(T.pb2[:, 0:2 * C], T.iotc[:], T.n16[:, 80 * t + 40:80 * t + 80], "iotc " + kn, "pk0", 2 * C)
+            for k in range(2):
+                gat(T.pb2[:, C * (2 + k):C * (3 + k)], T.pb2[:, C * k:C * k + C], T.e16[:], "pk0 e16", "pk%d" % (2 + k))
+            scan(T.dh[:, 4 * C:6 * C], T.c0h[:], T.pb2[:, 2 * C:4 * C], ADD, MIN, "pk2 pk3 c0h c0i", "dg4", C)
+            ts(p16, T.dh[:, 4 * C + 15:6 * C:16], SHH, float(A), ADD, ADD, "dg4 shh", kp)
         send(pl16, p16, "rp%d" % t, peer, eng, kp, kpl, 10240)
 
-        def toggle(win, kw, lists, c, n, s, own, kown, dst, kd):
+        def toggle(win, kw, lists, c, n, s, own, kown, dst, kd, last):
             k, z, m = s[0] % 4, s[1], n // 16
             js = PAR["run"][d]
-            low = js == d
+            top = d if z[0] == "a" else 1 - d
+            low = js == top
             at = 3 * (C * (4 * low + k) + 16 * c)
             d0, d1, v = T.d0[:, at:at + 3 * n], T.d1[:, at:at + 3 * n], T.vv[:, at % (12 * C):at % (12 * C) + 3 * n]
-            kc, old = " cs%d%d" % (low, k), ["a%d" % k] if z[0] != "a" else ["b%d" % k, "c%d" % k]
-            war = "".join(" vv" + o for o in old)
-            if (d, z) in PAR["plain"]:
+            kc, old = " c0%d c1%d" % (low, low), ["a%d" % k] if z[0] != "a" else ["b%d" % k, "c%d" % k]
+            war = "".join(" vv" + o for o in old) + kc
+            if (d, z) in PAR["plain"] or not PAR["steps"]:
                 for j, (l, kl, a) in enumerate(lists):
                     la, lb = [l[:, a + c + i:a + c + i + m] for i in (0, NB)]
                     ga, o = [u[:, C * (8 * j + s[0]) + 16 * c:C * (8 * j + s[0]) + 16 * c + n] for u in (T.ga, T.gb)]
                     gat(ga, win, la, kw + " " + kl, "ga%s%d" % (z, j), n)
-                    tt(o, win.indirect(lb), ga, MAX if j == d else MIN, "%s %s ga%s%d" % (kw, kl, z, j), "gb%s%d" % (z, j),
-                       max(pick(n), 50 + TB * n / C))
+                    if (d, z) in PAR["plain"] or j != js and (d, z) not in PAR["both"]:
+                        tt(o, win.indirect(lb), ga, MAX if j == top else MIN, "%s %s ga%s%d" % (kw, kl, z, j), "gb%s%d" % (z, j),
+                           max(pick(n), 50 + TB * n / C))
+                    else:
+                        gat(o, win, lb, kw + " " + kl, "gb%s%d" % (z, j), n)
+                        tt(o, o, ga, MAX if j == top else MIN, "ga%s%d gb%s%d" % (z, j, z, j), "lu%s%d gb%s%d" % (z, j, z, j), TB * n / C)
                 lo, hi, v = [u[:, C * i + 16 * c:C * i + 16 * c + n] for u, i in ((T.gb, s[0]), (T.gb, 8 + s[0]), (T.vw, s[0]))]
                 tt(v, lo, hi, ADD, "gb%s0 gb%s1" % (z, z), "vw" + z, TB * n / C)
-                tt(dst, v, own, SUB, "vw%s %s" % (z, kown), kd, TB * n / C)
+                tt(dst, own, v, SUB, "vw%s %s" % (z, kown), kd, last)
                 return
             l, kl, a = lists[js]
             la, lb = [l[:, a + c + i:a + c + i + m] for i in (0, NB)]
@@ -474,21 +512,30 @@ def build(g, rank, T, topo):
                 tt(o, win.indirect(lb), ga, fold, r + " ga" + y + war, "lu" + z, max(pick(n), 50 + TB * n / C))
             scan(v, d0, d1, SUB, MIN if low else MAX, "ga%s%d gb%s%d lu%s" % (z, js, z, js, z) + kc + "".join(" yy" + o for o in old),
                  "vv" + z, 1.5 * n)
-            tt(dst, T.vv[:, at % (12 * C) + 2:at % (12 * C) + 3 * n:3], own, SUB, "vv%s %s" % (z, kown), kd + " yy" + z, TB * n / C)
+            tt(dst, own, T.vv[:, at % (12 * C) + 2:at % (12 * C) + 3 * n:3], SUB, "vv%s %s" % (z, kown), kd + " yy" + z, last)
 
         for k in range(4):
             win = T.y0[:, C * k:C * k + C]
-            toggle(win, "y0_%d" % k, [(T.n16, kn, 80 * t), (T.nl16, knl, 40 * t)], 0, C, (k, "a%d" % k), win, "y0_%d" % k, T.y1[:, C * k:C * k + C], "y1_%d" % k)
+            toggle(win, "y0_%d" % k, [(T.n16, kn, 80 * t), (T.nl16, knl, 40 * t)], 0, C, (k, "a%d" % k), win, "y0_%d" % k,
+                   T.y1[:, C * k:C * k + C], "y1_%d" % k, TB)
         for h in range(2):
             for k in range(4):
                 win, own, z = T.y1[:, C * k:C * k + C], T.ye[:, C * k + A * h:C * k + A * h + A], "bc"[h] + str(k)
-                gat(own, win, T.e16[:, 10 * h:10 * h + 10], "y1_%d e16" % k, "ye" + z, A)
-                dst = T.f64[:, A * k:A * k + A] if h == 0 else T.zz[:, C * k + A:C * k + C]
-                toggle(win, "y1_%d" % k, [(T.p16, kp, 40 * t), (T.pl16, kpl, 40 * t)], 10 * h, A, (4 + k, z), own, "ye" + z, dst, ("f64_%d", "zy%d")[h] % k)
-                if h == 0:
-                    ts(T.ft[:, k:4 * A:4], dst, 0.015625, None, MUL, None, "f64_%d" % k, "ft%d" % k, A / 2)
+                if (d, z) in PAR["self"]:
+                    gat(own, win, T.e16[:, 10 * h:10 * h + 10], "y1_%d e16" % k, "ye" + z, A)
+                    kown, last = "ye" + z, TB / 2
+                else:
+                    own, kown, last = win.indirect(T.e16[:, 10 * h:10 * h + 10]), "y1_%d e16" % k, max(pick(A), 50 + TB / 2)
+                small, ks1 = (T.ft[:, k:4 * A:4], "ft%d" % k) if h == 0 else (T.ft[:, 4 * A + A * k:5 * A + A * k], "fu%d" % k)
+                big, kb1 = (T.f64[:, A * k:A * k + A], "f64_%d" % k) if h == 0 else (T.zz[:, C * k + A:C * k + C], "zy%d" % k)
+                dst, kd = (big, kb1) if PAR["big"] else (small, ks1)
+                toggle(win, "y1_%d" % k, [(T.p16, kp, 40 * t), (T.pl16, kpl, 40 * t)], 10 * h, A, (4 + k, z), own, kown, dst, kd, last)
+                if not PAR["big"]:
+                    lin(big, small, 64.0, 0.0, ks1, kb1, A, 0.5)
+                elif h == 0:
+                    lin(small, big, 0.015625, 0.0, kb1, ks1, A, 0.5)
             if h == 0:
-                quant(fq[:], fs[:], T.ft[:], A, "ft0 ft1 ft2 ft3", "fq%d" % t)
+                quant(fq[:], fs[:], T.ft[:, 0:4 * A], A, "ft0 ft1 ft2 ft3", "fq%d" % t)
                 send(lq[:].bitcast(u8), fq[:].bitcast(u8), "rf%d" % t, peer, eng, "fq%d" % t, "lc%d" % t, 81920, len(eng))
                 send(ls[:], fs[:], "rf%d" % t, peer, eng, "fq%d" % t, "lq%d" % t, 20480, len(eng))
         for k in range(4):
@@ -600,7 +647,70 @@ def arrange(make):
         if best is None or end < best[1]:
             lift, best = trial, (order, end, ends)
     ORDER["lift"] = lift
+    best = polish(best, node, pre, lane, [(took, lag)] + others, span)
     return [[(node[n][1], node[n][2]) for n in best[0] if node[n][0] == r] for r in range(len(progs))], best[2]
+
+
+def polish(best, node, pre, lane, times, span):
+    def chain(order, took, lag):
+        done, free, last, why, start = [0.0] * len(node), {}, {}, [-1] * len(node), [0.0] * len(node)
+        for n in order:
+            t, w = free.get(lane[n], 0.0), last.get(lane[n], -1)
+            for p in pre[n]:
+                if done[p] > t:
+                    t, w = done[p], p
+            why[n], last[lane[n]], start[n] = w, n, t
+            free[lane[n]] = t + took[n]
+            done[n] = t + took[n] + lag[n]
+        n, pairs = done.index(max(done)), []
+        while why[n] >= 0:
+            if lane[why[n]] == lane[n] and why[n] not in pre[n]:
+                pairs.append((why[n], n))
+            n = why[n]
+        return pairs, start
+
+    base, start = best[0], chain(best[0], *times[0])[1]
+    turn, count, seen, name = [], {}, {}, []
+    for n, z in enumerate(node):
+        count[z[0]] = count.get(z[0], -1) + (z[5][1] == "xq1")
+        turn.append(count[z[0]])
+        k = (z[0], turn[n], z[5], z[2])
+        seen[k] = seen.get(k, 0) + 1
+        name.append((z[5], z[2], seen[k], (0, 1, 1, 3)[turn[n]]) if turn[n] >= 0 else k + (seen[k],))
+    begin = [min(start[n] for n in base if turn[n] == t) for t in range(4)] + [0.0]
+    place = {}
+    for n in sorted(base, key=lambda n: (turn[n], node[n][0] & STEP[1 - turn[n] % 2])):
+        place.setdefault(name[n], start[n] - begin[turn[n]])
+
+    def lay(place):
+        key = [0.0] * len(node)
+        for n in base:
+            k = begin[turn[n]] + place[name[n]]
+            for p in pre[n]:
+                if key[p] >= k:
+                    k = key[p] + 0.01
+            key[n] = k
+        order = sorted(base, key=lambda n: key[n])
+        ends = [span(order, z) for z in times]
+        return order, sum(x / w for x, w in zip(ends, PAR["weigh"])), ends, key
+
+    now, pairs, seed = lay(place), [], 54321
+    for _ in range(PAR["polish"]):
+        seed = (seed * 1103515245 + 12345) % 2 ** 31
+        if len(pairs) < 1 or seed % 128 < 16:
+            pairs = chain(now[0], *times[(seed >> 12) % len(times)])[0]
+        p, n = pairs[(seed >> 8) % len(pairs)]
+        step, trial = (1, 1, 150, 400, 1000)[(seed >> 20) % 5], dict(place)
+        if (seed >> 27) % 2:
+            trial[name[n]] = now[3][p] - begin[turn[n]] - step
+        else:
+            trial[name[p]] = now[3][n] - begin[turn[p]] + step
+        new = lay(trial)
+        if new[1] < now[1] + PAR["slack"] * ((seed >> 16) % 16 == 0):
+            now, place, pairs = new, trial, []
+            if new[1] < best[1]:
+                best = new
+    return best
 
 
 def rank_program(g, core, T, topo):

@@ -1,3 +1,5 @@
+import math
+import numpy as np
 from concourse.mybir import dt, AluOpType, ActivationFunctionType
 
 C = 320
@@ -12,23 +14,13 @@ SH = float(2 ** 23)
 HUGE = float(2 ** 26)
 F32, BF, U16, I32, F16 = "float32", "bfloat16", "uint16", "int32", "float16"
 Q4, U8 = "float8_e4m3fn_x4", "uint8"
-PAR = {"nv": 12,
-       "both": [(1, "a1")], "run": [1, 1], "pack": [0, 1], "low": 12, "big": False, "steps": True, "ahead": [1], "slot": True,
-       "self": [(0, z) for z in ("b0", "b1", "b3", "c1", "c2", "c3")] + [(1, z) for z in ("b0", "b1", "b2", "b3", "c0", "c1", "c2")],
-       "plain": [(0, z) for z in ("a0", "a1", "a3", "b0", "b1", "c2")] + [(1, z) for z in ("a0", "a3", "b0", "b3", "c0", "c3")],
-       "onv": [z + ["x_21", "x_31", "x_30", "kwc", "gr1"] + ["f64_%d" % k for k in range(4)]
-               for z in (["gr2", "adw1", "yec2", "x_00"], ["yec0", "frow"])],
-       "lift": {(0, "ds"): -3000, (1, "ds"): -3000, (0, "dg"): -300, (1, "dg"): -300, (1, "cl"): -700, (0, "fr"): -700, (1, "fr"): -3000,
-                (0, "y0"): -700, (1, "y0"): -700, (1, "pr"): 700, (1, "se"): -1500, (1, "cr0_"): 1500, (0, "cl9"): -700, (0, "cr1"): -4500,
-                (0, "kw"): 1500, (1, "kw"): 1500, (1, "cr1"): -1500, (0, "cr2_"): 700, (0, "x_30"): 1500, (1, "x_30"): 1500, (0, "gac11"): 1500,
-                (1, "gba01"): -1400, (0, "pbw"): -100, (0, "row"): 700, (0, "ev"): 1500, (1, "ev"): 1500, (0, "ad"): -9000,
-                (0, "seed0"): 1500, (1, "seed0"): 1500, (0, "lua"): 700, (1, "lua"): 700, (1, "cr9_"): -1400, (1, "cr4"): -1500,
-                (0, "gd"): 1500, (1, "gd"): 1500, (0, "gd2"): -1500, (1, "gd2"): -1500, (0, "or"): -700, (1, "or"): -700, (0, "fa"): -1500,
-                (0, "cl4"): -700, (0, "cb"): 1500, (1, "cb"): 1500, (0, "kro"): 700, (1, "kro"): 700},
-       "also": [{"cyc": 0.83, "wake": 130.0, "gat": 1.2, "sca": 2.5}, {"cyc": 1.2, "wake": 100.0, "gat": 2.0, "sca": 5.5}],
-       "weigh": [1.0, 0.92, 1.42],
-       "scn": 1.0, "cyc": 0.9, "tt": 1.0, "gat": 1.56, "sca": 3.8, "sfix": 0.0, "wake": 110.0, "far": 2200.0, "issue": 400.0, "first": 1500.0,
-       "tries": 300, "polish": 7000, "slack": 100.0}
+PAR = {"nv": 12, "plain": ["a0", "b0", "c0"], "flat": [1], "ahead": [1],
+       "onv": ["x_21", "x_31", "x_30", "gr1", "gr2", "f64_0", "f64_1", "f64_2", "f64_3"],
+       "lift": {"ds": -3000, "xp": -3000},
+       "cyc": 0.9, "gat": 1.56, "sca": 3.8, "wake": 110.0, "far": 2200.0, "issue": 400.0, "first": 1500.0,
+       "also": [{"cyc": 0.83, "wake": 130.0, "gat": 1.1, "sca": 2.2},
+                {"cyc": 1.24, "wake": 120.0, "gat": 2.05, "sca": 5.8, "far": 2600.0, "issue": 500.0}],
+       "weigh": [1.2, 0.9, 1.0], "moves": 32000, "heat": (150.0, 10.0), "seed": 1}
 
 
 def _sb(n, d):
@@ -44,28 +36,28 @@ SCRATCH = {
     "lq0": _sb(A, Q4), "ls0": _sb(A, U8), "lq1": _sb(A, Q4), "ls1": _sb(A, U8), "lq2": _sb(A, Q4), "ls2": _sb(A, U8),
     "pa": ("psum", [128, 512], F32), "pb": ("psum", [128, 512], F32), "pw": ("psum", [128, 2048], F32),
     "pi": _sb(32, I32), "qc": _sb(16, F32), "q16": _sb(C, F32), "meq": _sb(C, BF), "keep": _sb(C, BF),
-    "c0a": _sb(C, F32), "c0b": _sb(C + 16, BF), "c0": _sb(C, BF), "c0h": _sb(2 * C, BF), "ur16": _sb(8, U16),
-    "iot": _sb(C, F32), "t512": _sb(2 * C, F32), "rho": _sb(2 * C, F32), "rhm": _sb(2 * C, F32), "phi": _sb(C, F32), "nstep": _sb(C, BF),
-    "m16": _sb(NB, F32), "c16": _sb(NB, F32), "self2": _sb(80, F32), "selfa": _sb(NB, F32), "cwin": _sb(80, F32),
-    "kwin": _sb(40, F32), "addc": _sb(80, F32), "cl16": _sb(80, U16), "cw": _sb(32 * 16, F32), "ci": _sb(16, I32),
-    "kp": _sb(PW, BF), "cpa": _sb(2 * PW, F32),
+    "c0a": _sb(C, F32), "c0b": _sb(C + 16, BF), "c0": _sb(C, BF), "c0h": _sb(C, BF), "ur16": _sb(8, U16),
+    "iot": _sb(C, F32), "iotc": _sb(C, BF), "t512": _sb(2 * C, F32), "rho": _sb(2 * C, F32), "rhm": _sb(2 * C, F32),
+    "phi": _sb(C, F32), "nstep": _sb(C, BF), "m16": _sb(NB, F32), "c16": _sb(NB, F32), "self2": _sb(40, F32), "selfa": _sb(NB, F32),
+    "cwin": _sb(80, F32), "kwin": _sb(40, F32), "addc": _sb(80, F32), "cl16": _sb(72, U16), "cw": _sb(656, F32), "ci": _sb(16, I32),
+    "kp": _sb(PW, BF), "cpa": _sb(2 * PW, F32), "own": _sb(80, F32),
     "dm": _sb(C, F32), "hold": _sb(C, F32), "eq": _sb(C, BF), "eqs": _sb(C, BF), "cmp": _sb(15 * C, BF), "cs": _sb(NB * C, F16),
-    "sg": _sb(9 * C, BF), "junk": _sb(21 * C, BF), "acc": _sb(32, F32), "sm1": _sb(32, F32),
-    "a16": _sb(72, U16), "b16": _sb(72, U16), "o16": _sb(72, U16), "ob16": _sb(72, U16), "dsn": _sb(36, F32), "s16": _sb(72, U16), "sl16": _sb(48, U16),
+    "sg": _sb(9 * C, BF), "junk": _sb(21 * C, BF), "acc": _sb(32, F32), "sm1": _sb(32, F32), "dsn": _sb(16, F32),
+    "a16": _sb(72, U16), "b16": _sb(72, U16), "o16": _sb(72, U16), "ob16": _sb(72, U16), "s16": _sb(48, U16), "sl16": _sb(48, U16),
     "n16": _sb(240, U16), "nl16": _sb(120, U16), "p16": _sb(120, U16), "pl16": _sb(120, U16),
-    "orow": _sb(C, BF), "dg": _sb(C, F32), "dh": _sb(6 * C, F16), "pb2": _sb(4 * C, BF), "rrow": _sb(C, F32), "hf": _sb(4 * C, F16),
-    "oy16": _sb(80, U16), "krow": _sb(C, F32), "kw": _sb(120, F32), "sum16": _sb(44, U16),
-    "brow": _sb(C, F32), "kbw": _sb(40, F32), "bw16": _sb(NB, U16), "pbw": _sb(80, F32),
-    "addw": _sb(120, F32), "qv": _sb(PW, F32), "cb": _sb(PW, BF), "cab": _sb(2 * PW, F32), "pr": _sb(2 * PW, F32), "prc": _sb(PW, BF),
+    "orow": _sb(C, BF), "dg": _sb(C, F32), "dh": _sb(5 * C, F16), "rrow": _sb(C, F32), "hf": _sb(3 * C, F16),
+    "krow": _sb(C, F32), "kw": _sb(120, F32), "sum16": _sb(44, U16), "oy16": _sb(80, U16),
+    "brow": _sb(C, F32), "kbw": _sb(40, BF), "bw16": _sb(NB, U16), "pbw": _sb(80, F32),
+    "addw": _sb(120, F32), "qv": _sb(PW, BF), "cb": _sb(PW, BF), "cab": _sb(2 * PW, F32), "pr": _sb(2 * PW, F32), "prc": _sb(PW, BF),
     "mm": _sb(2 * C, BF), "ma": _sb(C, F32), "rows": _sb(2 * C, F32), "gr": _sb(2 * C, F32),
-    "gd": _sb(2 * C, F32), "seed": _sb(72, F32), "zi": _sb(120, I32), "zf": _sb(52, F32), "ev": _sb(80, F32),
-    "own": _sb(80, F32), "li": _sb(80, I32), "lj": _sb(120, I32), "pk": _sb(3 * C, F32),
-    "iotc": _sb(C, BF), "erow": _sb(C, BF), "e16": _sb(NB, U16),
-    "y0": _sb(4 * C, BF), "y1": _sb(4 * C, BF), "ye": _sb(4 * C, BF), "ga": _sb(16 * C, BF), "gb": _sb(16 * C, BF), "vw": _sb(8 * C, BF),
-    "d0": _sb(24 * C, BF), "d1": _sb(24 * C, BF), "vv": _sb(12 * C, BF), "ft": _sb(8 * A, BF), "f64": _sb(4 * A, BF), "zz": _sb(4 * C, BF), "yo": _sb(C, F32),
+    "gd": _sb(2 * C, F32), "seed": _sb(80, F32), "zi": _sb(120, I32), "zf": _sb(48, F32), "ev": _sb(80, F32),
+    "li": _sb(80, I32), "lj": _sb(120, I32), "pk": _sb(3 * C, F32), "erow": _sb(C, BF), "e16": _sb(NB, U16),
+    "xp": _sb(4 * C, BF), "y0": _sb(4 * C, BF), "y1": _sb(4 * C, BF), "ga": _sb(16 * C, BF), "gb": _sb(16 * C, BF), "vw": _sb(8 * C, BF),
+    "d0": _sb(24 * C, BF), "d1": _sb(24 * C, BF), "vv": _sb(12 * C, BF), "ft": _sb(8 * A, BF), "f64": _sb(4 * A, BF),
+    "zz": _sb(4 * C, BF), "yo": _sb(C, F32),
 }
 SEMAPHORES = (["sv", "ss", "st", "sp", "ldx", "ldz", "ldu", "ldw", "lds", "ldv", "sto", "loc", "lc00", "lc01", "lc10", "lc11"]
-              + ["r%s%d" % (k, t) for k in "aopnsf" for t in range(3)])
+              + ["r%s%d" % (k, t) for k in "aopqnsf" for t in range(3)])
 
 ADD, SUB, MUL, MAX, MIN = AluOpType.add, AluOpType.subtract, AluOpType.mult, AluOpType.max, AluOpType.min
 GE, GT, LT, EQ = AluOpType.is_ge, AluOpType.is_gt, AluOpType.is_lt, AluOpType.is_equal
@@ -86,16 +78,16 @@ def build(g, rank, T, topo):
     V, S, P, Y = g.vector, g.scalar, g.tensor, g.sync
     NV = PAR["nv"]
     NS = NB - NV
-    cyc, TB = PAR["cyc"], PAR["tt"] * C
+    cyc = PAR["cyc"]
     ops, wrote, read, arrive, side = [], {}, {}, {}, [0]
 
     def add(alts, r, w, sem=None, late=0.0, out=None):
         r, w = r.split(), w.split()
-        q = list(alts)[0] if len(alts) == 1 else "v" if w[0] in PAR["onv"][side[0]] else "s"
+        q = list(alts)[0] if len(alts) == 1 else "v" if w[0] in PAR["onv"] else "s"
         pre = set(wrote[k] for k in r + w if k in wrote)
         for k in w:
             pre.update(read.get(k, []))
-        ops.append({"alts": {q: alts[q]}, "pre": sorted(pre), "far": [k for k in r if k in arrive], "sem": sem, "late": late, "out": out,
+        ops.append({"alts": alts, "q": q, "pre": sorted(pre), "far": [k for k in r if k in arrive], "sem": sem, "late": late, "out": out,
                     "w": (side[0], w[0] if w else "")})
         for k in r:
             read.setdefault(k, []).append(len(ops) - 1)
@@ -108,6 +100,9 @@ def build(g, rank, T, topo):
 
     def pick(n):
         return 50 / cyc + n * PAR["gat"]
+
+    def spread(n):
+        return 50 / cyc + n * PAR["sca"]
 
     def ts(o, i, s1, s2, o0, o1, r, w, c=64):
         if o1 is None:
@@ -122,7 +117,7 @@ def build(g, rank, T, topo):
         vec(lambda: V.tensor_copy(o, i), r, w, c)
 
     def scan(o, a, b, o0, o1, r, w, c, first=0.0):
-        vec(lambda: V.tensor_tensor_scan(o, a, b, first, o0, o1), r, w, c * PAR["scn"])
+        vec(lambda: V.tensor_tensor_scan(o, a, b, first, o0, o1), r, w, c)
 
     def fill(o, x, w, c=64):
         vec(lambda: V.memset(o, x), "", w, c)
@@ -134,10 +129,10 @@ def build(g, rank, T, topo):
         add({"t": (lambda: P.matmul_mx(o, a, sa, b, sb, True, True), (n + 16) * 0.83)}, r, w)
 
     def act(o, i, f, r, w, n, **k):
-        add({"s": (lambda: S.activation(o, i, f, **k), PAR["sfix"] + max(64, n) * cyc + (20 if "accum_out" in k else 0))}, r, w)
+        add({"s": (lambda: S.activation(o, i, f, **k), max(64, n) * cyc + (20 if "accum_out" in k else 0))}, r, w)
 
     def lin(o, i, scale, bias, r, w, n=NB, fast=1.0):
-        add({"s": (lambda: S.activation(o, i, AF.Identity, bias=bias, scale=scale), PAR["sfix"] + max(64, n) * cyc),
+        add({"s": (lambda: S.activation(o, i, AF.Identity, bias=bias, scale=scale), max(64, n) * cyc),
              "v": (lambda: V.tensor_scalar(o, i, scale, bias, MUL, ADD), max(64, n * fast) * cyc)}, r, w)
 
     def gat(o, win, off, r, w, n=C, scale=None, bias=None):
@@ -165,9 +160,9 @@ def build(g, rank, T, topo):
     def diag(o, i, n, r, w):
         scan(o, T.c0[:, 0:n], i, ADD, MIN, r + " c0", w, n)
 
-    def diag2(k, i, r, w):
-        scan(T.dh[:, C * k:C * k + C], T.c0h[:, 0:C], i, ADD, MIN, r + " c0h", w, C / 2)
-        return T.dh[:, C * k + 15:C * k + C:16]
+    def diag2(a, n, i, r, w):
+        scan(T.dh[:, a:a + n], T.c0h[:, 0:n], i, ADD, MIN, r + " c0h", w, n / 2)
+        return T.dh[:, a + 15:a + n:16]
 
     def send(dst, src, sem, peer, engines, r, w, size, before=0):
         rid, pid, _ = topo.addr(T.cores[peer])
@@ -175,13 +170,10 @@ def build(g, rank, T, topo):
         add({"g": (lambda: g.remote_dma(dst, src, T.sem[sem], T.sem.loc, pid, rid, _mask(engines)),
                    PAR["issue"] + (0 if arrive else PAR["first"]))}, r, "", "far", PAR["far"] - PAR["issue"] + size / 150.0, (peer, w, n, sem))
         if before is not None:
-            expect(sem, w, before + n)
+            arrive[w] = (sem, before + n)
 
-    def expect(sem, w, n):
-        arrive[w] = (sem, n)
-
-    QF, SHC, Q20, Q513 = [T.qc[:, k:k + 1] for k in range(4)]
-    SHH = T.qc[:, 8:9]
+    QF, SHC, Q513 = T.qc[:, 0:1], T.qc[:, 1:2], T.qc[:, 3:4]
+    SHH, SHD = T.qc[:, 8:9], T.qc[:, 9:10]
     u8, u32 = dt.uint8, dt.uint32
     sides = [0 if rank < (rank ^ s) else 1 for s in STEP]
 
@@ -214,7 +206,7 @@ def build(g, rank, T, topo):
     fill(T.nstep[:], -KS, "nstep", C / 2)
     ts(SHC, QF, 15.0, SH, LT, MUL, "qf", "shc")
     ts(SHH, QF, 15.0, 1024.0, LT, MUL, "qf", "shh")
-    lin(Q20, QF, 20.0, 0.0, "qf", "q20")
+    lin(SHD, SHH, 1.0, -float(A), "shh", "shd")
     lin(Q513, QF, 513.0, float(OFF), "qf", "q513")
     lin(T.self2[:, 0:20], T.m16[:], 1.0, QF, "m16 qf", "selfx")
     lin(T.self2[:, 20:40], T.m16[:], 1.0, QF, "m16 qf", "selfz")
@@ -224,15 +216,13 @@ def build(g, rank, T, topo):
     act(T.keep[:], T.dm[:], AF.Sign, "dm", "keep", C)
     quant(T.uq[:], T.us[:], T.ub[:], 128, "ub", "uq")
     quant(T.vq[:], T.vs[:], T.vb[:], 128, "vb", "vq")
-    ts(T.cl16[:, 60:80], T.m16[:], 0.0625, Q20, MUL, ADD, "m16 q20", "clf")
     cp(T.urq[:].bitcast(u32), T.uq[:].bitcast(u32).indirect(T.ur16[:]), "uq ur16", "urq", pick(128))
     cp(T.urs[:], T.us[:].indirect(T.ur16[:]), "uq ur16", "urs", pick(128))
     fill(T.c0b[:, 0:1], 0.0, "c0z")
-    lin(T.c0b[:, 1:C + 1], T.meq[:], SH, 0.0, "meq", "c0b", C)
-    lin(T.eq[:], T.meq[:], HUGE, 0.0, "meq", "eq", C)
-    tt(T.c0[:], T.eq[:], T.c0b[:, 0:C], SUB, "eq c0b c0z", "c0", TB)
-    lin(T.c0h[:, 0:C], T.c0[:], 1024.0 / SH, 0.0, "c0", "c0h", C)
-    lin(T.c0h[:, C:2 * C], T.c0[:], 1024.0 / SH, 0.0, "c0", "c0i", C)
+    lin(T.c0b[:, 1:C + 1], T.meq[:], SH, 0.0, "meq", "c0b", C, 0.5)
+    lin(T.eq[:], T.meq[:], HUGE, 0.0, "meq", "eq", C, 0.5)
+    tt(T.c0[:], T.eq[:], T.c0b[:, 0:C], SUB, "eq c0b c0z", "c0", C)
+    lin(T.c0h[:], T.c0[:], 1024.0 / SH, 0.0, "c0", "c0h", C, 0.5)
     W = [T.cw[:, 16 * k:16 * k + 14] for k in range(32)]
     E = [T.cw[:, 16 * k + 14:16 * k + 16] for k in range(32)]
     ts(T.ci[:, 0:14], T.self2[:, 0:14], -10.0, 1.0 / 21.0, ADD, MUL, "selfx", "ci")
@@ -253,20 +243,21 @@ def build(g, rank, T, topo):
     tt(W[9], W[4], W[7], SUB, "W4 W7", "W9")
     act(W[10], W[9], AF.Relu, "W9", "W10", 14, bias=1.0, scale=-1.0)
     for d in sorted(set(sides)):
-        ts(T.addc[:, 20 * d:20 * d + 20], T.cwin[:, 40 * d:40 * d + 20], SHC, None, SUB, None, "cw0 cw2 shc", "ac%d" % d)
         c, b = 30 * d, 11 + 8 * d
         sg, z = (1.0, 0.0) if d == 0 else (-1.0, 19.0)
         n = ["V%d" % (b + k) for k in range(8)]
         e = ["E%d" % (b + k) for k in range(8)]
         rho, tau, far = T.rho[:, C * d:C * d + C], T.qc[:, 4 + d:5 + d], 2.0 ** 22
+        ts(T.addc[:, 20 * d:20 * d + 20], T.cwin[:, 40 * d:40 * d + 20], SHC, None, SUB, None, "cw0 cw2 shc", "ac%d" % d)
         lin(T.pbw[:, 40 * d + 20:40 * d + 40], T.cwin[:, 40 * d + 20:40 * d + 40], 1.0, 0.0, "cw1 cw3", "pbw2%d" % d)
         lin(T.addw[:, 60 * d:60 * d + 20], T.m16[:], 0.0, SHC, "m16 shc", "adw0%d" % d)
+        lin(T.qc[:, 10 + d:11 + d], SHC, 1.0, sg * A * KS, "shc", "she%d" % d)
         if d == 0:
-            lin(T.addw[:, 40:60], T.m16[:], 0.0, SHH, "m16 shh", "adw20")
-            lin(T.own[:, 0:40], T.self2[:, 0:40], 1.0, SH, "selfx selfz", "own0")
+            fill(T.dh[:, 4 * C:4 * C + 192], 0.0, "pad", 96)
+            lin(T.own[:, 0:40], T.self2[:], 1.0, SH, "selfx selfz", "own0")
         else:
             lin(T.addc[:, 60:80], T.m16[:], 0.0625, SHH, "m16 shh", "acm")
-            lin(T.own[:, 40:80], T.self2[:, 0:40], -1.0, SH + 511.0, "selfx selfz", "own1")
+            lin(T.own[:, 40:80], T.self2[:], -1.0, SH + 511.0, "selfx selfz", "own1")
         lin(tau, QF, 512.0 * sg * far, far * (OFF if d == 0 else TOP - OFF - 511), "qf", "tau%d" % d)
         lin(T.c0a[:], rho, -far, tau, "rho%d tau%d" % (d, d), "c0a", C)
         tt(T.rhm[:, C * d:C * d + C], rho, T.c0a[:], MIN, "rho%d c0a" % d, "rhm%d" % d, 2 * C)
@@ -286,11 +277,15 @@ def build(g, rank, T, topo):
         tt(E[b + 5], E[b + 2], E[b + 3], MUL, e[2] + " " + e[3], e[5])
         tt(E[b + 6], E[b + 5], E[b + 4], ADD, e[5] + " " + e[4], e[6])
         cp(T.cl16[:, c + 28:c + 30], E[b + 6], e[6], "cle%d" % d)
+        gat(T.cw[:, 512:544], T.iot[:], T.cl16[:, c + 28:c + 30], "iot cle%d" % d, "F0", 32)
+        lin(T.cw[:, 560:580], T.cw[:, 512:532], 1.0, 0.0, "F0", "F1")
+        lin(T.cw[:, 580:608], T.cw[:, 512:540], 1.0, float(PW), "F0", "F3")
+        diag(T.cw[:, 608:656], T.cw[:, 560:608], 48, "F1 F3", "F2")
+        ts(T.cl16[:, 60 + 4 * d:63 + 4 * d], T.cw[:, 623:656:16], SHC, None, ADD, None, "F2 shc", "cld%d" % d)
         gat(T.cpa[:, PW * d:PW * d + PW], T.cwin[:, 40 * d:40 * d + 40], T.cl16[:, c:c + 14], "cw0 cw1 cw2 cw3 clp%d" % d, "cpa%d" % d, PW)
     c = 30 * sides[0]
     gat(T.kp[:], T.kwin[:], T.cl16[:, c:c + 14], "kw0 kw1 clp%d" % sides[0], "kp", PW)
-
-    for low in range(2 if PAR["steps"] else 0):
+    for low in range(2):
         at, big, n = 12 * C * low, 1e29 if low else -1e29, 3 * A
         iota(T.d0[:, at:at + n], [[0, n]], 0, 0, "c0%d" % low)
         for o, i, m, w in ((T.d1[:, at:at + n], T.d0[:, at:at + n], n, "c1%d"), (T.d0[:, at:at + n:3], T.d0[:, at + 1:at + n:3], A, "c0%d")):
@@ -299,21 +294,20 @@ def build(g, rank, T, topo):
             for j, u in enumerate((T.d0, T.d1)):
                 w = "c%d%d" % (j, low)
                 dma("y", u[:, at + (n << k):at + (n << k + 1)], u[:, at:at + (n << k)], w, w, "l" + w, 256 * n << k)
-    frow, oph, bph, gh = [T.hf[:, C * k:C * k + C] for k in range(4)]
+
+    frow, bph, gh = [T.hf[:, C * k:C * k + C] for k in range(3)]
     xi = T.zi[:, 64:84]
     xall = [" ".join("x_%d%d" % (k, h) for k in range(4)) for h in range(2)]
     for t in range(3):
         peer = rank ^ STEP[t]
         d = side[0] = sides[t]
         eng = topo.engines(core, T.cores[peer])
-        half = len(eng) // 2
+        few, others = (eng[:len(eng) // 2], eng[len(eng) // 2:]) if t == 0 else (eng, eng)
         X = T.x0 if t == 0 else T.x1
         xh = ["xl0", "xl1"] if t == 0 else xall
-        xk = " ".join(xh)
         a16, b16 = T.a16[:, 24 * t:24 * t + NB], T.b16[:, 24 * t:24 * t + NB]
-        o16, ob16, ko = T.o16[:, 24 * t:24 * t + NB], T.ob16[:, 24 * t:24 * t + NB], "o%d" % t
-        nl16 = T.nl16[:, 40 * t:40 * t + 40]
-        ka, kb, kd, kdl, kn, knl = ["%s%d" % (k, t) for k in ("a", "b", "ds", "dl", "n", "nl")]
+        o16, ob16 = T.o16[:, 24 * t:24 * t + NB], T.ob16[:, 24 * t:24 * t + NB]
+        ka, kb, ko, kob, kdl, kn, knl = ["%s%d" % (k, t) for k in ("a", "b", "o", "ob", "dl", "n", "nl")]
         fq, fs, lq, ls = T["fq%d" % t], T["fs%d" % t], T["lq%d" % t], T["ls%d" % t]
         for h in (1, 0):
             quant(T.xq[:, A * h:A * h + A], T.xs[:, A * h:A * h + A], X[:, 4 * A * h:4 * A * h + 4 * A], A, xh[h], "xq%d" % h)
@@ -345,46 +339,42 @@ def build(g, rank, T, topo):
         tt(T.cs[:, C * NV + C - 1:NB * C:C], T.sm1[:, 16:16 + NS], T.acc[:, 0:NS], SUB, "sm1b " + " ".join("lt%d" % k for k in range(NS)), "aw1")
         aw, kaw = T.cs[:, C - 1:NB * C:C], "aw1 " + " ".join("cs%d" % m for m in range(NV))
         cp(a16, aw, kaw, ka)
-        few = eng[:half] if t == 0 else eng
         send(b16, a16, "ra%d" % t, peer, few, ka, kb, 5120)
 
         al, kal = (a16, ka) if d == 0 else (b16, kb)
         pl, ql, el = T.cl16[:, 30 * d:30 * d + 14], T.cl16[:, 30 * d + 14:30 * d + 28], T.cl16[:, 30 * d + 28:30 * d + 30]
-        kbw = "kbw0 kbw2"
-        scatter = 50 + C * PAR["sca"]
-        if d == 0 and PAR["slot"]:
+        gat(T.rrow[:], T.rhm[:, C * d:C * d + C], al, kal + " rhm%d" % d, "rrow")
+        gat(frow, T.phi[:], al, kal + " phi", "frow")
+        if d == 0:
             ts(T.zi[:, 96:116], aw, -9.5, 0.05, ADD, MUL, kaw, "fa")
             ts(T.kw[:, 80:100], T.zi[:, 96:116], -319.0 / 16, None, MUL, None, "fa", "fb")
             tt(T.kw[:, 100:120], T.kw[:, 80:100], aw, ADD, "fb " + kaw, "fc")
             ts(T.sum16[:, 24:44], T.kw[:, 100:120], 16.0, None, MUL, None, "fc", "fd")
-            cp(T.orow[:].indirect(T.sum16[:, 24:44]), T.iotc[:], "fd iotc", "orow", scatter)
+            cp(T.orow[:].indirect(T.sum16[:, 24:44]), T.iotc[:], "fd iotc", "orow", spread(C))
         else:
-            cp(T.orow[:].indirect(a16), T.iotc[:], ka + " iotc", "orow", scatter)
-        gat(T.rrow[:], T.rhm[:, C * d:C * d + C], al, kal + " rhm%d" % d, "rrow")
-        gat(frow, T.phi[:], al, kal + " phi", "frow")
+            cp(T.orow[:].indirect(a16), T.iotc[:], ka + " iotc", "orow", spread(C))
+        ts(o16, diag2(0, C, T.orow[:], "orow", "dg0"), SHH, float(A), ADD, ADD, "dg0 shh", ko)
         if d == 0:
-            if PAR["slot"]:
-                ts(o16, diag2(0, T.orow[:], "orow", "dg0"), SHH, float(A), ADD, ADD, "dg0 shh", ko)
-            else:
-                gat(oph, T.orow[:], T.cl16[:, 60:80], "orow clf", "oph")
-                ts(o16, diag2(0, oph, "oph", "dg0"), SHH, float(A), ADD, ADD, "dg0 shh", ko)
-            send(ob16, o16, "ro%d" % t, peer, few, ko, "ob%d" % t, 5120, None)
-            cp(T.ma[:].indirect(b16), T.rrow[:], kb + " rrow", "ma", scatter)
+            send(ob16, o16, "ro%d" % t, peer, few, ko, kob, 5120, None)
+            cp(T.ma[:].indirect(b16), T.rrow[:], kb + " rrow", "ma", spread(C))
             gat(T.brow[:], T.iot[:], b16, kb + " iot", "brow")
             osl, kosl = o16, ko
         else:
-            ts(o16, diag2(0, T.orow[:], "orow", "dg0"), SHH, float(A), ADD, ADD, "dg0 shh", ko)
+            arrive[kob] = ("ro%d" % t, len(few))
             gat(T.ma[:], T.rrow[:], o16, "rrow " + ko, "ma")
-            osl, kosl = ob16, "ob%d" % t
-            expect("ro%d" % t, kosl, len(few))
             gat(T.brow[:], T.iot[:], a16, ka + " iot", "brow")
+            osl, kosl = ob16, kob
         gat(bph, T.brow[:], osl, "brow " + kosl, "bph")
-        ends = diag2(1, bph, "bph", "dg1")
+        ends = diag2(C, C, bph, "bph", "dg1")
         ts(T.bw16[:], ends, SHH, None, ADD, None, "dg1 shh", "bw16")
-        ts(T.kbw[:, 0:20], ends, SHH, 1.0 - 2 * d, ADD, MUL, "dg1 shh", "kbw0")
+        ts(T.kbw[:, 0:20], ends, SHD, 1.0 - 2 * d, ADD, MUL, "dg1 shd", "kbw0")
         for k in range(4):
-            ts(T.oy16[:, NB * k:NB * k + NB], osl, 4.0, float(k), MUL, ADD, kosl, "oy%d" % k)
-            gat(T.y0[:, C * k:C * k + C], X[:], T.oy16[:, NB * k:NB * k + NB], xk + " oy%d" % k, "y0_%d" % k, C, 64.0 if PAR["big"] else None)
+            if d in PAR["flat"]:
+                lin(T.xp[:, C * k:C * k + C], X[:, k:4 * C:4], 1.0, 0.0, " ".join(xh) + (" aw1" if k else ""), "xp%d" % k, C, 0.5)
+                gat(T.y0[:, C * k:C * k + C], T.xp[:, C * k:C * k + C], osl, "xp%d %s" % (k, kosl), "y0_%d" % k)
+            else:
+                ts(T.oy16[:, NB * k:NB * k + NB], osl, 4.0, float(k), MUL, ADD, kosl, "oy%d" % k)
+                gat(T.y0[:, C * k:C * k + C], X[:], T.oy16[:, NB * k:NB * k + NB], " ".join(xh) + " oy%d" % k, "y0_%d" % k)
         if d in PAR["ahead"]:
             tt(T.c0a[:], T.t512[:].indirect(a16), T.iot[:], ADD, ka + " t512 iot", "c0a", 50 + 2 * C)
             ts(T.kw[:, 0:20], aw, -512.0, None, MUL, None, kaw, "kwa")
@@ -399,25 +389,22 @@ def build(g, rank, T, topo):
             lin(T.kw[:, 40:60], T.kw[:, 20:40], -512.0, 0.0, "kwb", "kwc")
             tt(T.krow[:], T.t512[:].indirect(T.sum16[:, 0:NB]), T.iot[:], ADD, "sum16 t512 iot", "krow", 50 + 2 * C)
             tt(T.kw[:, 60:80], T.kw[:, 40:60], T.self2[:, 0:20], ADD, "kwc selfx", "kwd")
-        cut = [(0, PAR["low"]), (PAR["low"], NB)]
-        (m0, m1), (k0, k1) = cut[d], cut[1 - d]
-        dk = " ".join("ds_%d" % k for k in range(m1 - m0))
-        for k in range(m1 - m0):
+        for k in range(10):
             act(T.junk[:, C * (9 + k):C * (10 + k)], T.krow[:], AF.Sign, "krow kwd", "ds_%d js%d" % (k, k), C,
-                bias=T.kw[:, 60 + m0 + k:61 + m0 + k], scale=-1.0, accum_out=T.dsn[:, k:k + 1])
-        s16, ks = T.s16[:, 24 * t:24 * t + NB], "sa%d sb%d" % (t, t)
-        mine = T.s16[:, 24 * t + m0:24 * t + m1]
-        ts(mine, T.dsn[:, 0:m1 - m0], 319.0, 0.5, ADD, MUL, dk, "sa%d" % t)
-        send(T.sl16[:, 16 * t:16 * t + m1 - m0], mine, "rs%d" % t, peer, eng[half:] if t == 0 else eng, "sa%d" % t, kdl, 2560)
-        cp(T.s16[:, 24 * t + k0:24 * t + k1], T.sl16[:, 16 * t:16 * t + k1 - k0], kdl, "sb%d" % t)
-        cp(T.erow[:].indirect(s16), frow, ks + " frow", "erow", scatter)
-        ts(T.e16[:], diag2(2, T.erow[:], "erow", "dg3"), SHH, float(A), ADD, ADD, "dg3 shh", "e16")
-        gat(T.qv[:], T.kbw[:], ql, kbw + " clq%d" % d, "qv", PW)
-        lin(T.addw[:, 60 * d + 20:60 * d + 40], T.kbw[:, 0:20], KS, SHC, "kbw0 shc", "adw1")
-        if d == 1:
-            tt(T.addw[:, 100:120], T.addc[:, 60:80], T.kbw[:, 0:20], SUB, "acm kbw0", "adw21")
+                bias=T.kw[:, 60 + 10 * d + k:61 + 10 * d + k], scale=-1.0, accum_out=T.dsn[:, k:k + 1])
+        mine, theirs = T.s16[:, 16 * t:16 * t + 10], T.sl16[:, 16 * t:16 * t + 10]
+        sums = [(mine, "sa%d" % t), (theirs, kdl)][::1 - 2 * d]
+        ts(mine, T.dsn[:, 0:10], 319.0, 0.5, ADD, MUL, " ".join("ds_%d" % k for k in range(10)), "sa%d" % t)
+        send(theirs, mine, "rs%d" % t, peer, others, "sa%d" % t, kdl, 2560)
+        cp(T.erow[:].indirect(mine), T.hf[:, A * d:A * d + A], "sa%d frow" % t, "erow0 erow", spread(A))
+        cp(T.erow[:].indirect(theirs), T.hf[:, A - A * d:C - A * d], kdl + " frow", "erow", spread(A))
+        for h in range(2):
+            ts(T.e16[:, 10 * h:10 * h + 10], diag2(2 * C + A * h, A, T.erow[:, A * h:A * h + A], "erow", "dg3%d" % h), SHH, float(A),
+               ADD, ADD, "dg3%d shh" % h, "e16%d" % h)
+        gat(T.qv[:], T.kbw[:], ql, "kbw0 kbw2 clq%d" % d, "qv", PW)
+        lin(T.addw[:, 60 * d + 20:60 * d + 40], T.kbw[:, 0:20], KS, T.qc[:, 10 + d:11 + d], "kbw0 she%d" % d, "adw1")
         tt(T.pbw[:, 40 * d:40 * d + 20], T.addw[:, 60 * d + 20:60 * d + 40], T.addc[:, 20 * d:20 * d + 20], ADD, "adw1 ac%d" % d, "pbw0")
-        tt(T.cb[:], T.kbw[:].indirect(pl), T.qv[:], LT, kbw + " qv clp%d" % d, "cb", 50 + 2 * PW)
+        tt(T.cb[:], T.kbw[:].indirect(pl), T.qv[:], LT, "kbw0 kbw2 qv clp%d" % d, "cb", pick(PW))
         tt(T.cab[:, 0:PW], T.cb[:], T.cpa[:, PW * d:PW * d + PW], MUL, "cb cpa%d" % d, "ca", 2 * PW)
         tt(T.cab[:, PW:2 * PW], T.pbw[:, 40 * d:40 * d + 40].indirect(pl), T.cb[:], MUL, "cb pbw0 pbw2%d" % d, "cbb", 50 + 2 * PW)
         scan(T.prc[:], T.kp[:], T.cb[:], MUL, ADD, "kp cb", "pr2", PW / 2)
@@ -432,108 +419,80 @@ def build(g, rank, T, topo):
         scan(along(T.mm, 1), along(T.mm), T.nstep[:], MUL, MAX, "mm nstep", "row2", C / 2, 1.0)
         scan(along(T.rows, 0), along(T.ma), along(T.ma), MAX, MAX, "ma", "row0", C)
         scan(along(T.rows, 1), T.nstep[:], along(T.ma), ADD, MAX, "ma nstep", "row1", C)
-        gat(gh, T.mm[:, C:2 * C], T.bw16[:], "row2 bw16", "gr2", C, -0.5, 0.5)
+        gat(gh, T.mm[:, C:2 * C], T.bw16[:], "row2 bw16", "gr2", C, 0.5 - d, 0.5)
         for k in range(2):
             gat(T.gr[:, C * k:C * k + C], T.rows[:, C * k:C * k + C], T.bw16[:], "row%d bw16" % k, "gr%d" % k)
             diag(T.gd[:, C * k:C * k + C], T.gr[:, C * k:C * k + C], C, "gr%d" % k, "gd%d" % k)
-        ad = 60 * d
-        tt(T.seed[:, 40:60], diag2(3, gh, "gr2", "gd2"), T.addw[:, ad + 40:ad + 60], ADD, "gd2 adw2%d" % d, "seed1")
-        tt(T.zi[:, 0:32], T.prc[:].indirect(el), T.seed[:, 40:72], ADD, "pr2 cle%d seed1" % d, "zi2", 112)
-        tt(T.seed[:, 0:40], T.gd[:, 15:2 * C:16], T.addw[:, ad:ad + 40], ADD, "gd0 gd1 adw1 adw0%d" % d, "seed0", 80)
+        ends = diag2(3 * C, C, gh, "gr2", "gd2")
+        if d == 0:
+            tt(T.zi[:, 0:32], T.prc[:].indirect(el), T.dh[:, 3 * C + 15:3 * C + 512:16], ADD, "pr2 cle0 gd2 pad", "zi2", pick(32))
+        else:
+            tt(T.addw[:, 100:120], T.addc[:, 60:80], T.kbw[:, 0:20], SUB, "acm kbw0", "adw21")
+            tt(T.seed[:, 48:68], ends, T.addw[:, 100:120], ADD, "gd2 adw21", "seed1")
+            tt(T.zi[:, 0:32], T.prc[:].indirect(el), T.seed[:, 48:80], ADD, "pr2 cle1 seed1", "zi2", pick(32))
+        tt(T.seed[:, 0:40], T.gd[:, 15:2 * C:16], T.addw[:, 60 * d:60 * d + 40], ADD, "gd0 gd1 adw1 adw0%d" % d, "seed0", 80)
         ts(xi, T.zi[:, 0:20], 1, None, AND, None, "zi2", "xi2")
+        tt(T.zf[:], T.pr[:].indirect(T.cl16[:, 60 + 4 * d:63 + 4 * d]), T.seed[:, 0:48], MAX, "pr0 pr1 cld%d seed0" % d, "zf", pick(48))
         for k in range(2):
-            tt(T.zf[:, 20 * k:20 * k + 32], T.pr[:, PW * k:PW * k + PW].indirect(el), T.seed[:, 20 * k:20 * k + 32], MAX,
-               "pr%d cle%d seed0 seed1" % (k, d), "zf", 112)
             tt(T.ev[:, 20 * k:20 * k + 20], xi, T.own[:, 40 * d:40 * d + 20], MUL, "xi2 own%d" % d, "ev%d" % k)
         tt(T.ev[:, 40:80], T.own[:, 40 * d:40 * d + 40], T.ev[:, 0:40], SUB, "ev0 ev1 own%d" % d, "ev2", 80)
         for w in range(2):
-            c = 40 * ((w + d + 1) % 2)
-            tt(T.li[:, 40 * w:40 * w + 40], T.zf[:, 0:40], T.ev[:, c:c + 40], MAX, "zf ev0 ev1 ev2" if c else "zf ev0 ev1", "li%d" % w, 80)
-        ts(T.lj[:, 0:80], T.li[:], 511, None, AND, None, "li0 li1", "lj", 80)
-        ts(T.n16[:, 80 * t:80 * t + 80], T.lj[:, 0:80], 1.0 - 2 * d, 511.0 * d, MUL, ADD, "lj", kn, 80)
-        send(nl16, T.n16[:, 80 * t:80 * t + 40], "rn%d" % t, peer, few, kn, knl, 10240)
-        p16, pl16, kp, kpl = T.p16[:, 40 * t:40 * t + 40], T.pl16[:, 40 * t:40 * t + 40], "p%d" % t, "pl%d" % t
-        if d in PAR["pack"]:
-            gat(T.pk[:, 0:C], T.iot[:], T.n16[:, 80 * t + 40:80 * t + 60], "iot " + kn, "pk0", C, 512.0)
-            tt(T.pk[:, C:2 * C], T.iot[:].indirect(T.n16[:, 80 * t + 60:80 * t + 80]), T.pk[:, 0:C], ADD, "iot pk0 " + kn, "pk1",
-               max(pick(C), 50 + 2 * TB))
-            gat(T.pk[:, 2 * C:3 * C], T.pk[:, C:2 * C], T.e16[:], "pk1 e16", "pk2")
-            diag(T.dg[:], T.pk[:, 2 * C:3 * C], C, "pk2", "dg4")
-            ts(T.zi[:, 32:52], T.dg[:, 15:C:16], SHC, None, ADD, None, "dg4 shc", "zi3")
-            ts(T.lj[:, 80:100], T.zi[:, 32:52], 9, None, AluOpType.arith_shift_right, None, "zi3", "lk0")
-            ts(T.lj[:, 100:120], T.zi[:, 32:52], 511, None, AND, None, "zi3", "lk1")
-            cp(p16, T.lj[:, 80:120], "lk0 lk1", kp)
-        else:
-            gat(T.pb2[:, 0:2 * C], T.iotc[:], T.n16[:, 80 * t + 40:80 * t + 80], "iotc " + kn, "pk0", 2 * C)
-            for k in range(2):
-                gat(T.pb2[:, C * (2 + k):C * (3 + k)], T.pb2[:, C * k:C * k + C], T.e16[:], "pk0 e16", "pk%d" % (2 + k))
-            scan(T.dh[:, 4 * C:6 * C], T.c0h[:], T.pb2[:, 2 * C:4 * C], ADD, MIN, "pk2 pk3 c0h c0i", "dg4", C)
-            ts(p16, T.dh[:, 4 * C + 15:6 * C:16], SHH, float(A), ADD, ADD, "dg4 shh", kp)
-        send(pl16, p16, "rp%d" % t, peer, eng, kp, kpl, 10240)
+            c = 40 * w
+            tt(T.li[:, c:c + 40], T.zf[:, 0:40], T.ev[:, c:c + 40], MAX, "zf ev2" if w else "zf ev0 ev1", "li%d" % w, 80)
+            ts(T.lj[:, c:c + 40], T.li[:, c:c + 40], 511, None, AND, None, "li%d" % w, "lj%d" % w)
+            ts(T.n16[:, 80 * t + c:80 * t + c + 40], T.lj[:, c:c + 40], 1.0 - 2 * d, 511.0 * d, MUL, ADD, "lj%d" % w, (kn, "l16")[w])
+        send(T.nl16[:, 40 * t:40 * t + 40], T.n16[:, 80 * t:80 * t + 40], "rn%d" % t, peer, few, kn, knl, 10240)
+        kp, kpl = ["p%d%d" % (h, t) for h in range(2)], ["pl%d%d" % (h, t) for h in range(2)]
+        gat(T.pk[:, 0:C], T.iot[:], T.n16[:, 80 * t + 40:80 * t + 60], "iot l16", "pk0", C, 512.0)
+        tt(T.pk[:, C:2 * C], T.iot[:].indirect(T.n16[:, 80 * t + 60:80 * t + 80]), T.pk[:, 0:C], ADD, "iot pk0 l16", "pk1", 50 + 2 * C)
+        for h in range(2):
+            a, b, zi = A * h, 20 * h, T.zi[:, 32 + 16 * h:42 + 16 * h]
+            p16 = T.p16[:, 40 * t + b:40 * t + b + 20]
+            gat(T.pk[:, 2 * C + a:2 * C + a + A], T.pk[:, C:2 * C], T.e16[:, 10 * h:10 * h + 10], "pk1 e16%d" % h, "pk2%d" % h, A)
+            diag(T.dg[:, a:a + A], T.pk[:, 2 * C + a:2 * C + a + A], A, "pk2%d" % h, "dg4%d" % h)
+            ts(zi, T.dg[:, a + 15:a + A:16], SHC, None, ADD, None, "dg4%d shc" % h, "zi3%d" % h)
+            ts(T.lj[:, 80 + b:90 + b], zi, 9, None, AluOpType.arith_shift_right, None, "zi3%d" % h, "lk0%d" % h)
+            ts(T.lj[:, 90 + b:100 + b], zi, 511, None, AND, None, "zi3%d" % h, "lk1%d" % h)
+            cp(p16, T.lj[:, 80 + b:100 + b], "lk0%d lk1%d" % (h, h), kp[h])
+            send(T.pl16[:, 40 * t + b:40 * t + b + 20], p16, "r%s%d" % ("pq"[h], t), peer, eng, kp[h], kpl[h], 5120)
 
-        def toggle(win, kw, lists, c, n, s, own, kown, dst, kd, last):
-            k, z, m = s[0] % 4, s[1], n // 16
-            js = PAR["run"][d]
+        def toggle(z, win, kw, lists, c, n, own, kown, dst, kd, last):
+            k, m = int(z[1]), n // 16
             top = d if z[0] == "a" else 1 - d
-            low = js == top
-            at = 3 * (C * (4 * low + k) + 16 * c)
-            d0, d1, v = T.d0[:, at:at + 3 * n], T.d1[:, at:at + 3 * n], T.vv[:, at % (12 * C):at % (12 * C) + 3 * n]
-            kc, old = " c0%d c1%d" % (low, low), ["a%d" % k] if z[0] != "a" else ["b%d" % k, "c%d" % k]
-            war = "".join(" vv" + o for o in old) + kc
-            if (d, z) in PAR["plain"] or not PAR["steps"]:
-                for j, (l, kl, a) in enumerate(lists):
-                    la, lb = [l[:, a + c + i:a + c + i + m] for i in (0, NB)]
-                    ga, o = [u[:, C * (8 * j + s[0]) + 16 * c:C * (8 * j + s[0]) + 16 * c + n] for u in (T.ga, T.gb)]
-                    gat(ga, win, la, kw + " " + kl, "ga%s%d" % (z, j), n)
-                    if (d, z) in PAR["plain"] or j != js and (d, z) not in PAR["both"]:
-                        tt(o, win.indirect(lb), ga, MAX if j == top else MIN, "%s %s ga%s%d" % (kw, kl, z, j), "gb%s%d" % (z, j),
-                           max(pick(n), 50 + TB * n / C))
-                    else:
-                        gat(o, win, lb, kw + " " + kl, "gb%s%d" % (z, j), n)
-                        tt(o, o, ga, MAX if j == top else MIN, "ga%s%d gb%s%d" % (z, j, z, j), "lu%s%d gb%s%d" % (z, j, z, j), TB * n / C)
-                lo, hi, v = [u[:, C * i + 16 * c:C * i + 16 * c + n] for u, i in ((T.gb, s[0]), (T.gb, 8 + s[0]), (T.vw, s[0]))]
-                tt(v, lo, hi, ADD, "gb%s0 gb%s1" % (z, z), "vw" + z, TB * n / C)
-                tt(dst, own, v, SUB, "vw%s %s" % (z, kown), kd, last)
+            pair = [[l[:, a + i:a + i + m] for i in (0, m)] + [kw + " " + kl] for l, kl, a in lists]
+            at = C * (k + 4 * (z[0] != "a")) + c
+            if z in PAR["plain"]:
+                for j, (la, lb, r) in enumerate(pair):
+                    ga, gb = T.ga[:, 8 * C * j + at:8 * C * j + at + n], T.gb[:, 8 * C * j + at:8 * C * j + at + n]
+                    gat(ga, win, la, r, "ga%s%d" % (z, j), n)
+                    tt(gb, win.indirect(lb), ga, MAX if j == top else MIN, "%s ga%s%d" % (r, z, j), "gb%s%d" % (z, j), pick(n))
+                tt(T.vw[:, at:at + n], T.gb[:, at:at + n], T.gb[:, 8 * C + at:8 * C + at + n], ADD, "gb%s0 gb%s1" % (z, z), "vw" + z, n)
+                tt(dst, own, T.vw[:, at:at + n], SUB, "vw%s %s" % (z, kown), kd, last)
                 return
-            l, kl, a = lists[js]
-            la, lb = [l[:, a + c + i:a + c + i + m] for i in (0, NB)]
-            gat(T.d1[:, at:at + 3 * n:3], win, la, kw + " " + kl + war, "ga%s%d" % (z, js), n)
-            gat(T.d1[:, at + 1:at + 3 * n:3], win, lb, kw + " " + kl + war, "gb%s%d" % (z, js), n, -1.0)
-            l, kl, a = lists[1 - js]
-            la, lb = [l[:, a + c + i:a + c + i + m] for i in (0, NB)]
-            r, y = kw + " " + kl, "%s%d" % (z, 1 - js)
-            ga, gb = [u[:, C * (8 * (1 - js) + s[0]) + 16 * c:C * (8 * (1 - js) + s[0]) + 16 * c + n] for u in (T.ga, T.gb)]
-            o, fold = T.d0[:, at + 2:at + 3 * n:3], MIN if low else MAX
-            gat(ga, win, la, r, "ga" + y, n)
-            if (d, z) in PAR["both"]:
-                gat(gb, win, lb, r, "gb" + y, n)
-                tt(o, gb, ga, fold, "ga%s gb%s" % (y, y) + war, "lu" + z, TB * n / C)
-            else:
-                tt(o, win.indirect(lb), ga, fold, r + " ga" + y + war, "lu" + z, max(pick(n), 50 + TB * n / C))
-            scan(v, d0, d1, SUB, MIN if low else MAX, "ga%s%d gb%s%d lu%s" % (z, js, z, js, z) + kc + "".join(" yy" + o for o in old),
-                 "vv" + z, 1.5 * n)
-            tt(dst, own, T.vv[:, at % (12 * C) + 2:at % (12 * C) + 3 * n:3], SUB, "vv%s %s" % (z, kown), kd + " yy" + z, last)
+            fold, a, b = MIN if top else MAX, 3 * (C * (4 * top + k) + c), 3 * (C * k + c)
+            old = ["a%d" % k] if z[0] != "a" else ["b%d" % k, "c%d" % k]
+            free = " c0%d c1%d" % (top, top) + "".join(" vv" + o for o in old)
+            (la, lb, r), (ra, rb, rr) = pair
+            gat(T.d1[:, a:a + 3 * n:3], win, ra, rr + free, "ga%s1" % z, n)
+            gat(T.d1[:, a + 1:a + 3 * n:3], win, rb, rr + free, "gb%s1" % z, n, -1.0)
+            gat(T.ga[:, at:at + n], win, la, r, "ga%s0" % z, n)
+            tt(T.d0[:, a + 2:a + 3 * n:3], win.indirect(lb), T.ga[:, at:at + n], fold, "%s ga%s0" % (r, z) + free, "lu" + z, pick(n))
+            scan(T.vv[:, b:b + 3 * n], T.d0[:, a:a + 3 * n], T.d1[:, a:a + 3 * n], SUB, fold,
+                 "ga%s1 gb%s1 lu%s" % (z, z, z) + "".join(" yy" + o for o in old), "vv" + z, 1.5 * n)
+            tt(dst, own, T.vv[:, b + 2:b + 3 * n:3], SUB, "vv%s %s" % (z, kown), kd + " yy" + z, last)
 
         for k in range(4):
             win = T.y0[:, C * k:C * k + C]
-            toggle(win, "y0_%d" % k, [(T.n16, kn, 80 * t), (T.nl16, knl, 40 * t)], 0, C, (k, "a%d" % k), win, "y0_%d" % k,
-                   T.y1[:, C * k:C * k + C], "y1_%d" % k, TB)
+            toggle("a%d" % k, win, "y0_%d" % k, [(T.n16, kn, 80 * t), (T.nl16, knl, 40 * t)], 0, C, win, "y0_%d" % k,
+                   T.y1[:, C * k:C * k + C], "y1_%d" % k, C)
         for h in range(2):
             for k in range(4):
-                win, own, z = T.y1[:, C * k:C * k + C], T.ye[:, C * k + A * h:C * k + A * h + A], "bc"[h] + str(k)
-                if (d, z) in PAR["self"]:
-                    gat(own, win, T.e16[:, 10 * h:10 * h + 10], "y1_%d e16" % k, "ye" + z, A)
-                    kown, last = "ye" + z, TB / 2
-                else:
-                    own, kown, last = win.indirect(T.e16[:, 10 * h:10 * h + 10]), "y1_%d e16" % k, max(pick(A), 50 + TB / 2)
-                small, ks1 = (T.ft[:, k:4 * A:4], "ft%d" % k) if h == 0 else (T.ft[:, 4 * A + A * k:5 * A + A * k], "fu%d" % k)
-                big, kb1 = (T.f64[:, A * k:A * k + A], "f64_%d" % k) if h == 0 else (T.zz[:, C * k + A:C * k + C], "zy%d" % k)
-                dst, kd = (big, kb1) if PAR["big"] else (small, ks1)
-                toggle(win, "y1_%d" % k, [(T.p16, kp, 40 * t), (T.pl16, kpl, 40 * t)], 10 * h, A, (4 + k, z), own, kown, dst, kd, last)
-                if not PAR["big"]:
-                    lin(big, small, 64.0, 0.0, ks1, kb1, A, 0.5)
-                elif h == 0:
-                    lin(small, big, 0.015625, 0.0, kb1, ks1, A, 0.5)
+                win = T.y1[:, C * k:C * k + C]
+                small, ks = (T.ft[:, k:4 * A:4], "ft%d" % k) if h == 0 else (T.ft[:, 4 * A + A * k:5 * A + A * k], "fu%d" % k)
+                big, kd = (T.f64[:, A * k:A * k + A], "f64_%d" % k) if h == 0 else (T.zz[:, C * k + A:C * k + C], "zy%d" % k)
+                toggle("bc"[h] + str(k), win, "y1_%d" % k, [(T.p16, kp[h], 40 * t + 20 * h), (T.pl16, kpl[h], 40 * t + 20 * h)], A * h, A,
+                       win.indirect(T.e16[:, 10 * h:10 * h + 10]), "y1_%d e16%d" % (k, h), small, ks, pick(A))
+                lin(big, small, 64.0, 0.0, ks, kd, A, 0.5)
             if h == 0:
                 quant(fq[:], fs[:], T.ft[:, 0:4 * A], A, "ft0 ft1 ft2 ft3", "fq%d" % t)
                 send(lq[:].bitcast(u8), fq[:].bitcast(u8), "rf%d" % t, peer, eng, "fq%d" % t, "lc%d" % t, 81920, len(eng))
@@ -544,8 +503,8 @@ def build(g, rank, T, topo):
             tt(T.zz[:, C * k:C * k + A], T.pw[:, 512 * k:512 * k + A], T.f64[:, A * k:A * k + A], ADD, "pw%d f64_%d" % (k, k), "zh%d" % k, A)
         for h in (1, 0):
             for k in range(4):
-                gat(T.x1[:, 4 * A * h + k:4 * A * h + 4 * A:4], T.zz[:, C * k:C * k + C], T.s16[:, 24 * t + 10 * h:24 * t + 10 * h + 10],
-                    "zy%d zh%d %s" % (k, k, ks), "x_%d%d" % (k, h), A, 0.015625)
+                gat(T.x1[:, 4 * A * h + k:4 * A * h + 4 * A:4], T.zz[:, C * k:C * k + C], sums[h][0],
+                    "zy%d zh%d %s" % (k, k, sums[h][1]), "x_%d%d" % (k, h), A, 0.015625)
 
     for h in (1, 0):
         quant(T.xq[:, A * h:A * h + A], T.xs[:, A * h:A * h + A], T.x1[:, 4 * A * h:4 * A * h + 4 * A], A, xall[h], "xq%d" % h)
@@ -562,43 +521,36 @@ def build(g, rank, T, topo):
 
 
 def arrange(make):
-    others, held = [], dict(PAR)
-    for change in PAR["also"]:
+    costs, lags, held = [], [], dict(PAR)
+    for change in [{}] + PAR["also"]:
         PAR.update(change)
-        ops = [o for p, _ in make() for o in p]
-        others.append(([list(o["alts"].values())[0][1] for o in ops], [o["late"] + PAR["wake"] for o in ops]))
+        progs = make()
+        costs.append([{q: z[1] for q, z in o["alts"].items()} for p, _ in progs for o in p])
+        lags.append([o["late"] + PAR["wake"] for p, _ in progs for o in p])
         PAR.update(held)
-    progs, wake = make(), PAR["wake"]
-    node, at = [], {}
-    for r, (ops, _) in enumerate(progs):
-        for i, o in enumerate(ops):
-            at[(r, i)] = len(node)
-            q = list(o["alts"])[0]
-            node.append((r, i, q, o["alts"][q][1], o["late"] + wake, o["w"]))
+    node = [(r, i, o["w"], o["q"]) for r, (p, _) in enumerate(progs) for i, o in enumerate(p)]
+    at, size, never = {z[:2]: n for n, z in enumerate(node)}, len(node), 1e18
     pre = [[at[(z[0], p)] for p in progs[z[0]][0][z[1]]["pre"]] for z in node]
     for n, z in enumerate(node):
         out = progs[z[0]][0][z[1]]["out"]
-        if out:
-            for j, o in enumerate(progs[out[0]][0]):
-                if out[1] in o["far"]:
-                    pre[at[(out[0], j)]].append(n)
+        for j, o in enumerate(progs[out[0]][0] if out else []):
+            if out[1] in o["far"]:
+                pre[at[(out[0], j)]].append(n)
     suc = [[] for _ in node]
-    for n in range(len(node)):
+    for n in range(size):
         for p in pre[n]:
             suc[p].append(n)
-
-    lane = [5 * z[0] + "vstgy".index(z[2]) for z in node]
-    took, lag, never = [z[3] for z in node], [z[4] for z in node], 1e18
+    lane, lanes = [5 * z[0] + "vstgy".index(z[3]) for z in node], 5 * len(progs)
+    took, lag = [c[z[3]] for c, z in zip(costs[0], node)], lags[0]
 
     def run(before, after, weight, back):
         left, since = [len(b) for b in before], [x if back else 0.0 for x in lag]
-        ready, free = [[] for _ in range(5 * len(progs))], [0.0] * (5 * len(progs))
-        start = [never] * len(ready)
-        for n in range(len(node)):
+        ready, free, start = [[] for _ in range(lanes)], [0.0] * lanes, [never] * lanes
+        for n in range(size):
             if not left[n]:
                 ready[lane[n]].append(n)
                 start[lane[n]] = min(start[lane[n]], since[n])
-        done, order = [0.0] * len(node), []
+        done, order = [0.0] * size, []
         for _ in node:
             t0 = min(start)
             q = start.index(t0)
@@ -615,102 +567,129 @@ def arrange(make):
                     start[lane[s]] = min(start[lane[s]], max(free[lane[s]], since[s]))
         return done, order
 
-    def span(order, times):
-        done, free, (took, lag) = [0.0] * len(node), [0.0] * (5 * len(progs)), times
-        for n in order:
-            t = free[lane[n]]
-            for p in pre[n]:
-                if done[p] > t:
-                    t = done[p]
-            free[lane[n]] = t = t + took[n]
-            done[n] = t + lag[n]
-        return max(done)
-
-    rest = run(suc, pre, run(pre, suc, [-n for n in range(len(node))], False)[0], True)[0]
-    rest = [x - 1e-3 * n for n, x in enumerate(rest)]
-    kinds = sorted(set((z[5][0], z[5][1][:k]) for z in node if z[2] in "vs" and z[1] > 110 for k in (2, 3, 5)))
-    lift, best, seed = dict(PAR["lift"]), None, 12345
-    for k in range(PAR["tries"] + 1):
-        trial = dict(lift)
-        if k:
-            seed = (seed * 1103515245 + 12345) % 2 ** 31
-            kind = kinds[(seed >> 8) % len(kinds)]
-            step = (-3000, -1500, -700, -300, 300, 700, 1500, 3000)[(seed >> 20) % 8]
-            for z in ([kind] if (seed >> 24) % 2 else [(0, kind[1]), (1, kind[1])]):
-                trial[z] = trial.get(z, 0) + step
-        by = {}
-        for z in set(z[5] for z in node):
-            by[z] = sum(trial.get(y, 0) for y in set((z[0], z[1][:j]) for j in (2, 3, 5)))
-        order = run(pre, suc, [x + by[z[5]] for x, z in zip(rest, node)], False)[1]
-        ends = [span(order, times) for times in [(took, lag)] + others]
-        end = sum(x / w for x, w in zip(ends, PAR["weigh"]))
-        if best is None or end < best[1]:
-            lift, best = trial, (order, end, ends)
-    ORDER["lift"] = lift
-    best = polish(best, node, pre, lane, [(took, lag)] + others, span)
-    return [[(node[n][1], node[n][2]) for n in best[0] if node[n][0] == r] for r in range(len(progs))], best[2]
-
-
-def polish(best, node, pre, lane, times, span):
-    def chain(order, took, lag):
-        done, free, last, why, start = [0.0] * len(node), {}, {}, [-1] * len(node), [0.0] * len(node)
-        for n in order:
-            t, w = free.get(lane[n], 0.0), last.get(lane[n], -1)
-            for p in pre[n]:
-                if done[p] > t:
-                    t, w = done[p], p
-            why[n], last[lane[n]], start[n] = w, n, t
-            free[lane[n]] = t + took[n]
-            done[n] = t + took[n] + lag[n]
-        n, pairs = done.index(max(done)), []
-        while why[n] >= 0:
-            if lane[why[n]] == lane[n] and why[n] not in pre[n]:
-                pairs.append((why[n], n))
-            n = why[n]
-        return pairs, start
-
-    base, start = best[0], chain(best[0], *times[0])[1]
-    turn, count, seen, name = [], {}, {}, []
+    rest = run(suc, pre, run(pre, suc, [-n for n in range(size)], False)[0], True)[0]
+    done, base = run(pre, suc, [x - 1e-3 * n + PAR["lift"].get(node[n][2][1][:2], 0) for n, x in enumerate(rest)], False)
+    new = {n: k for k, n in enumerate(base)}
+    start = [done[n] - took[n] for n in base]
+    turn, count, seen, name = {}, {}, {}, {}
     for n, z in enumerate(node):
-        count[z[0]] = count.get(z[0], -1) + (z[5][1] == "xq1")
-        turn.append(count[z[0]])
-        k = (z[0], turn[n], z[5], z[2])
+        count[z[0]] = turn[n] = count.get(z[0], -1) + (z[2][1] == "xq1")
+        k = (z[0], turn[n], z[2])
         seen[k] = seen.get(k, 0) + 1
-        name.append((z[5], z[2], seen[k], (0, 1, 1, 3)[turn[n]]) if turn[n] >= 0 else k + (seen[k],))
-    begin = [min(start[n] for n in base if turn[n] == t) for t in range(4)] + [0.0]
-    place = {}
-    for n in sorted(base, key=lambda n: (turn[n], node[n][0] & STEP[1 - turn[n] % 2])):
-        place.setdefault(name[n], start[n] - begin[turn[n]])
+        name[n] = (z[2], seen[k], (0, 1, 1, 3)[turn[n]]) if turn[n] >= 0 else k + (seen[k],)
+    node, lane, turn, name = [[x[n] for n in base] for x in (node, lane, turn, name)]
+    costs, lags = [[[x[n] for n in base] for x in y] for y in (costs, lags)]
+    full, pre, above = [sorted(set(new[p] for p in pre[n]), reverse=True) for n in base], [], []
+    for ps in full:
+        a, keep = 0, []
+        for p in ps:
+            if not a >> p & 1 or lags[0][p] > 1000:
+                keep.append(p)
+            a |= above[p] | 1 << p
+        above.append(a)
+        pre.append(keep)
+    begin = [min(start[n] for n in range(size) if turn[n] == t) for t in range(4)] + [0.0]
+    off, ids, place, like = [begin[t] for t in turn], {}, [], {}
+    for n in sorted(range(size), key=lambda n: (turn[n], node[n][0] & STEP[1 - turn[n] % 2])):
+        if name[n] not in ids:
+            ids[name[n]] = len(place)
+            place.append(start[n] - off[n])
+        like.setdefault(node[n][2], []).append(n)
+    ident = [ids[k] for k in name]
+    first = [size] * len(place)
+    for n in range(size - 1, -1, -1):
+        first[ident[n]] = n
+    took = [[c[z[3]] for c, z in zip(cost, node)] for cost in costs]
+    (k0, k1, k2), (l0, l1, l2), (w0, w1, w2), gap = took, lags, PAR["weigh"], 200
 
-    def lay(place):
-        key = [0.0] * len(node)
-        for n in base:
-            k = begin[turn[n]] + place[name[n]]
+    def lay(old, since, moved):
+        key = old[1][:]
+        for n in range(since, size):
+            k = off[n] + place[ident[n]]
             for p in pre[n]:
                 if key[p] >= k:
                     k = key[p] + 0.01
             key[n] = k
-        order = sorted(base, key=lambda n: key[n])
-        ends = [span(order, z) for z in times]
-        return order, sum(x / w for x, w in zip(ends, PAR["weigh"])), ends, key
+        order, was, i = np.argsort(np.array(key), kind="stable").tolist(), old[0], 0
+        while i + gap < size and order[i:i + gap] == was[i:i + gap] and not moved.intersection(order[i:i + gap]):
+            i += gap
+        d0, d1, d2 = [x[:] for x in old[4]]
+        marks = old[5][:i // gap + 1]
+        f0, f1, f2 = [x[:] for x in marks[-1]]
+        for j in range(i, size, gap):
+            for n in order[j:j + gap]:
+                q = lane[n]
+                a, b, c = f0[q], f1[q], f2[q]
+                for p in pre[n]:
+                    if d0[p] > a:
+                        a = d0[p]
+                    if d1[p] > b:
+                        b = d1[p]
+                    if d2[p] > c:
+                        c = d2[p]
+                f0[q] = a = a + k0[n]
+                f1[q] = b = b + k1[n]
+                f2[q] = c = c + k2[n]
+                d0[n], d1[n], d2[n] = a + l0[n], b + l1[n], c + l2[n]
+            marks.append((f0[:], f1[:], f2[:]))
+        ends = (max(d0), max(d1), max(d2))
+        return order, key, ends[0] / w0 + ends[1] / w1 + ends[2] / w2 + (sum(d0) + sum(d1) + sum(d2)) / size, ends, (d0, d1, d2), marks
 
-    now, pairs, seed = lay(place), [], 54321
-    for _ in range(PAR["polish"]):
-        seed = (seed * 1103515245 + 12345) % 2 ** 31
-        if len(pairs) < 1 or seed % 128 < 16:
-            pairs = chain(now[0], *times[(seed >> 12) % len(times)])[0]
-        p, n = pairs[(seed >> 8) % len(pairs)]
-        step, trial = (1, 1, 150, 400, 1000)[(seed >> 20) % 5], dict(place)
-        if (seed >> 27) % 2:
-            trial[name[n]] = now[3][p] - begin[turn[n]] - step
+    def chain(now, m):
+        done, before, last, pairs, both = now[4][m], [-1] * size, [-1] * lanes, [], []
+        for n in now[0]:
+            before[n], last[lane[n]] = last[lane[n]], n
+        n = done.index(max(done))
+        while True:
+            t = done[n] - lags[m][n] - took[m][n] - 1e-6
+            if len(costs[0][n]) > 1:
+                both.append(n)
+            w = [p for p in pre[n] if done[p] >= t]
+            if not w:
+                w = [before[n]]
+                if w[0] < 0 or done[w[0]] - lags[m][w[0]] < t:
+                    return pairs, both
+                pairs.append((w[0], n))
+            n = w[-1]
+
+    def swap(calls):
+        for n in calls:
+            lane[n] += 1 - 2 * (lane[n] % 5)
+            for m in range(3):
+                took[m][n] = costs[m][n]["vs"[lane[n] % 5]]
+
+    def draw(seed):
+        seed = (seed * 6364136223846793005 + 1442695040888963407) % 2 ** 64
+        return seed, (seed >> 40) / 2.0 ** 24, (seed >> 16) % 2 ** 24
+
+    zero = [0.0] * size
+    now = lay(([], zero, 0, 0, (zero, zero, zero), [([0.0] * lanes,) * 3]), 0, set())
+    best, kept, pairs, seed, (hot, cold) = now, lane[:], None, PAR["seed"], PAR["heat"]
+    for k in range(PAR["moves"]):
+        seed, u, v = draw(seed)
+        if pairs is None or u < 0.1:
+            pairs, both = chain(now, v % 3)
+        seed, u, v = draw(seed)
+        if u < 0.12 and both:
+            calls = like[node[both[v % len(both)]][2]]
+            swap(calls)
+            trial = lay(now, size, set(calls))
         else:
-            trial[name[p]] = now[3][n] - begin[turn[p]] + step
-        new = lay(trial)
-        if new[1] < now[1] + PAR["slack"] * ((seed >> 16) % 16 == 0):
-            now, place, pairs = new, trial, []
-            if new[1] < best[1]:
-                best = new
-    return best
+            p, n = pairs[v % len(pairs)]
+            step, calls = (1, 1, 1, 100, 300, 800)[v // 4096 % 6], None
+            i, x = (ident[n], now[1][p] - off[n] - step) if u < 0.56 else (ident[p], now[1][n] - off[p] + step)
+            was, place[i] = place[i], x
+            trial = lay(now, first[i], set())
+        seed, u, v = draw(seed)
+        if trial[2] - now[2] < -hot * (cold / hot) ** (k / PAR["moves"]) * math.log(u + 1e-9):
+            now, pairs = trial, None
+            if now[2] < best[2]:
+                best, kept = now, lane[:]
+        elif calls:
+            swap(calls)
+        else:
+            place[i] = was
+    return [[(node[n][1], "vstgy"[kept[n] % 5]) for n in best[0] if node[n][0] == r] for r in range(len(progs))], best[3]
 
 
 def rank_program(g, core, T, topo):

import math
import numpy as np
from concourse.mybir import dt, AluOpType, ActivationFunctionType

C = 320
A = 160
STEP = [1, 2, 1]
NB = 20
PW = 224
KS = 8192.0
OFF = 3 * 2 ** 20
TOP = 3 * 2 ** 21 + 511
SH = float(2 ** 23)
HUGE = float(2 ** 26)
F32, BF, U16, I32, F16 = "float32", "bfloat16", "uint16", "int32", "float16"
Q4, U8 = "float8_e4m3fn_x4", "uint8"
PAR = {"nv": 12, "plain": ["a0", "b0", "c0"], "flat": [1], "ahead": [1],
       "onv": ["x_21", "x_31", "x_30", "gr1", "gr2", "f64_0", "f64_1", "f64_2", "f64_3"],
       "lift": {"ds": -3000, "xp": -3000},
       "cyc": 0.9, "gat": 1.56, "sca": 3.8, "wake": 110.0, "far": 2200.0, "issue": 400.0, "first": 1500.0,
       "also": [{"cyc": 0.83, "wake": 130.0, "gat": 1.1, "sca": 2.2},
                {"cyc": 1.24, "wake": 120.0, "gat": 2.05, "sca": 5.8, "far": 2600.0, "issue": 500.0}],
       "weigh": [1.2, 0.9, 1.0], "moves": 32000, "heat": (150.0, 10.0), "seed": 1}


def _sb(n, d):
    return ("sbuf", [128, n], d)


SCRATCH = {
    "x0": _sb(4 * C, BF), "x1": _sb(4 * C, BF), "ub": _sb(512, BF), "vb": _sb(512, BF),
    "uq": _sb(128, Q4), "us": _sb(128, U8), "urq": _sb(128, Q4), "urs": _sb(128, U8),
    "vq": _sb(128, Q4), "vs": _sb(128, U8), "wq": _sb(512, Q4), "wsc": _sb(512, U8),
    "xq": _sb(C, Q4), "xs": _sb(C, U8),
    "fq0": _sb(A, Q4), "fs0": _sb(A, U8), "fq1": _sb(A, Q4), "fs1": _sb(A, U8), "fq2": _sb(A, Q4), "fs2": _sb(A, U8),
    "lq0": _sb(A, Q4), "ls0": _sb(A, U8), "lq1": _sb(A, Q4), "ls1": _sb(A, U8), "lq2": _sb(A, Q4), "ls2": _sb(A, U8),
    "pa": ("psum", [128, 512], F32), "pb": ("psum", [128, 512], F32), "pw": ("psum", [128, 2048], F32),
    "pi": _sb(32, I32), "qc": _sb(16, F32), "q16": _sb(C, F32), "meq": _sb(C, BF), "keep": _sb(C, BF),
    "c0a": _sb(C, F32), "c0b": _sb(C + 16, BF), "c0": _sb(C, BF), "c0h": _sb(C, BF), "ur16": _sb(8, U16),
    "iot": _sb(C, F32), "iotc": _sb(C, BF), "t512": _sb(2 * C, F32), "rho": _sb(2 * C, F32), "rhm": _sb(2 * C, F32),
    "phi": _sb(C, F32), "nstep": _sb(C, BF), "m16": _sb(NB, F32), "c16": _sb(NB, F32), "self2": _sb(40, F32), "selfa": _sb(NB, F32),
    "cwin": _sb(80, F32), "kwin": _sb(40, F32), "addc": _sb(80, F32), "cl16": _sb(72, U16), "cw": _sb(656, F32), "ci": _sb(16, I32),
    "kp": _sb(PW, BF), "cpa": _sb(2 * PW, F32), "own": _sb(80, F32),
    "dm": _sb(C, F32), "hold": _sb(C, F32), "eq": _sb(C, BF), "eqs": _sb(C, BF), "cmp": _sb(15 * C, BF), "cs": _sb(NB * C, F16),
    "sg": _sb(9 * C, BF), "junk": _sb(21 * C, BF), "acc": _sb(32, F32), "sm1": _sb(32, F32), "dsn": _sb(16, F32),
    "a16": _sb(72, U16), "b16": _sb(72, U16), "o16": _sb(72, U16), "ob16": _sb(72, U16), "s16": _sb(48, U16), "sl16": _sb(48, U16),
    "n16": _sb(240, U16), "nl16": _sb(120, U16), "p16": _sb(120, U16), "pl16": _sb(120, U16),
    "orow": _sb(C, BF), "dg": _sb(C, F32), "dh": _sb(5 * C, F16), "rrow": _sb(C, F32), "hf": _sb(3 * C, F16),
    "krow": _sb(C, F32), "kw": _sb(120, F32), "sum16": _sb(44, U16), "oy16": _sb(80, U16),
    "brow": _sb(C, F32), "kbw": _sb(40, BF), "bw16": _sb(NB, U16), "pbw": _sb(80, F32),
    "addw": _sb(120, F32), "qv": _sb(PW, BF), "cb": _sb(PW, BF), "cab": _sb(2 * PW, F32), "pr": _sb(2 * PW, F32), "prc": _sb(PW, BF),
    "mm": _sb(2 * C, BF), "ma": _sb(C, F32), "rows": _sb(2 * C, F32), "gr": _sb(2 * C, F32),
    "gd": _sb(2 * C, F32), "seed": _sb(80, F32), "zi": _sb(120, I32), "zf": _sb(48, F32), "ev": _sb(80, F32),
    "li": _sb(80, I32), "lj": _sb(120, I32), "pk": _sb(3 * C, F32), "erow": _sb(C, BF), "e16": _sb(NB, U16),
    "xp": _sb(4 * C, BF), "y0": _sb(4 * C, BF), "y1": _sb(4 * C, BF), "ga": _sb(16 * C, BF), "gb": _sb(16 * C, BF), "vw": _sb(8 * C, BF),
    "d0": _sb(24 * C, BF), "d1": _sb(24 * C, BF), "vv": _sb(12 * C, BF), "ft": _sb(8 * A, BF), "f64": _sb(4 * A, BF),
    "zz": _sb(4 * C, BF), "yo": _sb(C, F32),
}
SEMAPHORES = (["sv", "ss", "st", "sp", "ldx", "ldz", "ldu", "ldw", "lds", "ldv", "sto", "loc", "lc00", "lc01", "lc10", "lc11"]
              + ["r%s%d" % (k, t) for k in "aopqnsf" for t in range(3)])

ADD, SUB, MUL, MAX, MIN = AluOpType.add, AluOpType.subtract, AluOpType.mult, AluOpType.max, AluOpType.min
GE, GT, LT, EQ = AluOpType.is_ge, AluOpType.is_gt, AluOpType.is_lt, AluOpType.is_equal
AND = AluOpType.bitwise_and
AF = ActivationFunctionType
ORDER = {}


def _mask(engines):
    m = 0
    for e in engines:
        m |= 1 << e
    return m


def build(g, rank, T, topo):
    core = T.cores[rank]
    V, S, P, Y = g.vector, g.scalar, g.tensor, g.sync
    NV = PAR["nv"]
    NS = NB - NV
    cyc = PAR["cyc"]
    ops, wrote, read, arrive, side = [], {}, {}, {}, [0]

    def add(alts, r, w, sem=None, late=0.0, out=None):
        r, w = r.split(), w.split()
        q = list(alts)[0] if len(alts) == 1 else "v" if w[0] in PAR["onv"] else "s"
        pre = set(wrote[k] for k in r + w if k in wrote)
        for k in w:
            pre.update(read.get(k, []))
        ops.append({"alts": alts, "q": q, "pre": sorted(pre), "far": [k for k in r if k in arrive], "sem": sem, "late": late, "out": out,
                    "w": (side[0], w[0] if w else "")})
        for k in r:
            read.setdefault(k, []).append(len(ops) - 1)
        for k in w:
            wrote[k] = len(ops) - 1
            read[k] = []

    def vec(make, r, w, c):
        add({"v": (make, max(64, c) * cyc)}, r, w)

    def pick(n):
        return 50 / cyc + n * PAR["gat"]

    def spread(n):
        return 50 / cyc + n * PAR["sca"]

    def ts(o, i, s1, s2, o0, o1, r, w, c=64):
        if o1 is None:
            vec(lambda: V.tensor_scalar(o, i, s1, None, o0), r, w, c)
        else:
            vec(lambda: V.tensor_scalar(o, i, s1, s2, o0, o1), r, w, c)

    def tt(o, a, b, o0, r, w, c=64):
        vec(lambda: V.tensor_tensor(o, a, b, o0), r, w, c)

    def cp(o, i, r, w, c=64):
        vec(lambda: V.tensor_copy(o, i), r, w, c)

    def scan(o, a, b, o0, o1, r, w, c, first=0.0):
        vec(lambda: V.tensor_tensor_scan(o, a, b, first, o0, o1), r, w, c)

    def fill(o, x, w, c=64):
        vec(lambda: V.memset(o, x), "", w, c)

    def quant(o, s, i, n, r, w):
        add({"v": (lambda: V.quantize_mx(o, s, i), 12 + 1.1 * n)}, r, w)

    def mm(o, a, sa, b, sb, n, r, w):
        add({"t": (lambda: P.matmul_mx(o, a, sa, b, sb, True, True), (n + 16) * 0.83)}, r, w)

    def act(o, i, f, r, w, n, **k):
        add({"s": (lambda: S.activation(o, i, f, **k), max(64, n) * cyc + (20 if "accum_out" in k else 0))}, r, w)

    def lin(o, i, scale, bias, r, w, n=NB, fast=1.0):
        add({"s": (lambda: S.activation(o, i, AF.Identity, bias=bias, scale=scale), max(64, n) * cyc),
             "v": (lambda: V.tensor_scalar(o, i, scale, bias, MUL, ADD), max(64, n * fast) * cyc)}, r, w)

    def gat(o, win, off, r, w, n=C, scale=None, bias=None):
        i = win.indirect(off)
        if scale is None:
            alts = {"s": lambda: S.activation(o, i, AF.Copy), "v": lambda: V.tensor_copy(o, i)}
        elif bias is not None:
            alts = {"s": lambda: S.activation(o, i, AF.Identity, bias=bias, scale=scale), "v": lambda: V.tensor_scalar(o, i, scale, bias, MUL, ADD)}
        else:
            alts = {"s": lambda: S.activation(o, i, AF.Copy, scale=scale), "v": lambda: V.tensor_scalar(o, i, scale, None, MUL)}
        add({"s": (alts["s"], pick(n) * cyc + 15), "v": (alts["v"], pick(n) * cyc)}, r, w)

    def iota(o, pat, base, cm, w, flt=True):
        n = 1
        for z in pat:
            n *= z[1]
        if flt:
            add({"g": (lambda: g.iota(o, pat, base, cm, allow_small_or_imprecise_dtypes=True), 130 + 2 * n * cyc)}, "", w)
        else:
            add({"g": (lambda: g.iota(o, pat, base, cm), 130 + 2 * n * cyc)}, "", w)

    def dma(q, o, i, r, w, sem, size):
        add({q: (lambda: {"s": S, "y": Y}[q].dma_start(o, i), 100.0)}, r, w, sem, 1800 + size / 150.0)

    def diag(o, i, n, r, w):
        scan(o, T.c0[:, 0:n], i, ADD, MIN, r + " c0", w, n)

    def diag2(a, n, i, r, w):
        scan(T.dh[:, a:a + n], T.c0h[:, 0:n], i, ADD, MIN, r + " c0h", w, n / 2)
        return T.dh[:, a + 15:a + n:16]

    def send(dst, src, sem, peer, engines, r, w, size, before=0):
        rid, pid, _ = topo.addr(T.cores[peer])
        n = len(engines)
        add({"g": (lambda: g.remote_dma(dst, src, T.sem[sem], T.sem.loc, pid, rid, _mask(engines)),
                   PAR["issue"] + (0 if arrive else PAR["first"]))}, r, "", "far", PAR["far"] - PAR["issue"] + size / 150.0, (peer, w, n, sem))
        if before is not None:
            arrive[w] = (sem, before + n)

    QF, SHC, Q513 = T.qc[:, 0:1], T.qc[:, 1:2], T.qc[:, 3:4]
    SHH, SHD = T.qc[:, 8:9], T.qc[:, 9:10]
    u8, u32 = dt.uint8, dt.uint32
    sides = [0 if rank < (rank ^ s) else 1 for s in STEP]

    dma("s", T.ub[:], T.u[:], "", "ub", "ldu", 131072)
    dma("y", T.x0[:, 4 * A:4 * C], T.x[:, 4 * A:4 * C], "", "xl1", "ldx", 294912)
    dma("y", T.x0[:, 0:4 * A], T.x[:, 0:4 * A], "", "xl0", "ldz", 458752)
    dma("y", T.wq[:].bitcast(u8), T.wc[:], "xl0", "wq", "ldw", 262144)
    dma("y", T.wsc[:], T.ws[:], "xl0", "wsc", "lds", 65536)
    dma("y", T.vb[:], T.v[:], "xl0", "vb", "ldv", 131072)
    iota(T.pi[:, 0:1], [[0, 1]], 0, 1, "pi0", False)
    iota(T.pi[:, 8:16], [[16, 8]], 0, 0, "pi8", False)
    iota(T.m16[:], [[16, NB]], 0, 0, "m16")
    iota(T.q16[:], [[0, NB], [1, 16]], 0, 0, "q16")
    iota(T.iot[:], [[1, C]], 0, 0, "iot")
    if 0 in sides:
        iota(T.rho[:, 0:C], [[513, 16], [16, NB]], OFF, 0, "rho0")
    if 1 in sides:
        iota(T.rho[:, C:2 * C], [[-513, 16], [-16, NB]], TOP - OFF, 0, "rho1")
    iota(T.phi[:], [[1, 16], [16, NB]], -A, 0, "phi")
    iota(T.iotc[:], [[1, C]], -A, 0, "iotc")
    iota(T.t512[:], [[-512, 2 * C]], 0, 0, "t512")
    ts(T.pi[:, 16:17], T.pi[:, 0:1], 15, None, AND, None, "pi0", "pj")
    fill(T.acc[:], 0.0, "lt gt")
    cp(QF, T.pi[:, 16:17], "pj", "qf")
    cp(T.ur16[:], T.pi[:, 8:16], "pi8", "ur16")
    fill(T.kwin[:, 0:20], 1.0, "kw0")
    fill(T.kwin[:, 20:40], 0.0, "kw1")
    fill(T.kbw[:, 20:40], -1000.0, "kbw2")
    fill(T.seed[:], 0.0, "seed0 seed1")
    fill(T.nstep[:], -KS, "nstep", C / 2)
    ts(SHC, QF, 15.0, SH, LT, MUL, "qf", "shc")
    ts(SHH, QF, 15.0, 1024.0, LT, MUL, "qf", "shh")
    lin(SHD, SHH, 1.0, -float(A), "shh", "shd")
    lin(Q513, QF, 513.0, float(OFF), "qf", "q513")
    lin(T.self2[:, 0:20], T.m16[:], 1.0, QF, "m16 qf", "selfx")
    lin(T.self2[:, 20:40], T.m16[:], 1.0, QF, "m16 qf", "selfz")
    lin(T.c16[:], T.m16[:], 1.0, 16.0, "m16", "c16")
    act(T.dm[:], T.q16[:], AF.Abs, "q16 qf", "dm", C, bias=QF, scale=-1.0)
    act(T.meq[:], T.dm[:], AF.Relu, "dm", "meq", C, bias=1.0, scale=-1.0)
    act(T.keep[:], T.dm[:], AF.Sign, "dm", "keep", C)
    quant(T.uq[:], T.us[:], T.ub[:], 128, "ub", "uq")
    quant(T.vq[:], T.vs[:], T.vb[:], 128, "vb", "vq")
    cp(T.urq[:].bitcast(u32), T.uq[:].bitcast(u32).indirect(T.ur16[:]), "uq ur16", "urq", pick(128))
    cp(T.urs[:], T.us[:].indirect(T.ur16[:]), "uq ur16", "urs", pick(128))
    fill(T.c0b[:, 0:1], 0.0, "c0z")
    lin(T.c0b[:, 1:C + 1], T.meq[:], SH, 0.0, "meq", "c0b", C, 0.5)
    lin(T.eq[:], T.meq[:], HUGE, 0.0, "meq", "eq", C, 0.5)
    tt(T.c0[:], T.eq[:], T.c0b[:, 0:C], SUB, "eq c0b c0z", "c0", C)
    lin(T.c0h[:], T.c0[:], 1024.0 / SH, 0.0, "c0", "c0h", C, 0.5)
    W = [T.cw[:, 16 * k:16 * k + 14] for k in range(32)]
    E = [T.cw[:, 16 * k + 14:16 * k + 16] for k in range(32)]
    ts(T.ci[:, 0:14], T.self2[:, 0:14], -10.0, 1.0 / 21.0, ADD, MUL, "selfx", "ci")
    lin(T.selfa[:], T.self2[:, 0:20], -1.0, 511.0, "selfx", "selfa")
    cp(W[0], T.ci[:, 0:14], "ci", "W0")
    lin(T.cwin[:, 0:20], T.m16[:], 1.0, Q513, "m16 q513", "cw0")
    lin(W[1], W[0], -21.0, 0.0, "W0", "W1")
    lin(W[2], W[0], -2.0, 19.0, "W0", "W2")
    lin(W[3], W[0], 1.0, 1.0, "W0", "W3")
    tt(W[4], W[1], T.self2[:, 0:14], ADD, "W1 selfx", "W4")
    lin(T.cwin[:, 20:40], T.self2[:, 0:20], 1.0, float(OFF - 512), "selfx", "cw1")
    tt(W[5], W[4], W[3], GE, "W4 W3", "W5")
    lin(T.cwin[:, 60:80], T.selfa[:], 1.0, 51200.0, "selfa", "cw3")
    tt(W[6], W[5], W[2], MUL, "W5 W2", "W6")
    tt(W[7], W[5], W[3], MUL, "W5 W3", "W7")
    lin(T.cwin[:, 40:60], T.cwin[:, 0:20], -1.0, float(TOP), "cw0", "cw2")
    tt(W[8], W[6], W[0], ADD, "W6 W0", "W8")
    tt(W[9], W[4], W[7], SUB, "W4 W7", "W9")
    act(W[10], W[9], AF.Relu, "W9", "W10", 14, bias=1.0, scale=-1.0)
    for d in sorted(set(sides)):
        c, b = 30 * d, 11 + 8 * d
        sg, z = (1.0, 0.0) if d == 0 else (-1.0, 19.0)
        n = ["V%d" % (b + k) for k in range(8)]
        e = ["E%d" % (b + k) for k in range(8)]
        rho, tau, far = T.rho[:, C * d:C * d + C], T.qc[:, 4 + d:5 + d], 2.0 ** 22
        ts(T.addc[:, 20 * d:20 * d + 20], T.cwin[:, 40 * d:40 * d + 20], SHC, None, SUB, None, "cw0 cw2 shc", "ac%d" % d)
        lin(T.pbw[:, 40 * d + 20:40 * d + 40], T.cwin[:, 40 * d + 20:40 * d + 40], 1.0, 0.0, "cw1 cw3", "pbw2%d" % d)
        lin(T.addw[:, 60 * d:60 * d + 20], T.m16[:], 0.0, SHC, "m16 shc", "adw0%d" % d)
        lin(T.qc[:, 10 + d:11 + d], SHC, 1.0, sg * A * KS, "shc", "she%d" % d)
        if d == 0:
            fill(T.dh[:, 4 * C:4 * C + 192], 0.0, "pad", 96)
            lin(T.own[:, 0:40], T.self2[:], 1.0, SH, "selfx selfz", "own0")
        else:
            lin(T.addc[:, 60:80], T.m16[:], 0.0625, SHH, "m16 shh", "acm")
            lin(T.own[:, 40:80], T.self2[:], -1.0, SH + 511.0, "selfx selfz", "own1")
        lin(tau, QF, 512.0 * sg * far, far * (OFF if d == 0 else TOP - OFF - 511), "qf", "tau%d" % d)
        lin(T.c0a[:], rho, -far, tau, "rho%d tau%d" % (d, d), "c0a", C)
        tt(T.rhm[:, C * d:C * d + C], rho, T.c0a[:], MIN, "rho%d c0a" % d, "rhm%d" % d, 2 * C)
        lin(W[b], W[8], sg, z, "W8", n[0])
        lin(W[b + 1], W[9], sg, z - sg, "W9", n[1])
        cp(T.cl16[:, c + 14:c + 28], W[b], n[0], "clq%d" % d)
        tt(W[b + 2], W[b], W[b + 1], SUB, n[0] + " " + n[1], n[2])
        lin(W[b + 3], W[b + 2], 1.0, 20.0, n[2], n[3])
        tt(W[b + 4], W[b + 3], W[10], MUL, n[3] + " W10", n[4])
        tt(W[b + 5], W[b + 4], W[b + 1], ADD, n[4] + " " + n[1], n[5])
        cp(T.cl16[:, c:c + 14], W[b + 5], n[5], "clp%d" % d)
        ts(E[b], T.self2[:, 0:2], 19.0, sg, MIN, MUL, "selfx", e[0])
        lin(E[b + 1], E[b], 1.0, z, e[0], e[1])
        ts(E[b + 2], E[b + 1], 9.5, None, GT, None, e[1], e[2])
        lin(E[b + 3], E[b + 1], -43.0, 419.0, e[1], e[3])
        lin(E[b + 4], E[b + 1], 22.0, 0.0, e[1], e[4])
        tt(E[b + 5], E[b + 2], E[b + 3], MUL, e[2] + " " + e[3], e[5])
        tt(E[b + 6], E[b + 5], E[b + 4], ADD, e[5] + " " + e[4], e[6])
        cp(T.cl16[:, c + 28:c + 30], E[b + 6], e[6], "cle%d" % d)
        gat(T.cw[:, 512:544], T.iot[:], T.cl16[:, c + 28:c + 30], "iot cle%d" % d, "F0", 32)
        lin(T.cw[:, 560:580], T.cw[:, 512:532], 1.0, 0.0, "F0", "F1")
        lin(T.cw[:, 580:608], T.cw[:, 512:540], 1.0, float(PW), "F0", "F3")
        diag(T.cw[:, 608:656], T.cw[:, 560:608], 48, "F1 F3", "F2")
        ts(T.cl16[:, 60 + 4 * d:63 + 4 * d], T.cw[:, 623:656:16], SHC, None, ADD, None, "F2 shc", "cld%d" % d)
        gat(T.cpa[:, PW * d:PW * d + PW], T.cwin[:, 40 * d:40 * d + 40], T.cl16[:, c:c + 14], "cw0 cw1 cw2 cw3 clp%d" % d, "cpa%d" % d, PW)
    c = 30 * sides[0]
    gat(T.kp[:], T.kwin[:], T.cl16[:, c:c + 14], "kw0 kw1 clp%d" % sides[0], "kp", PW)
    for low in range(2):
        at, big, n = 12 * C * low, 1e29 if low else -1e29, 3 * A
        iota(T.d0[:, at:at + n], [[0, n]], 0, 0, "c0%d" % low)
        for o, i, m, w in ((T.d1[:, at:at + n], T.d0[:, at:at + n], n, "c1%d"), (T.d0[:, at:at + n:3], T.d0[:, at + 1:at + n:3], A, "c0%d")):
            add({"g": (lambda o=o, i=i, m=m, big=big: g.affine_select(o, i, [[0, m]], GT, big, 0, 0), 170 + 2 * m * cyc)}, "c0%d" % low, w % low)
        for k in range(3):
            for j, u in enumerate((T.d0, T.d1)):
                w = "c%d%d" % (j, low)
                dma("y", u[:, at + (n << k):at + (n << k + 1)], u[:, at:at + (n << k)], w, w, "l" + w, 256 * n << k)

    frow, bph, gh = [T.hf[:, C * k:C * k + C] for k in range(3)]
    xi = T.zi[:, 64:84]
    xall = [" ".join("x_%d%d" % (k, h) for k in range(4)) for h in range(2)]
    for t in range(3):
        peer = rank ^ STEP[t]
        d = side[0] = sides[t]
        eng = topo.engines(core, T.cores[peer])
        few, others = (eng[:len(eng) // 2], eng[len(eng) // 2:]) if t == 0 else (eng, eng)
        X = T.x0 if t == 0 else T.x1
        xh = ["xl0", "xl1"] if t == 0 else xall
        a16, b16 = T.a16[:, 24 * t:24 * t + NB], T.b16[:, 24 * t:24 * t + NB]
        o16, ob16 = T.o16[:, 24 * t:24 * t + NB], T.ob16[:, 24 * t:24 * t + NB]
        ka, kb, ko, kob, kdl, kn, knl = ["%s%d" % (k, t) for k in ("a", "b", "o", "ob", "dl", "n", "nl")]
        fq, fs, lq, ls = T["fq%d" % t], T["fs%d" % t], T["lq%d" % t], T["ls%d" % t]
        for h in (1, 0):
            quant(T.xq[:, A * h:A * h + A], T.xs[:, A * h:A * h + A], X[:, 4 * A * h:4 * A * h + 4 * A], A, xh[h], "xq%d" % h)
        mm(T.pw[:, 0:A], T.urq[:], T.urs[:], T.xq[:, A:C], T.xs[:, A:C], A, "urq urs xq1", "pw0")
        mm(T.pb[:, 0:C], T.urq[:], T.urs[:], T.xq[:], T.xs[:], C, "urq urs xq0 xq1", "pb")
        mm(T.pa[:, 0:C], T.urq[:], T.urs[:], T.xq[:], T.xs[:], C, "urq urs xq0 xq1", "pa")
        for h, s, ks in ((1, T.pw[:, 0:A], "pw0"), (0, T.pa[:, 0:A], "pa")):
            a, b = A * h, A * h + A
            tt(T.dm[:, a:b], s, T.meq[:, a:b], MUL, ks + " meq keep", "dm%d" % h, A)
            scan(T.hold[:, a:b], T.keep[:, a:b], T.dm[:, a:b], MUL, ADD, "keep dm%d" % h, "hold%d" % h, A)
            tt(T.eq[:, a:b], s, T.hold[:, a:b], EQ, ks + " hold%d c0" % h, "eq%d" % h, A)
            scan(T.eqs[:, a:b], T.keep[:, a:b], T.eq[:, a:b], MUL, SUB, "keep eq%d" % h, "eqs%d" % h, A / 2)
        for k in range(NS):
            n = 16 * (NV + k) + 16
            act(T.sg[:, C * k:C * k + C], T.pb[:, 0:C], AF.Sign, "pb hold1", "sg%d" % k, C, bias=T.hold[:, n - 1:n], scale=-1.0)
            act(T.junk[:, C * k:C * k + n], T.sg[:, C * k:C * k + n], AF.Relu, "sg%d lt" % k, "lt%d jk%d" % (k, k), n, accum_out=T.acc[:, k:k + 1])
            if n < C:
                act(T.junk[:, C * k + n:C * k + C], T.sg[:, C * k + n:C * k + C], AF.Relu, "sg%d gt" % k, "gt%d jr%d" % (k, k), C - n,
                    scale=-1.0, accum_out=T.acc[:, 16 + k:17 + k])
        for m in range(NV - 1, -1, -1):
            n = 16 * m + 16
            sc, r = T.hold[:, n - 1:n], "pa hold%d" % (m // 10)
            ts(T.cmp[:, C * m:C * m + n], T.pa[:, 0:n], sc, None, GE, None, r, "cl%d_" % m, n)
            ts(T.cmp[:, C * m + n:C * m + C], T.pa[:, n:C], sc, None, GT, None, r, "cr%d_" % m, C - n)
            scan(T.cs[:, C * m + A:C * m + C], T.cmp[:, C * m:C * m + A], T.cmp[:, C * m + A:C * m + C], ADD, ADD,
                 "cl%d_ cr%d_ eqs%d" % (m, m, m // 10), "cs%d" % m, C / 4, T.eqs[:, n - 1:n])
        tt(T.sm1[:, 0:NS], T.c16[:, NV:NB], T.eqs[:, 16 * NV + 15:C:16], ADD, "c16 eqs1", "sm1a")
        tt(T.sm1[:, 16:16 + NS], T.acc[:, 16:16 + NS], T.sm1[:, 0:NS], ADD, "sm1a gt " + " ".join("gt%d" % k for k in range(NS - 1)), "sm1b")
        tt(T.cs[:, C * NV + C - 1:NB * C:C], T.sm1[:, 16:16 + NS], T.acc[:, 0:NS], SUB, "sm1b " + " ".join("lt%d" % k for k in range(NS)), "aw1")
        aw, kaw = T.cs[:, C - 1:NB * C:C], "aw1 " + " ".join("cs%d" % m for m in range(NV))
        cp(a16, aw, kaw, ka)
        send(b16, a16, "ra%d" % t, peer, few, ka, kb, 5120)

        al, kal = (a16, ka) if d == 0 else (b16, kb)
        pl, ql, el = T.cl16[:, 30 * d:30 * d + 14], T.cl16[:, 30 * d + 14:30 * d + 28], T.cl16[:, 30 * d + 28:30 * d + 30]
        gat(T.rrow[:], T.rhm[:, C * d:C * d + C], al, kal + " rhm%d" % d, "rrow")
        gat(frow, T.phi[:], al, kal + " phi", "frow")
        if d == 0:
            ts(T.zi[:, 96:116], aw, -9.5, 0.05, ADD, MUL, kaw, "fa")
            ts(T.kw[:, 80:100], T.zi[:, 96:116], -319.0 / 16, None, MUL, None, "fa", "fb")
            tt(T.kw[:, 100:120], T.kw[:, 80:100], aw, ADD, "fb " + kaw, "fc")
            ts(T.sum16[:, 24:44], T.kw[:, 100:120], 16.0, None, MUL, None, "fc", "fd")
            cp(T.orow[:].indirect(T.sum16[:, 24:44]), T.iotc[:], "fd iotc", "orow", spread(C))
        else:
            cp(T.orow[:].indirect(a16), T.iotc[:], ka + " iotc", "orow", spread(C))
        ts(o16, diag2(0, C, T.orow[:], "orow", "dg0"), SHH, float(A), ADD, ADD, "dg0 shh", ko)
        if d == 0:
            send(ob16, o16, "ro%d" % t, peer, few, ko, kob, 5120, None)
            cp(T.ma[:].indirect(b16), T.rrow[:], kb + " rrow", "ma", spread(C))
            gat(T.brow[:], T.iot[:], b16, kb + " iot", "brow")
            osl, kosl = o16, ko
        else:
            arrive[kob] = ("ro%d" % t, len(few))
            gat(T.ma[:], T.rrow[:], o16, "rrow " + ko, "ma")
            gat(T.brow[:], T.iot[:], a16, ka + " iot", "brow")
            osl, kosl = ob16, kob
        gat(bph, T.brow[:], osl, "brow " + kosl, "bph")
        ends = diag2(C, C, bph, "bph", "dg1")
        ts(T.bw16[:], ends, SHH, None, ADD, None, "dg1 shh", "bw16")
        ts(T.kbw[:, 0:20], ends, SHD, 1.0 - 2 * d, ADD, MUL, "dg1 shd", "kbw0")
        for k in range(4):
            if d in PAR["flat"]:
                lin(T.xp[:, C * k:C * k + C], X[:, k:4 * C:4], 1.0, 0.0, " ".join(xh) + (" aw1" if k else ""), "xp%d" % k, C, 0.5)
                gat(T.y0[:, C * k:C * k + C], T.xp[:, C * k:C * k + C], osl, "xp%d %s" % (k, kosl), "y0_%d" % k)
            else:
                ts(T.oy16[:, NB * k:NB * k + NB], osl, 4.0, float(k), MUL, ADD, kosl, "oy%d" % k)
                gat(T.y0[:, C * k:C * k + C], X[:], T.oy16[:, NB * k:NB * k + NB], " ".join(xh) + " oy%d" % k, "y0_%d" % k)
        if d in PAR["ahead"]:
            tt(T.c0a[:], T.t512[:].indirect(a16), T.iot[:], ADD, ka + " t512 iot", "c0a", 50 + 2 * C)
            ts(T.kw[:, 0:20], aw, -512.0, None, MUL, None, kaw, "kwa")
            tt(T.kw[:, 20:40], T.kw[:, 0:20], T.self2[:, 0:20], ADD, "kwa selfx", "kwb")
            tt(T.krow[:], T.t512[:].indirect(b16), T.c0a[:], ADD, kb + " t512 c0a", "krow", 50 + 2 * C)
            ts(T.kw[:, 40:60], b16, -512.0, None, MUL, None, kb, "kwc")
            tt(T.kw[:, 60:80], T.kw[:, 40:60], T.kw[:, 20:40], ADD, "kwc kwb", "kwd")
        else:
            ts(T.kw[:, 0:20], b16, 0.0, None, ADD, None, kb, "kwa")
            tt(T.kw[:, 20:40], T.kw[:, 0:20], aw, ADD, "kwa " + kaw, "kwb")
            cp(T.sum16[:, 0:NB], T.kw[:, 20:40], "kwb", "sum16")
            lin(T.kw[:, 40:60], T.kw[:, 20:40], -512.0, 0.0, "kwb", "kwc")
            tt(T.krow[:], T.t512[:].indirect(T.sum16[:, 0:NB]), T.iot[:], ADD, "sum16 t512 iot", "krow", 50 + 2 * C)
            tt(T.kw[:, 60:80], T.kw[:, 40:60], T.self2[:, 0:20], ADD, "kwc selfx", "kwd")
        for k in range(10):
            act(T.junk[:, C * (9 + k):C * (10 + k)], T.krow[:], AF.Sign, "krow kwd", "ds_%d js%d" % (k, k), C,
                bias=T.kw[:, 60 + 10 * d + k:61 + 10 * d + k], scale=-1.0, accum_out=T.dsn[:, k:k + 1])
        mine, theirs = T.s16[:, 16 * t:16 * t + 10], T.sl16[:, 16 * t:16 * t + 10]
        sums = [(mine, "sa%d" % t), (theirs, kdl)][::1 - 2 * d]
        ts(mine, T.dsn[:, 0:10], 319.0, 0.5, ADD, MUL, " ".join("ds_%d" % k for k in range(10)), "sa%d" % t)
        send(theirs, mine, "rs%d" % t, peer, others, "sa%d" % t, kdl, 2560)
        cp(T.erow[:].indirect(mine), T.hf[:, A * d:A * d + A], "sa%d frow" % t, "erow0 erow", spread(A))
        cp(T.erow[:].indirect(theirs), T.hf[:, A - A * d:C - A * d], kdl + " frow", "erow", spread(A))
        for h in range(2):
            ts(T.e16[:, 10 * h:10 * h + 10], diag2(2 * C + A * h, A, T.erow[:, A * h:A * h + A], "erow", "dg3%d" % h), SHH, float(A),
               ADD, ADD, "dg3%d shh" % h, "e16%d" % h)
        gat(T.qv[:], T.kbw[:], ql, "kbw0 kbw2 clq%d" % d, "qv", PW)
        lin(T.addw[:, 60 * d + 20:60 * d + 40], T.kbw[:, 0:20], KS, T.qc[:, 10 + d:11 + d], "kbw0 she%d" % d, "adw1")
        tt(T.pbw[:, 40 * d:40 * d + 20], T.addw[:, 60 * d + 20:60 * d + 40], T.addc[:, 20 * d:20 * d + 20], ADD, "adw1 ac%d" % d, "pbw0")
        tt(T.cb[:], T.kbw[:].indirect(pl), T.qv[:], LT, "kbw0 kbw2 qv clp%d" % d, "cb", pick(PW))
        tt(T.cab[:, 0:PW], T.cb[:], T.cpa[:, PW * d:PW * d + PW], MUL, "cb cpa%d" % d, "ca", 2 * PW)
        tt(T.cab[:, PW:2 * PW], T.pbw[:, 40 * d:40 * d + 40].indirect(pl), T.cb[:], MUL, "cb pbw0 pbw2%d" % d, "cbb", 50 + 2 * PW)
        scan(T.prc[:], T.kp[:], T.cb[:], MUL, ADD, "kp cb", "pr2", PW / 2)
        scan(T.pr[:, 0:PW], T.kp[:], T.cab[:, 0:PW], MUL, MAX, "kp ca", "pr0", PW)
        scan(T.pr[:, PW:2 * PW], T.kp[:], T.cab[:, PW:2 * PW], MUL, MAX, "kp cbb", "pr1", PW)

        def along(b, k=0):
            if d == 0:
                return b[:, C * k:C * k + C]
            return b[:, C * k + C - 1:C * k - 1:-1] if k else b[:, C - 1::-1]
        act(T.mm[:, 0:C], T.ma[:], AF.Sign, "ma", "mm", C, bias=0.5, scale=-1.0)
        scan(along(T.mm, 1), along(T.mm), T.nstep[:], MUL, MAX, "mm nstep", "row2", C / 2, 1.0)
        scan(along(T.rows, 0), along(T.ma), along(T.ma), MAX, MAX, "ma", "row0", C)
        scan(along(T.rows, 1), T.nstep[:], along(T.ma), ADD, MAX, "ma nstep", "row1", C)
        gat(gh, T.mm[:, C:2 * C], T.bw16[:], "row2 bw16", "gr2", C, 0.5 - d, 0.5)
        for k in range(2):
            gat(T.gr[:, C * k:C * k + C], T.rows[:, C * k:C * k + C], T.bw16[:], "row%d bw16" % k, "gr%d" % k)
            diag(T.gd[:, C * k:C * k + C], T.gr[:, C * k:C * k + C], C, "gr%d" % k, "gd%d" % k)
        ends = diag2(3 * C, C, gh, "gr2", "gd2")
        if d == 0:
            tt(T.zi[:, 0:32], T.prc[:].indirect(el), T.dh[:, 3 * C + 15:3 * C + 512:16], ADD, "pr2 cle0 gd2 pad", "zi2", pick(32))
        else:
            tt(T.addw[:, 100:120], T.addc[:, 60:80], T.kbw[:, 0:20], SUB, "acm kbw0", "adw21")
            tt(T.seed[:, 48:68], ends, T.addw[:, 100:120], ADD, "gd2 adw21", "seed1")
            tt(T.zi[:, 0:32], T.prc[:].indirect(el), T.seed[:, 48:80], ADD, "pr2 cle1 seed1", "zi2", pick(32))
        tt(T.seed[:, 0:40], T.gd[:, 15:2 * C:16], T.addw[:, 60 * d:60 * d + 40], ADD, "gd0 gd1 adw1 adw0%d" % d, "seed0", 80)
        ts(xi, T.zi[:, 0:20], 1, None, AND, None, "zi2", "xi2")
        tt(T.zf[:], T.pr[:].indirect(T.cl16[:, 60 + 4 * d:63 + 4 * d]), T.seed[:, 0:48], MAX, "pr0 pr1 cld%d seed0" % d, "zf", pick(48))
        for k in range(2):
            tt(T.ev[:, 20 * k:20 * k + 20], xi, T.own[:, 40 * d:40 * d + 20], MUL, "xi2 own%d" % d, "ev%d" % k)
        tt(T.ev[:, 40:80], T.own[:, 40 * d:40 * d + 40], T.ev[:, 0:40], SUB, "ev0 ev1 own%d" % d, "ev2", 80)
        for w in range(2):
            c = 40 * w
            tt(T.li[:, c:c + 40], T.zf[:, 0:40], T.ev[:, c:c + 40], MAX, "zf ev2" if w else "zf ev0 ev1", "li%d" % w, 80)
            ts(T.lj[:, c:c + 40], T.li[:, c:c + 40], 511, None, AND, None, "li%d" % w, "lj%d" % w)
            ts(T.n16[:, 80 * t + c:80 * t + c + 40], T.lj[:, c:c + 40], 1.0 - 2 * d, 511.0 * d, MUL, ADD, "lj%d" % w, (kn, "l16")[w])
        send(T.nl16[:, 40 * t:40 * t + 40], T.n16[:, 80 * t:80 * t + 40], "rn%d" % t, peer, few, kn, knl, 10240)
        kp, kpl = ["p%d%d" % (h, t) for h in range(2)], ["pl%d%d" % (h, t) for h in range(2)]
        gat(T.pk[:, 0:C], T.iot[:], T.n16[:, 80 * t + 40:80 * t + 60], "iot l16", "pk0", C, 512.0)
        tt(T.pk[:, C:2 * C], T.iot[:].indirect(T.n16[:, 80 * t + 60:80 * t + 80]), T.pk[:, 0:C], ADD, "iot pk0 l16", "pk1", 50 + 2 * C)
        for h in range(2):
            a, b, zi = A * h, 20 * h, T.zi[:, 32 + 16 * h:42 + 16 * h]
            p16 = T.p16[:, 40 * t + b:40 * t + b + 20]
            gat(T.pk[:, 2 * C + a:2 * C + a + A], T.pk[:, C:2 * C], T.e16[:, 10 * h:10 * h + 10], "pk1 e16%d" % h, "pk2%d" % h, A)
            diag(T.dg[:, a:a + A], T.pk[:, 2 * C + a:2 * C + a + A], A, "pk2%d" % h, "dg4%d" % h)
            ts(zi, T.dg[:, a + 15:a + A:16], SHC, None, ADD, None, "dg4%d shc" % h, "zi3%d" % h)
            ts(T.lj[:, 80 + b:90 + b], zi, 9, None, AluOpType.arith_shift_right, None, "zi3%d" % h, "lk0%d" % h)
            ts(T.lj[:, 90 + b:100 + b], zi, 511, None, AND, None, "zi3%d" % h, "lk1%d" % h)
            cp(p16, T.lj[:, 80 + b:100 + b], "lk0%d lk1%d" % (h, h), kp[h])
            send(T.pl16[:, 40 * t + b:40 * t + b + 20], p16, "r%s%d" % ("pq"[h], t), peer, eng, kp[h], kpl[h], 5120)

        def toggle(z, win, kw, lists, c, n, own, kown, dst, kd, last):
            k, m = int(z[1]), n // 16
            top = d if z[0] == "a" else 1 - d
            pair = [[l[:, a + i:a + i + m] for i in (0, m)] + [kw + " " + kl] for l, kl, a in lists]
            at = C * (k + 4 * (z[0] != "a")) + c
            if z in PAR["plain"]:
                for j, (la, lb, r) in enumerate(pair):
                    ga, gb = T.ga[:, 8 * C * j + at:8 * C * j + at + n], T.gb[:, 8 * C * j + at:8 * C * j + at + n]
                    gat(ga, win, la, r, "ga%s%d" % (z, j), n)
                    tt(gb, win.indirect(lb), ga, MAX if j == top else MIN, "%s ga%s%d" % (r, z, j), "gb%s%d" % (z, j), pick(n))
                tt(T.vw[:, at:at + n], T.gb[:, at:at + n], T.gb[:, 8 * C + at:8 * C + at + n], ADD, "gb%s0 gb%s1" % (z, z), "vw" + z, n)
                tt(dst, own, T.vw[:, at:at + n], SUB, "vw%s %s" % (z, kown), kd, last)
                return
            fold, a, b = MIN if top else MAX, 3 * (C * (4 * top + k) + c), 3 * (C * k + c)
            old = ["a%d" % k] if z[0] != "a" else ["b%d" % k, "c%d" % k]
            free = " c0%d c1%d" % (top, top) + "".join(" vv" + o for o in old)
            (la, lb, r), (ra, rb, rr) = pair
            gat(T.d1[:, a:a + 3 * n:3], win, ra, rr + free, "ga%s1" % z, n)
            gat(T.d1[:, a + 1:a + 3 * n:3], win, rb, rr + free, "gb%s1" % z, n, -1.0)
            gat(T.ga[:, at:at + n], win, la, r, "ga%s0" % z, n)
            tt(T.d0[:, a + 2:a + 3 * n:3], win.indirect(lb), T.ga[:, at:at + n], fold, "%s ga%s0" % (r, z) + free, "lu" + z, pick(n))
            scan(T.vv[:, b:b + 3 * n], T.d0[:, a:a + 3 * n], T.d1[:, a:a + 3 * n], SUB, fold,
                 "ga%s1 gb%s1 lu%s" % (z, z, z) + "".join(" yy" + o for o in old), "vv" + z, 1.5 * n)
            tt(dst, own, T.vv[:, b + 2:b + 3 * n:3], SUB, "vv%s %s" % (z, kown), kd + " yy" + z, last)

        for k in range(4):
            win = T.y0[:, C * k:C * k + C]
            toggle("a%d" % k, win, "y0_%d" % k, [(T.n16, kn, 80 * t), (T.nl16, knl, 40 * t)], 0, C, win, "y0_%d" % k,
                   T.y1[:, C * k:C * k + C], "y1_%d" % k, C)
        for h in range(2):
            for k in range(4):
                win = T.y1[:, C * k:C * k + C]
                small, ks = (T.ft[:, k:4 * A:4], "ft%d" % k) if h == 0 else (T.ft[:, 4 * A + A * k:5 * A + A * k], "fu%d" % k)
                big, kd = (T.f64[:, A * k:A * k + A], "f64_%d" % k) if h == 0 else (T.zz[:, C * k + A:C * k + C], "zy%d" % k)
                toggle("bc"[h] + str(k), win, "y1_%d" % k, [(T.p16, kp[h], 40 * t + 20 * h), (T.pl16, kpl[h], 40 * t + 20 * h)], A * h, A,
                       win.indirect(T.e16[:, 10 * h:10 * h + 10]), "y1_%d e16%d" % (k, h), small, ks, pick(A))
                lin(big, small, 64.0, 0.0, ks, kd, A, 0.5)
            if h == 0:
                quant(fq[:], fs[:], T.ft[:, 0:4 * A], A, "ft0 ft1 ft2 ft3", "fq%d" % t)
                send(lq[:].bitcast(u8), fq[:].bitcast(u8), "rf%d" % t, peer, eng, "fq%d" % t, "lc%d" % t, 81920, len(eng))
                send(ls[:], fs[:], "rf%d" % t, peer, eng, "fq%d" % t, "lq%d" % t, 20480, len(eng))
        for k in range(4):
            mm(T.pw[:, 512 * k:512 * k + A], T.wq[:, 128 * k:128 * k + 128], T.wsc[:, 128 * k:128 * k + 128], lq[:], ls[:], A,
               "wq wsc lc%d lq%d" % (t, t), "pw%d" % k)
            tt(T.zz[:, C * k:C * k + A], T.pw[:, 512 * k:512 * k + A], T.f64[:, A * k:A * k + A], ADD, "pw%d f64_%d" % (k, k), "zh%d" % k, A)
        for h in (1, 0):
            for k in range(4):
                gat(T.x1[:, 4 * A * h + k:4 * A * h + 4 * A:4], T.zz[:, C * k:C * k + C], sums[h][0],
                    "zy%d zh%d %s" % (k, k, sums[h][1]), "x_%d%d" % (k, h), A, 0.015625)

    for h in (1, 0):
        quant(T.xq[:, A * h:A * h + A], T.xs[:, A * h:A * h + A], T.x1[:, 4 * A * h:4 * A * h + 4 * A], A, xall[h], "xq%d" % h)
    mm(T.pb[:, 0:A], T.vq[:], T.vs[:], T.xq[:, A:C], T.xs[:, A:C], A, "vq xq1", "pb")
    mm(T.pa[:, 0:A], T.vq[:], T.vs[:], T.xq[:, 0:A], T.xs[:, 0:A], A, "vq xq0", "pa")
    dma("y", T.oc[:], T.xq[:].bitcast(u8), "xq0 xq1", "", "sto", 163840)
    for k in range(4):
        dma("ys"[k % 2], T.osc[4 * k:4 * k + 4, :], T.xs[32 * k:32 * k + 4, :], "xq0 xq1", "", "sto", 1280)
    act(T.yo[:, A:C], T.pb[:, 0:A], AF.Copy, "pb", "yo1", A)
    cp(T.yo[:, 0:A], T.pa[:, 0:A], "pa", "yo0", A)
    dma("s", T.y[:, A:C], T.yo[:, A:C], "yo1", "", "sto", 81920)
    dma("y", T.y[:, 0:A], T.yo[:, 0:A], "yo0", "", "sto", 81920)
    return ops, arrive


def arrange(make):
    costs, lags, held = [], [], dict(PAR)
    for change in [{}] + PAR["also"]:
        PAR.update(change)
        progs = make()
        costs.append([{q: z[1] for q, z in o["alts"].items()} for p, _ in progs for o in p])
        lags.append([o["late"] + PAR["wake"] for p, _ in progs for o in p])
        PAR.update(held)
    node = [(r, i, o["w"], o["q"]) for r, (p, _) in enumerate(progs) for i, o in enumerate(p)]
    at, size, never = {z[:2]: n for n, z in enumerate(node)}, len(node), 1e18
    pre = [[at[(z[0], p)] for p in progs[z[0]][0][z[1]]["pre"]] for z in node]
    for n, z in enumerate(node):
        out = progs[z[0]][0][z[1]]["out"]
        for j, o in enumerate(progs[out[0]][0] if out else []):
            if out[1] in o["far"]:
                pre[at[(out[0], j)]].append(n)
    suc = [[] for _ in node]
    for n in range(size):
        for p in pre[n]:
            suc[p].append(n)
    lane, lanes = [5 * z[0] + "vstgy".index(z[3]) for z in node], 5 * len(progs)
    took, lag = [c[z[3]] for c, z in zip(costs[0], node)], lags[0]

    def run(before, after, weight, back):
        left, since = [len(b) for b in before], [x if back else 0.0 for x in lag]
        ready, free, start = [[] for _ in range(lanes)], [0.0] * lanes, [never] * lanes
        for n in range(size):
            if not left[n]:
                ready[lane[n]].append(n)
                start[lane[n]] = min(start[lane[n]], since[n])
        done, order = [0.0] * size, []
        for _ in node:
            t0 = min(start)
            q = start.index(t0)
            n = max((z for z in ready[q] if since[z] <= t0), key=lambda z: weight[z])
            ready[q].remove(n)
            done[n] = free[q] = t = t0 + took[n]
            order.append(n)
            start[q] = max(t, min(since[z] for z in ready[q])) if ready[q] else never
            for s in after[n]:
                since[s] = max(since[s], t + (lag[s] if back else lag[n]))
                left[s] -= 1
                if not left[s]:
                    ready[lane[s]].append(s)
                    start[lane[s]] = min(start[lane[s]], max(free[lane[s]], since[s]))
        return done, order

    rest = run(suc, pre, run(pre, suc, [-n for n in range(size)], False)[0], True)[0]
    done, base = run(pre, suc, [x - 1e-3 * n + PAR["lift"].get(node[n][2][1][:2], 0) for n, x in enumerate(rest)], False)
    new = {n: k for k, n in enumerate(base)}
    start = [done[n] - took[n] for n in base]
    turn, count, seen, name = {}, {}, {}, {}
    for n, z in enumerate(node):
        count[z[0]] = turn[n] = count.get(z[0], -1) + (z[2][1] == "xq1")
        k = (z[0], turn[n], z[2])
        seen[k] = seen.get(k, 0) + 1
        name[n] = (z[2], seen[k], (0, 1, 1, 3)[turn[n]]) if turn[n] >= 0 else k + (seen[k],)
    node, lane, turn, name = [[x[n] for n in base] for x in (node, lane, turn, name)]
    costs, lags = [[[x[n] for n in base] for x in y] for y in (costs, lags)]
    full, pre, above = [sorted(set(new[p] for p in pre[n]), reverse=True) for n in base], [], []
    for ps in full:
        a, keep = 0, []
        for p in ps:
            if not a >> p & 1 or lags[0][p] > 1000:
                keep.append(p)
            a |= above[p] | 1 << p
        above.append(a)
        pre.append(keep)
    begin = [min(start[n] for n in range(size) if turn[n] == t) for t in range(4)] + [0.0]
    off, ids, place, like = [begin[t] for t in turn], {}, [], {}
    for n in sorted(range(size), key=lambda n: (turn[n], node[n][0] & STEP[1 - turn[n] % 2])):
        if name[n] not in ids:
            ids[name[n]] = len(place)
            place.append(start[n] - off[n])
        like.setdefault(node[n][2], []).append(n)
    ident = [ids[k] for k in name]
    first = [size] * len(place)
    for n in range(size - 1, -1, -1):
        first[ident[n]] = n
    took = [[c[z[3]] for c, z in zip(cost, node)] for cost in costs]
    (k0, k1, k2), (l0, l1, l2), (w0, w1, w2), gap = took, lags, PAR["weigh"], 200

    def lay(old, since, moved):
        key = old[1][:]
        for n in range(since, size):
            k = off[n] + place[ident[n]]
            for p in pre[n]:
                if key[p] >= k:
                    k = key[p] + 0.01
            key[n] = k
        order, was, i = np.argsort(np.array(key), kind="stable").tolist(), old[0], 0
        while i + gap < size and order[i:i + gap] == was[i:i + gap] and not moved.intersection(order[i:i + gap]):
            i += gap
        d0, d1, d2 = [x[:] for x in old[4]]
        marks = old[5][:i // gap + 1]
        f0, f1, f2 = [x[:] for x in marks[-1]]
        for j in range(i, size, gap):
            for n in order[j:j + gap]:
                q = lane[n]
                a, b, c = f0[q], f1[q], f2[q]
                for p in pre[n]:
                    if d0[p] > a:
                        a = d0[p]
                    if d1[p] > b:
                        b = d1[p]
                    if d2[p] > c:
                        c = d2[p]
                f0[q] = a = a + k0[n]
                f1[q] = b = b + k1[n]
                f2[q] = c = c + k2[n]
                d0[n], d1[n], d2[n] = a + l0[n], b + l1[n], c + l2[n]
            marks.append((f0[:], f1[:], f2[:]))
        ends = (max(d0), max(d1), max(d2))
        return order, key, ends[0] / w0 + ends[1] / w1 + ends[2] / w2 + (sum(d0) + sum(d1) + sum(d2)) / size, ends, (d0, d1, d2), marks

    def chain(now, m):
        done, before, last, pairs, both = now[4][m], [-1] * size, [-1] * lanes, [], []
        for n in now[0]:
            before[n], last[lane[n]] = last[lane[n]], n
        n = done.index(max(done))
        while True:
            t = done[n] - lags[m][n] - took[m][n] - 1e-6
            if len(costs[0][n]) > 1:
                both.append(n)
            w = [p for p in pre[n] if done[p] >= t]
            if not w:
                w = [before[n]]
                if w[0] < 0 or done[w[0]] - lags[m][w[0]] < t:
                    return pairs, both
                pairs.append((w[0], n))
            n = w[-1]

    def swap(calls):
        for n in calls:
            lane[n] += 1 - 2 * (lane[n] % 5)
            for m in range(3):
                took[m][n] = costs[m][n]["vs"[lane[n] % 5]]

    def draw(seed):
        seed = (seed * 6364136223846793005 + 1442695040888963407) % 2 ** 64
        return seed, (seed >> 40) / 2.0 ** 24, (seed >> 16) % 2 ** 24

    zero = [0.0] * size
    now = lay(([], zero, 0, 0, (zero, zero, zero), [([0.0] * lanes,) * 3]), 0, set())
    best, kept, pairs, seed, (hot, cold) = now, lane[:], None, PAR["seed"], PAR["heat"]
    for k in range(PAR["moves"]):
        seed, u, v = draw(seed)
        if pairs is None or u < 0.1:
            pairs, both = chain(now, v % 3)
        seed, u, v = draw(seed)
        if u < 0.12 and both:
            calls = like[node[both[v % len(both)]][2]]
            swap(calls)
            trial = lay(now, size, set(calls))
        else:
            p, n = pairs[v % len(pairs)]
            step, calls = (1, 1, 1, 100, 300, 800)[v // 4096 % 6], None
            i, x = (ident[n], now[1][p] - off[n] - step) if u < 0.56 else (ident[p], now[1][n] - off[p] + step)
            was, place[i] = place[i], x
            trial = lay(now, first[i], set())
        seed, u, v = draw(seed)
        if trial[2] - now[2] < -hot * (cold / hot) ** (k / PAR["moves"]) * math.log(u + 1e-9):
            now, pairs = trial, None
            if now[2] < best[2]:
                best, kept = now, lane[:]
        elif calls:
            swap(calls)
        else:
            place[i] = was
    return [[(node[n][1], "vstgy"[kept[n] % 5]) for n in best[0] if node[n][0] == r] for r in range(len(progs))], best[3]


def rank_program(g, core, T, topo):
    rank = T.rank_of(core)
    if rank is None:
        return
    if "order" not in ORDER:
        ORDER["order"] = arrange(lambda: [build(g, r, T, topo) for r in range(len(T.cores))])[0]
    ops, arrive = build(g, rank, T, topo)
    queue = {"v": g.vector, "s": g.scalar, "t": g.tensor, "g": g, "y": g.sync}
    own = {"v": "sv", "s": "ss", "t": "st", "g": "sp"}
    count = {}
    known = {q: {} for q in queue}
    clocks, token = {}, {}
    for i, q in ORDER["order"][rank]:
        o = ops[i]
        need = {}
        for s, n in [token[p] for p in o["pre"]] + [arrive[k] for k in o["far"]]:
            need[s] = max(need.get(s, 0), n)
        for s, n in sorted(need.items(), key=lambda z: -len(clocks.get(z, {}))):
            if known[q].get(s, 0) < n:
                queue[q].wait_ge(T.sem[s], n)
                known[q][s] = n
                for s2, n2 in clocks.get((s, n), {}).items():
                    known[q][s2] = max(known[q].get(s2, 0), n2)
        ins = o["alts"][q][0]()
        if o["out"]:
            count["loc"] = count.get("loc", 0) + o["out"][2]
            continue
        s, n = (o["sem"], 16) if o["sem"] else (own[q], 1)
        ins.then_inc(T.sem[s], n)
        count[s] = count.get(s, 0) + n
        token[i] = (s, count[s])
        clocks[token[i]] = dict(known[q])
    for s, n in arrive.values():
        count[s] = max(count.get(s, 0), n)
    for s in sorted(count):
        g.wait_ge(T.sem[s], count[s])
